import numpy as np
import ml_dtypes


def mxq(x, axis, fmt="e4m3"):
    dtype, down = {"e4m3": (ml_dtypes.float8_e4m3fn, 7), "e5m2": (ml_dtypes.float8_e5m2, 14)}[fmt]
    v = np.moveaxis(np.asarray(x, np.float32).astype(ml_dtypes.bfloat16).astype(np.float64), axis, -1)
    blocks = v.reshape(v.shape[:-1] + (-1, 32))
    amax = np.abs(blocks).max(-1, keepdims=True)
    byte = np.maximum(np.where(amax > 0, np.frexp(amax)[1] - 1 + 127, 0) - down, 1)
    scale = np.exp2(byte - 127.0)
    codes = (blocks / scale).astype(np.float32).astype(dtype).astype(np.float64)
    return np.moveaxis((codes * scale).reshape(v.shape), -1, axis)


WIDE = False


def mx_kscale(k):
    if not WIDE:
        return np.ones(k)
    levels = np.array([10, -10, 5, -5, 0])
    if k % 512:
        return np.exp2(np.random.permutation(np.resize(levels, k // 32))).repeat(32)
    a = np.empty((k // 512, 16))
    for p in range(k // 512):
        a[p, :8] = np.random.permutation(np.resize(levels, 8))
        for g in range(8):
            far = levels[np.abs(levels - a[p, g]) >= 10]
            a[p, g + 8] = far[np.random.randint(len(far))]
    return np.exp2(a.ravel()).repeat(32)


def f64(x):
    return np.asarray(x).astype(np.float64)


def striped(idx):
    return np.tile(idx.reshape(-1, 16).T, (8, 1)).astype(np.uint16)


def unstriped(offs):
    return offs[:16].T.reshape(-1).astype(np.int64)


def pack_weight(w):
    k, n = w.shape
    w = f64(np.asarray(w, np.float32).astype(ml_dtypes.bfloat16)).reshape(k // 32, 32, n)
    amax = np.abs(w).max(1)
    byte = np.clip(np.where(amax > 0, np.frexp(amax)[1] - 1 + 127 - 7, 1), 1, 254)
    scaled = (w * np.exp2(127.0 - byte)[:, None, :]).reshape(k, n).astype(np.float32)
    words = np.ascontiguousarray(scaled.reshape(k // 512, 128, 4, n).transpose(0, 1, 3, 2)).astype(ml_dtypes.float8_e4m3fn).view(np.uint8)
    return words, np.ascontiguousarray(byte.astype(np.uint8).reshape(k // 512, 16, n))


def unpack_weight(words, scales):
    g, p, n, _ = words.shape
    vals = np.ascontiguousarray(words).view(ml_dtypes.float8_e4m3fn).astype(np.float64) * np.repeat(np.exp2(scales.astype(np.float64) - 127.0), 8, axis=1)[..., None]
    return vals.transpose(0, 1, 3, 2).reshape(g * 512, n)


E2M1 = np.array([0.0, 0.5, 1.0, 1.5, 2.0, 3.0, 4.0, 6.0, -0.0, -0.5, -1.0, -1.5, -2.0, -3.0, -4.0, -6.0])


def pack_fp4(w):
    k, n = w.shape
    w = f64(np.asarray(w, np.float32).astype(ml_dtypes.bfloat16)).reshape(k // 32, 32, n)
    amax = np.abs(w).max(1)
    mant, ex = np.frexp(amax / 6.0)
    byte = np.clip(np.where(amax > 0, np.where(mant > 0.5, ex, ex - 1) + 127, 1), 1, 254)
    scaled = (w * np.exp2(127.0 - byte)[:, None, :]).reshape(k, n).astype(np.float32)
    c = np.ascontiguousarray(scaled.reshape(k // 512, 128, 4, n).transpose(0, 1, 3, 2)).astype(ml_dtypes.float4_e2m1fn).view(np.uint8) & 0xF
    words = (c[..., 0::2] | (c[..., 1::2] << 4)).reshape(k // 512, 128, 2 * n)
    return np.ascontiguousarray(words), np.ascontiguousarray(byte.astype(np.uint8).reshape(k // 512, 16, n))


def unpack_fp4(words, scales):
    g, _, n = scales.shape
    words = np.ascontiguousarray(words).reshape(g, 128, n, 2)
    nib = np.empty((g, 128, n, 4), np.uint8)
    nib[..., 0::2] = words & 0xF
    nib[..., 1::2] = words >> 4
    vals = E2M1[nib] * np.repeat(np.exp2(scales.astype(np.float64) - 127.0), 8, axis=1)[..., None]
    return vals.transpose(0, 1, 3, 2).reshape(g * 512, n)


def planes(y):
    n, m = y.shape
    v = y.astype(np.float32).astype(ml_dtypes.bfloat16).astype(np.float64).reshape(n // 32, 32, m)
    top = np.abs(v).max(1)
    byte = np.clip(np.where(top > 0, np.frexp(top)[1] - 1 + 127 - 7, 1), 1, 254)
    codes = (v * np.exp2(127.0 - byte)[:, None, :]).reshape(n, m).astype(np.float32).astype(ml_dtypes.float8_e4m3fn).view(np.uint8)
    words = codes.reshape(n // 512, 128, 4, m).transpose(0, 1, 3, 2)
    return np.ascontiguousarray(words), np.ascontiguousarray(byte.astype(np.uint8).reshape(n // 512, 16, m))


K, T, S, V, H, N = 512, 2048, 1536, 512, 512, 512


def setup_inputs():
    n = np.random.standard_normal
    s = mx_kscale(K)[:, None]
    u = mx_kscale(H)
    packed_xT = pack_weight(n((K, T)) * s)
    packed_w2 = pack_fp4(n((K, N)) / np.sqrt(K) / s)
    packed_w3 = pack_fp4(n((H, N)) / np.sqrt(H) / u[:, None])
    return {
        "x_words": packed_xT[0],
        "x_scales": packed_xT[1],
        "w1": (n((K, H)) / np.sqrt(K) / s * u).astype(np.float32),
        "w2_words": packed_w2[0],
        "w2_scales": packed_w2[1],
        "w3_words": packed_w3[0],
        "w3_scales": packed_w3[1],
        "offs": striped(np.random.permutation(T)[:S]),
    }


def reference(x_words, x_scales, w1, w2_words, w2_scales, w3_words, w3_scales, offs):
    xq = unpack_weight(x_words, x_scales)[:, unstriped(offs)]
    w1q = mxq(f64(w1), 0, "e4m3")
    h0 = w1q.T @ xq[:, :V]
    w2q = unpack_fp4(w2_words, w2_scales)
    e1 = w2q.T @ xq[:, V:2 * V]
    e2 = w2q.T @ xq[:, 2 * V:3 * V]
    h1 = w1q.T @ xq[:, V:2 * V]
    z = h0 * e1 + h0 * e2 + h1 * e2
    out_0 = unpack_fp4(w3_words, w3_scales).T @ mxq(z, 0, "e4m3")
    return (out_0,) + planes(out_0)

@@ -1,0 +1,243 @@
+from contextlib import ExitStack
+
+import concourse.mybir as mybir
+from concourse.masks import make_identity
+
+K, T, S, V, H, N = 512, 2048, 1536, 512, 512, 512
+FLOPS = 5 * 2 * K * H * V
+
+F32 = mybir.dt.float32
+BF16 = mybir.dt.bfloat16
+I32 = mybir.dt.int32
+U32 = mybir.dt.uint32
+U16 = mybir.dt.uint16
+U8 = mybir.dt.uint8
+FP8X4 = mybir.dt.float8_e4m3fn_x4
+FP4X4 = mybir.dt.float4_e2m1fn_x4
+MULT = mybir.AluOpType.mult
+
+P = 128
+PACK = 4
+QUADS = 4
+GATHER = 256
+CHUNKS = V // P
+
+
+def load_scale_rows(queue, plane, rows):
+    for q in range(QUADS):
+        queue.dma_start(
+            out=plane[32 * q : 32 * q + 4, :].bitcast(I32), in_=rows[0, 4 * q : 4 * q + 4, :].bitcast(I32)
+        )
+
+
+def tile_picked_zfibi_none_po_kernel(
+    tc, x_words, x_scales, w1, w2_words, w2_scales, w3_words, w3_scales, offs, out_0, out_1, out_2
+):
+    nc = tc.nc
+    with ExitStack() as ctx:
+        keep = ctx.enter_context(tc.tile_pool(name="keep", bufs=1))
+        ring = ctx.enter_context(tc.tile_pool(name="ring", bufs=4))
+        reused = ctx.enter_context(tc.tile_pool(name="reused", bufs=1))
+        psum = ctx.enter_context(tc.psum_pool(name="psum", bufs=1))
+
+        offsets = keep.tile([P, S // 16], U16, name="offsets")
+        x_scale_table = reused.tile([P, T], U8, name="x_scale_table", align_bytes=64, offset=0)
+        x_word_table = keep.tile([P, T], I32, name="x_word_table", align_bytes=64)
+        w2_codes = keep.tile([P, 2 * H], U8, name="w2_codes", align_bytes=64)
+        w2_plane = keep.tile([P, H], U8, name="w2_plane", align_bytes=64)
+        w1_raw = [keep.tile([P, PACK, H // 2], F32, name=f"w1_raw{u}", align_bytes=64) for u in range(2)]
+        identity = keep.tile([P, P], F32, name="identity", align_bytes=64)
+
+        nc.vector.memset(x_scale_table[:].bitcast(I32), 0)
+        nc.gpsimd.memset(w2_plane[:].bitcast(I32), 0)
+
+        w1_rows = w1.rearrange("(p j) c -> p j c", j=PACK)
+        nc.sync.dma_start(offsets[:], offs)
+        load_scale_rows(nc.sync, x_scale_table, x_scales)
+        nc.scalar.dma_start(out=x_word_table[:], in_=x_words[0].rearrange("p c r -> p (c r)").bitcast(I32))
+        nc.scalar.dma_start(out=w1_raw[0][:], in_=w1_rows[:, :, 0 : H // 2])
+        nc.scalar.dma_start(out=w1_raw[1][:], in_=w1_rows[:, :, H // 2 : H])
+        load_scale_rows(nc.gpsimd, w2_plane, w2_scales)
+        nc.gpsimd.dma_start(out=w2_codes[:].bitcast(I32), in_=w2_words[0].bitcast(I32))
+        make_identity(nc, identity[:])
+
+        picked_scales = keep.tile([P, S], U8, name="picked_scales", align_bytes=64)
+        nc.vector.tensor_copy(picked_scales[:], x_scale_table[:].indirect(offsets[:]))
+
+        w3_codes = reused.tile([P, 2 * N], U8, name="w3_codes", align_bytes=64, offset=0)
+        w3_plane = reused.tile([P, N], U8, name="w3_plane", align_bytes=64, offset=2 * N)
+        picked_words = reused.tile([P, S], U32, name="picked_words", align_bytes=64, offset=3 * N)
+        nc.gpsimd.memset(w3_plane[:].bitcast(I32), 0)
+        nc.sync.dma_start(out=w3_codes[:].bitcast(I32), in_=w3_words[0].bitcast(I32))
+        load_scale_rows(nc.sync, w3_plane, w3_scales)
+
+        def gather_words(field, half):
+            first = field * V + half * GATHER
+            nc.vector.tensor_copy(
+                picked_words[:, first : first + GATHER],
+                x_word_table[:].bitcast(U32).indirect(offsets[:, first // 16 : (first + GATHER) // 16]),
+            )
+
+        w1_bf = keep.tile([P, H, PACK], BF16, name="w1_bf", align_bytes=64)
+        w1_codes = keep.tile([P, H], U32, name="w1_codes", align_bytes=64)
+        w1_plane = keep.tile([P, H], U8, name="w1_plane", align_bytes=64)
+
+        def cast_w1(u):
+            cols = slice(u * (H // 2), (u + 1) * (H // 2))
+            nc.scalar.copy(
+                out=w1_bf[:, cols, :].rearrange("p (c i) j -> p c j i", i=4),
+                in_=w1_raw[u][:].rearrange("p j (c i) -> p c j i", i=4),
+            )
+
+        def quantize_w1(u):
+            cols = slice(u * (H // 2), (u + 1) * (H // 2))
+            nc.vector.quantize_mx(
+                out=w1_codes[:, cols].bitcast(FP8X4),
+                scales=w1_plane[:, cols],
+                in_=w1_bf[:, cols, :].rearrange("p c j -> p (c j)"),
+            )
+
+        w3_dealt = keep.tile([P, 2 * N], U8, name="w3_dealt", align_bytes=64)
+        w3_dealt_plane = keep.tile([P, N], U8, name="w3_dealt_plane", align_bytes=64)
+
+        def deal_w3():
+            nc.vector.tensor_copy(
+                out=w3_dealt[:].rearrange("p (t m b) -> p t m b", t=PACK, b=2),
+                in_=w3_codes[:].rearrange("p (m t b) -> p t m b", t=PACK, b=2),
+            )
+            nc.vector.tensor_copy(
+                out=w3_dealt_plane[:].rearrange("p (t m) -> p t m", t=PACK),
+                in_=w3_plane[:].rearrange("p (m t) -> p t m", t=PACK),
+            )
+
+        def project(bank, chunk, fields, codes, plane):
+            for n, field in enumerate(fields):
+                first = field * V + chunk * P
+                nc.tensor.matmul_mx(
+                    out=bank[:],
+                    lhsT=picked_words[:, first : first + P].bitcast(FP8X4),
+                    lhsT_scale=picked_scales[:, first : first + P],
+                    rhs=codes,
+                    rhs_scale=plane[:],
+                    start=(n == 0),
+                    stop=(n == len(fields) - 1),
+                )
+
+        right = {}
+        terms = {}
+        z_bf = {}
+        z_q = {}
+        y32 = {}
+        y_bf = {}
+
+        def right_factors(chunk):
+            for n, fields in enumerate(((2,), (2, 1))):
+                bank = psum.tile([P, H], F32, name="e_bank", bufs=2)
+                project(bank, chunk, fields, w2_codes[:].bitcast(FP4X4), w2_plane)
+                e = ring.tile([P, PACK, P], F32, name=f"e{n}")
+                nc.scalar.copy(out=e[:], in_=bank[:].rearrange("p (m t) -> p t m", t=PACK))
+                right[chunk, n] = e
+
+        def products(chunk):
+            for n, field in enumerate((1, 0)):
+                bank = psum.tile([P, H], F32, name="h_bank", bufs=3)
+                project(bank, chunk, (field,), w1_codes[:].bitcast(FP8X4), w1_plane)
+                term = ring.tile([P, PACK, P], F32, name=f"term{n}")
+                nc.vector.tensor_tensor(
+                    out=term[:], in0=bank[:].rearrange("p (m t) -> p t m", t=PACK), in1=right[chunk, n][:], op=MULT
+                )
+                terms[chunk, n] = term
+
+        def turn_and_add(chunk):
+            bank = psum.tile([P, PACK, P], F32, name="z_bank", bufs=2)
+            for n in range(2):
+                for t in range(PACK):
+                    nc.tensor.matmul(
+                        out=bank[:, t, :],
+                        lhsT=terms[chunk, n][:, t, :],
+                        rhs=identity[:],
+                        is_transpose=True,
+                        start=(n == 0 and t == 0),
+                        stop=(n == 1 and t == PACK - 1),
+                    )
+            z = ring.tile([P, P, PACK], BF16, name="z_bf", align_bytes=64)
+            nc.scalar.copy(out=z[:], in_=bank[:].rearrange("p t v -> p v t"))
+            z_bf[chunk] = z
+
+        def quantize_z(chunk):
+            codes = ring.tile([P, P], U32, name="z_codes", align_bytes=64)
+            plane = ring.tile([P, P], U8, name="z_plane", align_bytes=64)
+            nc.vector.quantize_mx(
+                out=codes[:].bitcast(FP8X4), scales=plane[:], in_=z_bf[chunk][:].rearrange("p v t -> p (v t)")
+            )
+            z_q[chunk] = (codes, plane)
+
+        y_rows = out_0.rearrange("(p t) v -> p t v", t=PACK)
+
+        def last_layer(chunk):
+            codes, plane = z_q[chunk]
+            bank = psum.tile([P, PACK, P], F32, name="y_bank", bufs=1)
+            for t in range(PACK):
+                nc.tensor.matmul_mx(
+                    out=bank[:, t, :],
+                    lhsT=w3_dealt[:, 2 * P * t : 2 * P * (t + 1)].bitcast(FP4X4),
+                    lhsT_scale=w3_dealt_plane[:, P * t : P * (t + 1)],
+                    rhs=codes[:].bitcast(FP8X4),
+                    rhs_scale=plane[:],
+                    start=True,
+                    stop=True,
+                )
+            y = ring.tile([P, PACK, P], F32, name="y32")
+            nc.scalar.copy(out=y[:], in_=bank[:])
+            nc.sync.dma_start(out=y_rows[:, :, chunk * P : (chunk + 1) * P], in_=y[:])
+            y32[chunk] = y
+
+        y_codes = keep.tile([P, V], I32, name="y_codes", align_bytes=64)
+        y_plane = keep.tile([P, V], U8, name="y_plane", align_bytes=64)
+        y_words = out_1[0].rearrange("p v r -> p (v r)").bitcast(I32)
+
+        def round_y(chunk):
+            y = ring.tile([P, P, PACK], BF16, name="y_bf", align_bytes=64)
+            nc.vector.tensor_copy(out=y[:], in_=y32[chunk][:].rearrange("p t v -> p v t"))
+            y_bf[chunk] = y
+
+        def quantize_y(chunk):
+            cols = slice(chunk * P, (chunk + 1) * P)
+            nc.vector.quantize_mx(
+                out=y_codes[:, cols].bitcast(FP8X4),
+                scales=y_plane[:, cols],
+                in_=y_bf[chunk][:].rearrange("p v t -> p (v t)"),
+            )
+            nc.sync.dma_start(out=y_words[:, cols], in_=y_codes[:, cols])
+
+        for field in (2, 1, 0):
+            gather_words(field, 0)
+        cast_w1(0)
+        cast_w1(1)
+        quantize_w1(0)
+        right_factors(0)
+        right_factors(1)
+        gather_words(2, 1)
+        quantize_w1(1)
+        gather_words(1, 1)
+        gather_words(0, 1)
+        deal_w3()
+        for step in range(CHUNKS + 3):
+            if step < CHUNKS:
+                products(step)
+            if step + 2 < CHUNKS:
+                right_factors(step + 2)
+            if step < CHUNKS:
+                turn_and_add(step)
+            if 0 <= step - 1 < CHUNKS:
+                quantize_z(step - 1)
+                last_layer(step - 1)
+            if 0 <= step - 2 < CHUNKS:
+                round_y(step - 2)
+            if 0 <= step - 3 < CHUNKS:
+                quantize_y(step - 3)
+
+        for q in range(QUADS):
+            nc.scalar.dma_start(
+                out=out_2[0, 4 * q : 4 * q + 4, :].bitcast(I32), in_=y_plane[32 * q : 32 * q + 4, :].bitcast(I32)
+            )

@@ -15,12 +15,14 @@ U8 = mybir.dt.uint8
 FP8X4 = mybir.dt.float8_e4m3fn_x4
 FP4X4 = mybir.dt.float4_e2m1fn_x4
 MULT = mybir.AluOpType.mult
+ADD = mybir.AluOpType.add
 
 P = 128
 PACK = 4
 QUADS = 4
 GATHER = 256
 CHUNKS = V // P
+MODES = "TTNN"
 
 
 def load_scale_rows(queue, plane, rows):
@@ -45,31 +47,55 @@ def tile_picked_zfibi_none_po_kernel(
         x_word_table = keep.tile([P, T], I32, name="x_word_table", align_bytes=64)
         w2_codes = keep.tile([P, 2 * H], U8, name="w2_codes", align_bytes=64)
         w2_plane = keep.tile([P, H], U8, name="w2_plane", align_bytes=64)
+        w3_codes = keep.tile([P, 2 * N], U8, name="w3_codes", align_bytes=64)
+        w3_plane = keep.tile([P, N], U8, name="w3_plane", align_bytes=64)
         w1_raw = [keep.tile([P, PACK, H // 2], F32, name=f"w1_raw{u}", align_bytes=64) for u in range(2)]
-        identity = keep.tile([P, P], F32, name="identity", align_bytes=64)
-
-        nc.vector.memset(x_scale_table[:].bitcast(I32), 0)
-        nc.gpsimd.memset(w2_plane[:].bitcast(I32), 0)
-
         w1_rows = w1.rearrange("(p j) c -> p j c", j=PACK)
+
+        nc.vector.memset(x_scale_table[:, : T // 2].bitcast(I32), 0)
+        nc.gpsimd.memset(x_scale_table[:, T // 2 :].bitcast(I32), 0)
+        nc.vector.memset(w2_plane[:].bitcast(I32), 0)
+        nc.vector.memset(w3_plane[:].bitcast(I32), 0)
         nc.sync.dma_start(offsets[:], offs)
+        nc.sync.dma_start(out=w2_codes[:].bitcast(I32), in_=w2_words[0].bitcast(I32))
+        nc.sync.dma_start(out=w3_codes[:].bitcast(I32), in_=w3_words[0].bitcast(I32))
         load_scale_rows(nc.sync, x_scale_table, x_scales)
-        nc.scalar.dma_start(out=x_word_table[:], in_=x_words[0].rearrange("p c r -> p (c r)").bitcast(I32))
-        nc.scalar.dma_start(out=w1_raw[0][:], in_=w1_rows[:, :, 0 : H // 2])
-        nc.scalar.dma_start(out=w1_raw[1][:], in_=w1_rows[:, :, H // 2 : H])
-        load_scale_rows(nc.gpsimd, w2_plane, w2_scales)
-        nc.gpsimd.dma_start(out=w2_codes[:].bitcast(I32), in_=w2_words[0].bitcast(I32))
+        nc.sync.dma_start(out=x_word_table[:], in_=x_words[0].rearrange("p c r -> p (c r)").bitcast(I32))
+        nc.sync.dma_start(out=w1_raw[0][:], in_=w1_rows[:, :, 0 : H // 2])
+        load_scale_rows(nc.sync, w2_plane, w2_scales)
+        nc.sync.dma_start(out=w1_raw[1][:], in_=w1_rows[:, :, H // 2 : H])
+        load_scale_rows(nc.sync, w3_plane, w3_scales)
+        identity = keep.tile([P, P], F32, name="identity", align_bytes=64)
         make_identity(nc, identity[:])
 
-        picked_scales = keep.tile([P, S], U8, name="picked_scales", align_bytes=64)
-        nc.vector.tensor_copy(picked_scales[:], x_scale_table[:].indirect(offsets[:]))
+        w2_dealt = keep.tile([P, 2 * H], U8, name="w2_dealt", align_bytes=64)
+        w2_dealt_plane = keep.tile([P, H], U8, name="w2_dealt_plane", align_bytes=64)
+        w3_dealt = keep.tile([P, 2 * N], U8, name="w3_dealt", align_bytes=64)
+        w3_dealt_plane = keep.tile([P, N], U8, name="w3_dealt_plane", align_bytes=64)
 
-        w3_codes = reused.tile([P, 2 * N], U8, name="w3_codes", align_bytes=64, offset=0)
-        w3_plane = reused.tile([P, N], U8, name="w3_plane", align_bytes=64, offset=2 * N)
-        picked_words = reused.tile([P, S], U32, name="picked_words", align_bytes=64, offset=3 * N)
-        nc.gpsimd.memset(w3_plane[:].bitcast(I32), 0)
-        nc.sync.dma_start(out=w3_codes[:].bitcast(I32), in_=w3_words[0].bitcast(I32))
-        load_scale_rows(nc.sync, w3_plane, w3_scales)
+        def deal_codes(engine, dealt, codes):
+            engine.tensor_copy(
+                out=dealt[:].rearrange("p (t m b) -> p t m b", t=PACK, b=2),
+                in_=codes[:].rearrange("p (m t b) -> p t m b", t=PACK, b=2),
+            )
+
+        def deal_plane(engine, dealt, plane):
+            engine.tensor_copy(
+                out=dealt[:].rearrange("p (t m) -> p t m", t=PACK),
+                in_=plane[:].rearrange("p (m t) -> p t m", t=PACK),
+            )
+
+        picked_scales = keep.tile([P, S], U8, name="picked_scales", align_bytes=64)
+
+        def gather_scales():
+            nc.vector.tensor_copy(picked_scales[:], x_scale_table[:].indirect(offsets[:]))
+
+        gather_scales()
+        deal_codes(nc.gpsimd, w2_dealt, w2_codes)
+        deal_plane(nc.gpsimd, w2_dealt_plane, w2_plane)
+        deal_codes(nc.gpsimd, w3_dealt, w3_codes)
+        deal_plane(nc.gpsimd, w3_dealt_plane, w3_plane)
+        picked_words = reused.tile([P, S], U32, name="picked_words", align_bytes=64, offset=0)
 
         def gather_words(field, half):
             first = field * V + half * GATHER
@@ -78,105 +104,132 @@ def tile_picked_zfibi_none_po_kernel(
                 x_word_table[:].bitcast(U32).indirect(offsets[:, first // 16 : (first + GATHER) // 16]),
             )
 
-        w1_bf = keep.tile([P, H, PACK], BF16, name="w1_bf", align_bytes=64)
+        w1_bf = keep.tile([P, PACK, P, PACK], BF16, name="w1_bf", align_bytes=64)
         w1_codes = keep.tile([P, H], U32, name="w1_codes", align_bytes=64)
         w1_plane = keep.tile([P, H], U8, name="w1_plane", align_bytes=64)
 
         def cast_w1(u):
-            cols = slice(u * (H // 2), (u + 1) * (H // 2))
             nc.scalar.copy(
-                out=w1_bf[:, cols, :].rearrange("p (c i) j -> p c j i", i=4),
-                in_=w1_raw[u][:].rearrange("p j (c i) -> p c j i", i=4),
+                out=w1_bf[:, :, u * (P // 2) : (u + 1) * (P // 2), :].rearrange("p t m j -> p m j t"),
+                in_=w1_raw[u][:].rearrange("p j (m t) -> p m j t", t=PACK),
             )
 
-        def quantize_w1(u):
-            cols = slice(u * (H // 2), (u + 1) * (H // 2))
+        def quantize_w1():
             nc.vector.quantize_mx(
-                out=w1_codes[:, cols].bitcast(FP8X4),
-                scales=w1_plane[:, cols],
-                in_=w1_bf[:, cols, :].rearrange("p c j -> p (c j)"),
+                out=w1_codes[:].bitcast(FP8X4),
+                scales=w1_plane[:],
+                in_=w1_bf[:].rearrange("p t m j -> p (t m j)"),
             )
 
-        w3_dealt = keep.tile([P, 2 * N], U8, name="w3_dealt", align_bytes=64)
-        w3_dealt_plane = keep.tile([P, N], U8, name="w3_dealt_plane", align_bytes=64)
+        def weights(which, lo, hi):
+            if which == 1:
+                return w1_codes[:, lo:hi].bitcast(FP8X4), w1_plane[:, lo:hi]
+            return w2_dealt[:, 2 * lo : 2 * hi].bitcast(FP4X4), w2_dealt_plane[:, lo:hi]
 
-        def deal_w3():
-            nc.vector.tensor_copy(
-                out=w3_dealt[:].rearrange("p (t m b) -> p t m b", t=PACK, b=2),
-                in_=w3_codes[:].rearrange("p (m t b) -> p t m b", t=PACK, b=2),
-            )
-            nc.vector.tensor_copy(
-                out=w3_dealt_plane[:].rearrange("p (t m) -> p t m", t=PACK),
-                in_=w3_plane[:].rearrange("p (m t) -> p t m", t=PACK),
-            )
+        def project(bank, chunk, fields, which):
+            if MODES[chunk] == "T":
+                codes, plane = weights(which, 0, H)
+                for n, field in enumerate(fields):
+                    first = field * V + chunk * P
+                    nc.tensor.matmul_mx(
+                        out=bank[:].rearrange("p t m -> p (t m)"),
+                        lhsT=picked_words[:, first : first + P].bitcast(FP8X4),
+                        lhsT_scale=picked_scales[:, first : first + P],
+                        rhs=codes,
+                        rhs_scale=plane,
+                        start=(n == 0),
+                        stop=(n == len(fields) - 1),
+                    )
+                return bank[:]
+            for t in range(PACK):
+                codes, plane = weights(which, t * P, (t + 1) * P)
+                for n, field in enumerate(fields):
+                    first = field * V + chunk * P
+                    nc.tensor.matmul_mx(
+                        out=bank[:, t, :],
+                        lhsT=codes,
+                        lhsT_scale=plane,
+                        rhs=picked_words[:, first : first + P].bitcast(FP8X4),
+                        rhs_scale=picked_scales[:, first : first + P],
+                        start=(n == 0),
+                        stop=(n == len(fields) - 1),
+                    )
+            return bank[:].rearrange("p t v -> p v t")
 
-        def project(bank, chunk, fields, codes, plane):
-            for n, field in enumerate(fields):
-                first = field * V + chunk * P
-                nc.tensor.matmul_mx(
-                    out=bank[:],
-                    lhsT=picked_words[:, first : first + P].bitcast(FP8X4),
-                    lhsT_scale=picked_scales[:, first : first + P],
-                    rhs=codes,
-                    rhs_scale=plane[:],
-                    start=(n == 0),
-                    stop=(n == len(fields) - 1),
-                )
+        def shaped(tile, chunk):
+            if MODES[chunk] == "T":
+                return tile[:].rearrange("p (t m) -> p t m", t=PACK)
+            return tile[:].rearrange("p (v t) -> p v t", t=PACK)
 
         right = {}
+        left = {}
         terms = {}
         z_bf = {}
         z_q = {}
         y32 = {}
         y_bf = {}
 
-        def right_factors(chunk):
-            for n, fields in enumerate(((2,), (2, 1))):
-                bank = psum.tile([P, H], F32, name="e_bank", bufs=2)
-                project(bank, chunk, fields, w2_codes[:].bitcast(FP4X4), w2_plane)
-                e = ring.tile([P, PACK, P], F32, name=f"e{n}")
-                nc.scalar.copy(out=e[:], in_=bank[:].rearrange("p (m t) -> p t m", t=PACK))
-                right[chunk, n] = e
+        def right_factor(chunk, n):
+            bank = psum.tile([P, PACK, P], F32, name="e_bank", tag="ez", bufs=2)
+            view = project(bank, chunk, ((2,), (2, 1))[n], 2)
+            e = ring.tile([P, H], F32, name=f"e{n}")
+            nc.scalar.copy(out=shaped(e, chunk), in_=view)
+            right[chunk, n] = e
 
-        def products(chunk):
-            for n, field in enumerate((1, 0)):
-                bank = psum.tile([P, H], F32, name="h_bank", bufs=3)
-                project(bank, chunk, (field,), w1_codes[:].bitcast(FP8X4), w1_plane)
-                term = ring.tile([P, PACK, P], F32, name=f"term{n}")
-                nc.vector.tensor_tensor(
-                    out=term[:], in0=bank[:].rearrange("p (m t) -> p t m", t=PACK), in1=right[chunk, n][:], op=MULT
-                )
-                terms[chunk, n] = term
+        def left_factor(chunk, n):
+            bank = psum.tile([P, PACK, P], F32, name="h_bank", bufs=4)
+            left[chunk, n] = project(bank, chunk, ((1, 0)[n],), 1)
+
+        def right_factors(chunk):
+            right_factor(chunk, 0)
+            right_factor(chunk, 1)
+
+        def left_factors(chunk):
+            left_factor(chunk, 0)
+            left_factor(chunk, 1)
+
+        def multiply(chunk, n):
+            term = ring.tile([P, H], F32, name=f"term{n}")
+            nc.vector.tensor_tensor(
+                out=shaped(term, chunk), in0=left[chunk, n], in1=shaped(right[chunk, n], chunk), op=MULT
+            )
+            terms[chunk, n] = term
+
+        def add(chunk, engine):
+            z = ring.tile([P, H], BF16, name="z_bf", align_bytes=64)
+            engine.tensor_tensor(out=z[:], in0=terms[chunk, 0][:], in1=terms[chunk, 1][:], op=ADD)
+            z_bf[chunk] = z
 
         def turn_and_add(chunk):
-            bank = psum.tile([P, PACK, P], F32, name="z_bank", bufs=2)
+            bank = psum.tile([P, PACK, P], F32, name="z_bank", tag="ez", bufs=2)
             for n in range(2):
                 for t in range(PACK):
                     nc.tensor.matmul(
                         out=bank[:, t, :],
-                        lhsT=terms[chunk, n][:, t, :],
+                        lhsT=terms[chunk, n][:, t * P : (t + 1) * P],
                         rhs=identity[:],
                         is_transpose=True,
                         start=(n == 0 and t == 0),
                         stop=(n == 1 and t == PACK - 1),
                     )
-            z = ring.tile([P, P, PACK], BF16, name="z_bf", align_bytes=64)
-            nc.scalar.copy(out=z[:], in_=bank[:].rearrange("p t v -> p v t"))
+            z = ring.tile([P, H], BF16, name="z_bf", align_bytes=64)
+            nc.scalar.copy(
+                out=z[:].rearrange("p (v t) -> p v t", t=PACK), in_=bank[:].rearrange("p t v -> p v t")
+            )
             z_bf[chunk] = z
 
         def quantize_z(chunk):
             codes = ring.tile([P, P], U32, name="z_codes", align_bytes=64)
             plane = ring.tile([P, P], U8, name="z_plane", align_bytes=64)
-            nc.vector.quantize_mx(
-                out=codes[:].bitcast(FP8X4), scales=plane[:], in_=z_bf[chunk][:].rearrange("p v t -> p (v t)")
-            )
+            nc.vector.quantize_mx(out=codes[:].bitcast(FP8X4), scales=plane[:], in_=z_bf[chunk][:])
             z_q[chunk] = (codes, plane)
 
         y_rows = out_0.rearrange("(p t) v -> p t v", t=PACK)
+        y_bank = {}
 
         def last_layer(chunk):
             codes, plane = z_q[chunk]
-            bank = psum.tile([P, PACK, P], F32, name="y_bank", bufs=1)
+            bank = psum.tile([P, PACK, P], F32, name="y_bank", bufs=2)
             for t in range(PACK):
                 nc.tensor.matmul_mx(
                     out=bank[:, t, :],
@@ -187,8 +240,11 @@ def tile_picked_zfibi_none_po_kernel(
                     start=True,
                     stop=True,
                 )
+            y_bank[chunk] = bank
+
+        def store_y(chunk):
             y = ring.tile([P, PACK, P], F32, name="y32")
-            nc.scalar.copy(out=y[:], in_=bank[:])
+            nc.scalar.copy(out=y[:], in_=y_bank[chunk][:])
             nc.sync.dma_start(out=y_rows[:, :, chunk * P : (chunk + 1) * P], in_=y[:])
             y32[chunk] = y
 
@@ -196,9 +252,14 @@ def tile_picked_zfibi_none_po_kernel(
         y_plane = keep.tile([P, V], U8, name="y_plane", align_bytes=64)
         y_words = out_1[0].rearrange("p v r -> p (v r)").bitcast(I32)
 
-        def round_y(chunk):
+        def round_y(chunk, how):
             y = ring.tile([P, P, PACK], BF16, name="y_bf", align_bytes=64)
-            nc.vector.tensor_copy(out=y[:], in_=y32[chunk][:].rearrange("p t v -> p v t"))
+            if how == "vs":
+                nc.vector.tensor_copy(out=y[:], in_=y32[chunk][:].rearrange("p t v -> p v t"))
+            elif how == "vp":
+                nc.vector.tensor_copy(out=y[:], in_=y_bank[chunk][:].rearrange("p t v -> p v t"))
+            else:
+                nc.scalar.copy(out=y[:], in_=y_bank[chunk][:].rearrange("p t v -> p v t"))
             y_bf[chunk] = y
 
         def quantize_y(chunk):
@@ -208,36 +269,67 @@ def tile_picked_zfibi_none_po_kernel(
                 scales=y_plane[:, cols],
                 in_=y_bf[chunk][:].rearrange("p v t -> p (v t)"),
             )
-            nc.sync.dma_start(out=y_words[:, cols], in_=y_codes[:, cols])
 
-        for field in (2, 1, 0):
-            gather_words(field, 0)
-        cast_w1(0)
-        cast_w1(1)
-        quantize_w1(0)
-        right_factors(0)
-        right_factors(1)
-        gather_words(2, 1)
-        quantize_w1(1)
-        gather_words(1, 1)
-        gather_words(0, 1)
-        deal_w3()
-        for step in range(CHUNKS + 3):
-            if step < CHUNKS:
-                products(step)
-            if step + 2 < CHUNKS:
-                right_factors(step + 2)
-            if step < CHUNKS:
-                turn_and_add(step)
-            if 0 <= step - 1 < CHUNKS:
-                quantize_z(step - 1)
-                last_layer(step - 1)
-            if 0 <= step - 2 < CHUNKS:
-                round_y(step - 2)
-            if 0 <= step - 3 < CHUNKS:
-                quantize_y(step - 3)
+        def store_codes(lo, hi):
+            nc.sync.dma_start(out=y_words[:, lo * P : hi * P], in_=y_codes[:, lo * P : hi * P])
 
-        for q in range(QUADS):
-            nc.scalar.dma_start(
+        def store_plane(queue, q):
+            queue.dma_start(
                 out=out_2[0, 4 * q : 4 * q + 4, :].bitcast(I32), in_=y_plane[32 * q : 32 * q + 4, :].bitcast(I32)
             )
+
+        gather_words(2, 0)
+        gather_words(1, 0)
+        gather_words(0, 0)
+        cast_w1(0)
+        cast_w1(1)
+        quantize_w1()
+        right_factors(0)
+        left_factors(0)
+        right_factors(1)
+        left_factors(1)
+        gather_words(2, 1)
+        gather_words(1, 1)
+        gather_words(0, 1)
+        right_factors(2)
+        multiply(0, 0)
+        multiply(0, 1)
+        right_factors(3)
+        turn_and_add(0)
+        left_factors(2)
+        multiply(1, 0)
+        multiply(1, 1)
+        turn_and_add(1)
+        left_factors(3)
+        multiply(2, 0)
+        quantize_z(0)
+        last_layer(0)
+        store_y(0)
+        round_y(0, "s")
+        multiply(2, 1)
+        multiply(3, 0)
+        quantize_z(1)
+        last_layer(1)
+        store_y(1)
+        round_y(1, "s")
+        add(2, nc.vector)
+        multiply(3, 1)
+        quantize_z(2)
+        last_layer(2)
+        add(3, nc.vector)
+        quantize_y(0)
+        quantize_z(3)
+        last_layer(3)
+        store_y(2)
+        round_y(2, "vs")
+        quantize_y(1)
+        round_y(3, "vp")
+        store_y(3)
+        quantize_y(2)
+        store_codes(0, 3)
+        quantize_y(3)
+        store_codes(3, 4)
+        store_plane(nc.sync, 0)
+        store_plane(nc.scalar, 1)
+        store_plane(nc.sync, 2)
+        store_plane(nc.scalar, 3)

@@ -22,7 +22,7 @@ PACK = 4
 QUADS = 4
 GATHER = 256
 CHUNKS = V // P
-MODES = "TTNN"
+MODES = "TTTT"
 
 
 def load_scale_rows(queue, plane, rows):
@@ -49,7 +49,10 @@ def tile_picked_zfibi_none_po_kernel(
         w2_plane = keep.tile([P, H], U8, name="w2_plane", align_bytes=64)
         w3_codes = keep.tile([P, 2 * N], U8, name="w3_codes", align_bytes=64)
         w3_plane = keep.tile([P, N], U8, name="w3_plane", align_bytes=64)
-        w1_raw = [keep.tile([P, PACK, H // 2], F32, name=f"w1_raw{u}", align_bytes=64) for u in range(2)]
+        w1_raw = [
+            reused.tile([P, PACK, H // 2], F32, name=f"w1_raw{u}", align_bytes=64, offset=8192 + 4096 * u)
+            for u in range(2)
+        ]
         w1_rows = w1.rearrange("(p j) c -> p j c", j=PACK)
 
         nc.vector.memset(x_scale_table[:, : T // 2].bitcast(I32), 0)
@@ -57,8 +60,8 @@ def tile_picked_zfibi_none_po_kernel(
         nc.vector.memset(w2_plane[:].bitcast(I32), 0)
         nc.vector.memset(w3_plane[:].bitcast(I32), 0)
         nc.sync.dma_start(offsets[:], offs)
-        nc.sync.dma_start(out=w2_codes[:].bitcast(I32), in_=w2_words[0].bitcast(I32))
         nc.sync.dma_start(out=w3_codes[:].bitcast(I32), in_=w3_words[0].bitcast(I32))
+        nc.sync.dma_start(out=w2_codes[:].bitcast(I32), in_=w2_words[0].bitcast(I32))
         load_scale_rows(nc.sync, x_scale_table, x_scales)
         nc.sync.dma_start(out=x_word_table[:], in_=x_words[0].rearrange("p c r -> p (c r)").bitcast(I32))
         nc.sync.dma_start(out=w1_raw[0][:], in_=w1_rows[:, :, 0 : H // 2])
@@ -68,8 +71,6 @@ def tile_picked_zfibi_none_po_kernel(
         identity = keep.tile([P, P], F32, name="identity", align_bytes=64)
         make_identity(nc, identity[:])
 
-        w2_dealt = keep.tile([P, 2 * H], U8, name="w2_dealt", align_bytes=64)
-        w2_dealt_plane = keep.tile([P, H], U8, name="w2_dealt_plane", align_bytes=64)
         w3_dealt = keep.tile([P, 2 * N], U8, name="w3_dealt", align_bytes=64)
         w3_dealt_plane = keep.tile([P, N], U8, name="w3_dealt_plane", align_bytes=64)
 
@@ -90,41 +91,50 @@ def tile_picked_zfibi_none_po_kernel(
         def gather_scales():
             nc.vector.tensor_copy(picked_scales[:], x_scale_table[:].indirect(offsets[:]))
 
+        deal_codes(nc.vector, w3_dealt, w3_codes)
         gather_scales()
-        deal_codes(nc.gpsimd, w2_dealt, w2_codes)
-        deal_plane(nc.gpsimd, w2_dealt_plane, w2_plane)
-        deal_codes(nc.gpsimd, w3_dealt, w3_codes)
-        deal_plane(nc.gpsimd, w3_dealt_plane, w3_plane)
-        picked_words = reused.tile([P, S], U32, name="picked_words", align_bytes=64, offset=0)
+        early_words = reused.tile([P, 4 * GATHER], U32, name="early_words", align_bytes=64, offset=0)
+        word_tiles = {"early": early_words}
+        places = {
+            (2, 0): ("early", 0), (1, 0): ("early", 1), (0, 0): ("early", 2), (2, 1): ("early", 3),
+            (1, 1): ("late", 0), (0, 1): ("late", 1),
+        }
+
+        def picked(field, record, count):
+            half, inner = divmod(record, GATHER)
+            tile_name, slot = places[field, half]
+            first = slot * GATHER + inner
+            return word_tiles[tile_name][:, first : first + count]
 
         def gather_words(field, half):
             first = field * V + half * GATHER
             nc.vector.tensor_copy(
-                picked_words[:, first : first + GATHER],
+                picked(field, half * GATHER, GATHER),
                 x_word_table[:].bitcast(U32).indirect(offsets[:, first // 16 : (first + GATHER) // 16]),
             )
 
-        w1_bf = keep.tile([P, PACK, P, PACK], BF16, name="w1_bf", align_bytes=64)
+        w1_bf = reused.tile([P, H, PACK], BF16, name="w1_bf", align_bytes=64, offset=4096)
         w1_codes = keep.tile([P, H], U32, name="w1_codes", align_bytes=64)
         w1_plane = keep.tile([P, H], U8, name="w1_plane", align_bytes=64)
 
         def cast_w1(u):
             nc.scalar.copy(
-                out=w1_bf[:, :, u * (P // 2) : (u + 1) * (P // 2), :].rearrange("p t m j -> p m j t"),
-                in_=w1_raw[u][:].rearrange("p j (m t) -> p m j t", t=PACK),
+                out=w1_bf[:, u * (H // 2) : (u + 1) * (H // 2), :].rearrange("p (c i) j -> p c j i", i=4),
+                in_=w1_raw[u][:].rearrange("p j (c i) -> p c j i", i=4),
             )
 
         def quantize_w1():
             nc.vector.quantize_mx(
                 out=w1_codes[:].bitcast(FP8X4),
                 scales=w1_plane[:],
-                in_=w1_bf[:].rearrange("p t m j -> p (t m j)"),
+                in_=w1_bf[:].rearrange("p c j -> p (c j)"),
             )
+            word_tiles["late"] = reused.tile([P, 2 * GATHER], U32, name="late_words", align_bytes=64, offset=4096)
 
         def weights(which, lo, hi):
             if which == 1:
                 return w1_codes[:, lo:hi].bitcast(FP8X4), w1_plane[:, lo:hi]
-            return w2_dealt[:, 2 * lo : 2 * hi].bitcast(FP4X4), w2_dealt_plane[:, lo:hi]
+            return w2_codes[:, 2 * lo : 2 * hi].bitcast(FP4X4), w2_plane[:, lo:hi]
 
         def project(bank, chunk, fields, which):
             if MODES[chunk] == "T":
@@ -133,14 +143,14 @@ def tile_picked_zfibi_none_po_kernel(
                     first = field * V + chunk * P
                     nc.tensor.matmul_mx(
                         out=bank[:].rearrange("p t m -> p (t m)"),
-                        lhsT=picked_words[:, first : first + P].bitcast(FP8X4),
+                        lhsT=picked(field, chunk * P, P).bitcast(FP8X4),
                         lhsT_scale=picked_scales[:, first : first + P],
                         rhs=codes,
                         rhs_scale=plane,
                         start=(n == 0),
                         stop=(n == len(fields) - 1),
                     )
-                return bank[:]
+                return bank[:].rearrange("p a b -> p (a b)").rearrange("p (m t) -> p t m", t=PACK)
             for t in range(PACK):
                 codes, plane = weights(which, t * P, (t + 1) * P)
                 for n, field in enumerate(fields):
@@ -149,7 +159,7 @@ def tile_picked_zfibi_none_po_kernel(
                         out=bank[:, t, :],
                         lhsT=codes,
                         lhsT_scale=plane,
-                        rhs=picked_words[:, first : first + P].bitcast(FP8X4),
+                        rhs=picked(field, chunk * P, P).bitcast(FP8X4),
                         rhs_scale=picked_scales[:, first : first + P],
                         start=(n == 0),
                         stop=(n == len(fields) - 1),
@@ -158,8 +168,8 @@ def tile_picked_zfibi_none_po_kernel(
 
         def shaped(tile, chunk):
             if MODES[chunk] == "T":
-                return tile[:].rearrange("p (t m) -> p t m", t=PACK)
-            return tile[:].rearrange("p (v t) -> p v t", t=PACK)
+                return tile.rearrange("p (t m) -> p t m", t=PACK)
+            return tile.rearrange("p (v t) -> p v t", t=PACK)
 
         right = {}
         left = {}
@@ -170,14 +180,19 @@ def tile_picked_zfibi_none_po_kernel(
         y_bf = {}
 
         def right_factor(chunk, n):
-            bank = psum.tile([P, PACK, P], F32, name="e_bank", tag="ez", bufs=2)
+            bank = psum.tile([P, PACK, P], F32, name="e_bank", tag="ez", bufs=3)
             view = project(bank, chunk, ((2,), (2, 1))[n], 2)
-            e = ring.tile([P, H], F32, name=f"e{n}")
+            if not right:
+                word_tiles["right"] = reused.tile(
+                    [P, 2 * CHUNKS * H], F32, name="right_factors", align_bytes=64, offset=12288
+                )
+            slot = 2 * chunk + n
+            e = word_tiles["right"][:, slot * H : (slot + 1) * H]
             nc.scalar.copy(out=shaped(e, chunk), in_=view)
             right[chunk, n] = e
 
         def left_factor(chunk, n):
-            bank = psum.tile([P, PACK, P], F32, name="h_bank", bufs=4)
+            bank = psum.tile([P, PACK, P], F32, name="h_bank", tag="hy", bufs=5)
             left[chunk, n] = project(bank, chunk, ((1, 0)[n],), 1)
 
         def right_factors(chunk):
@@ -191,7 +206,7 @@ def tile_picked_zfibi_none_po_kernel(
         def multiply(chunk, n):
             term = ring.tile([P, H], F32, name=f"term{n}")
             nc.vector.tensor_tensor(
-                out=shaped(term, chunk), in0=left[chunk, n], in1=shaped(right[chunk, n], chunk), op=MULT
+                out=shaped(term[:], chunk), in0=left[chunk, n], in1=shaped(right[chunk, n], chunk), op=MULT
             )
             terms[chunk, n] = term
 
@@ -201,7 +216,7 @@ def tile_picked_zfibi_none_po_kernel(
             z_bf[chunk] = z
 
         def turn_and_add(chunk):
-            bank = psum.tile([P, PACK, P], F32, name="z_bank", tag="ez", bufs=2)
+            bank = psum.tile([P, PACK, P], F32, name="z_bank", tag="ez", bufs=3)
             for n in range(2):
                 for t in range(PACK):
                     nc.tensor.matmul(
@@ -229,7 +244,7 @@ def tile_picked_zfibi_none_po_kernel(
 
         def last_layer(chunk):
             codes, plane = z_q[chunk]
-            bank = psum.tile([P, PACK, P], F32, name="y_bank", bufs=2)
+            bank = psum.tile([P, PACK, P], F32, name="y_bank", tag="hy", bufs=5)
             for t in range(PACK):
                 nc.tensor.matmul_mx(
                     out=bank[:, t, :],
@@ -242,6 +257,36 @@ def tile_picked_zfibi_none_po_kernel(
                 )
             y_bank[chunk] = bank
 
+        def last_layer_split(chunk):
+            codes, plane = z_q[chunk]
+            y = ring.tile([P, PACK, P], F32, name="y32")
+            for u, copy in enumerate((nc.vector.tensor_copy, nc.scalar.copy)):
+                bank = psum.tile([P, PACK, P], F32, name="y_bank", tag="hy", bufs=5)
+                for t in (2 * u, 2 * u + 1):
+                    nc.tensor.matmul_mx(
+                        out=bank[:, t, :],
+                        lhsT=w3_dealt[:, 2 * P * t : 2 * P * (t + 1)].bitcast(FP4X4),
+                        lhsT_scale=w3_dealt_plane[:, P * t : P * (t + 1)],
+                        rhs=codes[:].bitcast(FP8X4),
+                        rhs_scale=plane[:],
+                        start=True,
+                        stop=True,
+                    )
+                copy(out=y[:, 2 * u : 2 * u + 2, :], in_=bank[:, 2 * u : 2 * u + 2, :])
+            nc.sync.dma_start(out=y_rows[:, :, chunk * P : (chunk + 1) * P], in_=y[:])
+            y32[chunk] = y
+
+        def multiply_halves(chunk, n):
+            term = ring.tile([P, H], F32, name=f"term{n}")
+            for u in range(2):
+                nc.vector.tensor_tensor(
+                    out=shaped(term[:], chunk)[:, 2 * u : 2 * u + 2, :],
+                    in0=left[chunk, n][:, 2 * u : 2 * u + 2, :],
+                    in1=shaped(right[chunk, n], chunk)[:, 2 * u : 2 * u + 2, :],
+                    op=MULT,
+                )
+            terms[chunk, n] = term
+
         def store_y(chunk):
             y = ring.tile([P, PACK, P], F32, name="y32")
             nc.scalar.copy(out=y[:], in_=y_bank[chunk][:])
@@ -252,22 +297,23 @@ def tile_picked_zfibi_none_po_kernel(
         y_plane = keep.tile([P, V], U8, name="y_plane", align_bytes=64)
         y_words = out_1[0].rearrange("p v r -> p (v r)").bitcast(I32)
 
-        def round_y(chunk, how):
-            y = ring.tile([P, P, PACK], BF16, name="y_bf", align_bytes=64)
-            if how == "vs":
-                nc.vector.tensor_copy(out=y[:], in_=y32[chunk][:].rearrange("p t v -> p v t"))
-            elif how == "vp":
-                nc.vector.tensor_copy(out=y[:], in_=y_bank[chunk][:].rearrange("p t v -> p v t"))
-            else:
-                nc.scalar.copy(out=y[:], in_=y_bank[chunk][:].rearrange("p t v -> p v t"))
-            y_bf[chunk] = y
+        y_round = keep.tile([P, V * PACK], BF16, name="y_round", align_bytes=64)
 
-        def quantize_y(chunk):
-            cols = slice(chunk * P, (chunk + 1) * P)
+        def round_y(chunk, how):
+            y = y_round[:, chunk * H : (chunk + 1) * H].rearrange("p (v t) -> p v t", t=PACK)
+            if how == "vs":
+                nc.vector.tensor_copy(out=y, in_=y32[chunk][:].rearrange("p t v -> p v t"))
+            elif how == "vp":
+                nc.vector.tensor_copy(out=y, in_=y_bank[chunk][:].rearrange("p t v -> p v t"))
+            else:
+                nc.scalar.copy(out=y, in_=y_bank[chunk][:].rearrange("p t v -> p v t"))
+
+        def quantize_y(lo, hi):
+            cols = slice(lo * P, hi * P)
             nc.vector.quantize_mx(
                 out=y_codes[:, cols].bitcast(FP8X4),
                 scales=y_plane[:, cols],
-                in_=y_bf[chunk][:].rearrange("p v t -> p (v t)"),
+                in_=y_round[:, lo * H : hi * H],
             )
 
         def store_codes(lo, hi):
@@ -283,52 +329,52 @@ def tile_picked_zfibi_none_po_kernel(
         gather_words(0, 0)
         cast_w1(0)
         cast_w1(1)
-        quantize_w1()
         right_factors(0)
+        gather_words(2, 1)
+        quantize_w1()
         left_factors(0)
         right_factors(1)
         left_factors(1)
-        gather_words(2, 1)
         gather_words(1, 1)
         gather_words(0, 1)
+        deal_plane(nc.vector, w3_dealt_plane, w3_plane)
         right_factors(2)
         multiply(0, 0)
+        left_factor(2, 0)
         multiply(0, 1)
-        right_factors(3)
         turn_and_add(0)
-        left_factors(2)
+        right_factors(3)
+        left_factor(2, 1)
         multiply(1, 0)
         multiply(1, 1)
         turn_and_add(1)
         left_factors(3)
         multiply(2, 0)
         quantize_z(0)
-        last_layer(0)
-        store_y(0)
-        round_y(0, "s")
         multiply(2, 1)
+        last_layer(0)
+        turn_and_add(2)
+        store_y(0)
         multiply(3, 0)
         quantize_z(1)
+        multiply_halves(3, 1)
         last_layer(1)
-        store_y(1)
-        round_y(1, "s")
-        add(2, nc.vector)
-        multiply(3, 1)
+        turn_and_add(3)
         quantize_z(2)
         last_layer(2)
-        add(3, nc.vector)
-        quantize_y(0)
-        quantize_z(3)
-        last_layer(3)
+        round_y(0, "vs")
+        store_y(1)
         store_y(2)
+        quantize_z(3)
+        round_y(1, "vs")
+        quantize_y(0, 2)
+        store_codes(0, 2)
+        last_layer_split(3)
         round_y(2, "vs")
-        quantize_y(1)
-        round_y(3, "vp")
-        store_y(3)
-        quantize_y(2)
-        store_codes(0, 3)
-        quantize_y(3)
-        store_codes(3, 4)
+        quantize_y(2, 3)
+        round_y(3, "vs")
+        quantize_y(3, 4)
+        store_codes(2, 4)
         store_plane(nc.sync, 0)
         store_plane(nc.scalar, 1)
         store_plane(nc.sync, 2)

@@ -19,17 +19,44 @@ ADD = mybir.AluOpType.add
 
 P = 128
 PACK = 4
-QUADS = 4
+QUADRANTS = 4
+LIST_ROWS = 16
 GATHER = 256
 CHUNKS = V // P
-MODES = "TTTT"
+TURNED_CHUNKS = 2
+SCALAR_READ_BANKS = 3
+HELD_BANKS = 5
+
+LEFT_FIELD = (1, 0)
+RIGHT_FIELDS = ((2,), (2, 1))
+
+SCALE_TABLE_AT = EARLY_WORDS_AT = 0
+W1_ROUNDED_AT = LATE_WORDS_AT = 4096
+W1_HALVES_AT = (8192, 12288)
+RIGHT_FACTORS_AT = W1_HALVES_AT[1]
+EARLY_GATHERS = ((2, 0), (1, 0), (0, 0), (2, 1))
+LATE_GATHERS = ((1, 1), (0, 1))
 
 
-def load_scale_rows(queue, plane, rows):
-    for q in range(QUADS):
-        queue.dma_start(
+def load_plane(nc, plane, rows):
+    for q in range(QUADRANTS):
+        nc.sync.dma_start(
             out=plane[32 * q : 32 * q + 4, :].bitcast(I32), in_=rows[0, 4 * q : 4 * q + 4, :].bitcast(I32)
         )
+
+
+def deal_codes(engine, dealt, codes):
+    engine.tensor_copy(
+        out=dealt[:].rearrange("k (t p b) -> k t p b", t=PACK, b=2),
+        in_=codes[:].rearrange("k (p t b) -> k t p b", t=PACK, b=2),
+    )
+
+
+def deal_plane(engine, dealt, plane):
+    engine.tensor_copy(
+        out=dealt[:].rearrange("k (t p) -> k t p", t=PACK),
+        in_=plane[:].rearrange("k (p t) -> k t p", t=PACK),
+    )
 
 
 def tile_picked_zfibi_none_po_kernel(
@@ -38,19 +65,19 @@ def tile_picked_zfibi_none_po_kernel(
     nc = tc.nc
     with ExitStack() as ctx:
         keep = ctx.enter_context(tc.tile_pool(name="keep", bufs=1))
-        ring = ctx.enter_context(tc.tile_pool(name="ring", bufs=4))
+        ring = ctx.enter_context(tc.tile_pool(name="ring", bufs=CHUNKS))
         reused = ctx.enter_context(tc.tile_pool(name="reused", bufs=1))
         psum = ctx.enter_context(tc.psum_pool(name="psum", bufs=1))
 
-        offsets = keep.tile([P, S // 16], U16, name="offsets")
-        x_scale_table = reused.tile([P, T], U8, name="x_scale_table", align_bytes=64, offset=0)
+        offsets = keep.tile([P, S // LIST_ROWS], U16, name="offsets")
+        x_scale_table = reused.tile([P, T], U8, name="x_scale_table", align_bytes=64, offset=SCALE_TABLE_AT)
         x_word_table = keep.tile([P, T], I32, name="x_word_table", align_bytes=64)
         w2_codes = keep.tile([P, 2 * H], U8, name="w2_codes", align_bytes=64)
         w2_plane = keep.tile([P, H], U8, name="w2_plane", align_bytes=64)
         w3_codes = keep.tile([P, 2 * N], U8, name="w3_codes", align_bytes=64)
         w3_plane = keep.tile([P, N], U8, name="w3_plane", align_bytes=64)
-        w1_raw = [
-            reused.tile([P, PACK, H // 2], F32, name=f"w1_raw{u}", align_bytes=64, offset=8192 + 4096 * u)
+        w1_halves = [
+            reused.tile([P, PACK, H // 2], F32, name=f"w1_half{u}", align_bytes=64, offset=W1_HALVES_AT[u])
             for u in range(2)
         ]
         w1_rows = w1.rearrange("(p j) c -> p j c", j=PACK)
@@ -62,161 +89,134 @@ def tile_picked_zfibi_none_po_kernel(
         nc.sync.dma_start(offsets[:], offs)
         nc.sync.dma_start(out=w3_codes[:].bitcast(I32), in_=w3_words[0].bitcast(I32))
         nc.sync.dma_start(out=w2_codes[:].bitcast(I32), in_=w2_words[0].bitcast(I32))
-        load_scale_rows(nc.sync, x_scale_table, x_scales)
+        load_plane(nc, x_scale_table, x_scales)
         nc.sync.dma_start(out=x_word_table[:], in_=x_words[0].rearrange("p c r -> p (c r)").bitcast(I32))
-        nc.sync.dma_start(out=w1_raw[0][:], in_=w1_rows[:, :, 0 : H // 2])
-        load_scale_rows(nc.sync, w2_plane, w2_scales)
-        nc.sync.dma_start(out=w1_raw[1][:], in_=w1_rows[:, :, H // 2 : H])
-        load_scale_rows(nc.sync, w3_plane, w3_scales)
+        nc.sync.dma_start(out=w1_halves[0][:], in_=w1_rows[:, :, 0 : H // 2])
+        load_plane(nc, w2_plane, w2_scales)
+        nc.sync.dma_start(out=w1_halves[1][:], in_=w1_rows[:, :, H // 2 : H])
+        load_plane(nc, w3_plane, w3_scales)
         identity = keep.tile([P, P], F32, name="identity", align_bytes=64)
         make_identity(nc, identity[:])
 
+        w2_dealt = keep.tile([P, 2 * H], U8, name="w2_dealt", align_bytes=64)
+        w2_dealt_plane = keep.tile([P, H], U8, name="w2_dealt_plane", align_bytes=64)
         w3_dealt = keep.tile([P, 2 * N], U8, name="w3_dealt", align_bytes=64)
         w3_dealt_plane = keep.tile([P, N], U8, name="w3_dealt_plane", align_bytes=64)
-
-        def deal_codes(engine, dealt, codes):
-            engine.tensor_copy(
-                out=dealt[:].rearrange("p (t m b) -> p t m b", t=PACK, b=2),
-                in_=codes[:].rearrange("p (m t b) -> p t m b", t=PACK, b=2),
-            )
-
-        def deal_plane(engine, dealt, plane):
-            engine.tensor_copy(
-                out=dealt[:].rearrange("p (t m) -> p t m", t=PACK),
-                in_=plane[:].rearrange("p (m t) -> p t m", t=PACK),
-            )
-
         picked_scales = keep.tile([P, S], U8, name="picked_scales", align_bytes=64)
 
-        def gather_scales():
-            nc.vector.tensor_copy(picked_scales[:], x_scale_table[:].indirect(offsets[:]))
-
         deal_codes(nc.vector, w3_dealt, w3_codes)
-        gather_scales()
-        early_words = reused.tile([P, 4 * GATHER], U32, name="early_words", align_bytes=64, offset=0)
-        word_tiles = {"early": early_words}
-        places = {
-            (2, 0): ("early", 0), (1, 0): ("early", 1), (0, 0): ("early", 2), (2, 1): ("early", 3),
-            (1, 1): ("late", 0), (0, 1): ("late", 1),
-        }
+        nc.vector.tensor_copy(picked_scales[:], x_scale_table[:].indirect(offsets[:]))
+        deal_codes(nc.gpsimd, w2_dealt, w2_codes)
+        deal_plane(nc.gpsimd, w2_dealt_plane, w2_plane)
+        deal_plane(nc.gpsimd, w3_dealt_plane, w3_plane)
 
-        def picked(field, record, count):
-            half, inner = divmod(record, GATHER)
-            tile_name, slot = places[field, half]
-            first = slot * GATHER + inner
-            return word_tiles[tile_name][:, first : first + count]
+        picked_words = {}
+
+        def place_words(gathers, name, offset):
+            tile = reused.tile([P, len(gathers) * GATHER], U32, name=name, align_bytes=64, offset=offset)
+            for slot, key in enumerate(gathers):
+                picked_words[key] = tile[:, slot * GATHER : (slot + 1) * GATHER]
 
         def gather_words(field, half):
             first = field * V + half * GATHER
-            nc.vector.tensor_copy(
-                picked(field, half * GATHER, GATHER),
-                x_word_table[:].bitcast(U32).indirect(offsets[:, first // 16 : (first + GATHER) // 16]),
-            )
+            entries = offsets[:, first // LIST_ROWS : (first + GATHER) // LIST_ROWS]
+            nc.vector.tensor_copy(picked_words[field, half], x_word_table[:].bitcast(U32).indirect(entries))
 
-        w1_bf = reused.tile([P, H, PACK], BF16, name="w1_bf", align_bytes=64, offset=4096)
+        def picked(field, chunk):
+            half, inner = divmod(chunk * P, GATHER)
+            first = field * V + chunk * P
+            return picked_words[field, half][:, inner : inner + P].bitcast(FP8X4), picked_scales[:, first : first + P]
+
+        w1_rounded = reused.tile([P, PACK, P, PACK], BF16, name="w1_rounded", align_bytes=64, offset=W1_ROUNDED_AT)
         w1_codes = keep.tile([P, H], U32, name="w1_codes", align_bytes=64)
         w1_plane = keep.tile([P, H], U8, name="w1_plane", align_bytes=64)
 
-        def cast_w1(u):
+        def round_w1(u):
             nc.scalar.copy(
-                out=w1_bf[:, u * (H // 2) : (u + 1) * (H // 2), :].rearrange("p (c i) j -> p c j i", i=4),
-                in_=w1_raw[u][:].rearrange("p j (c i) -> p c j i", i=4),
+                out=w1_rounded[:, :, u * (P // 2) : (u + 1) * (P // 2), :].rearrange("p t m j -> p m j t"),
+                in_=w1_halves[u][:].rearrange("p j (m t) -> p m j t", t=PACK),
             )
 
         def quantize_w1():
             nc.vector.quantize_mx(
                 out=w1_codes[:].bitcast(FP8X4),
                 scales=w1_plane[:],
-                in_=w1_bf[:].rearrange("p c j -> p (c j)"),
+                in_=w1_rounded[:].rearrange("p t m j -> p (t m j)"),
             )
-            word_tiles["late"] = reused.tile([P, 2 * GATHER], U32, name="late_words", align_bytes=64, offset=4096)
 
-        def weights(which, lo, hi):
-            if which == 1:
-                return w1_codes[:, lo:hi].bitcast(FP8X4), w1_plane[:, lo:hi]
-            return w2_codes[:, 2 * lo : 2 * hi].bitcast(FP4X4), w2_plane[:, lo:hi]
+        def records_stationary(bank, chunk, fields, codes, plane):
+            for n, field in enumerate(fields):
+                words, scales = picked(field, chunk)
+                nc.tensor.matmul_mx(
+                    out=bank[:].rearrange("p a b -> p (a b)"),
+                    lhsT=words,
+                    lhsT_scale=scales,
+                    rhs=codes,
+                    rhs_scale=plane,
+                    start=(n == 0),
+                    stop=(n == len(fields) - 1),
+                )
 
-        def project(bank, chunk, fields, which):
-            if MODES[chunk] == "T":
-                codes, plane = weights(which, 0, H)
-                for n, field in enumerate(fields):
-                    first = field * V + chunk * P
-                    nc.tensor.matmul_mx(
-                        out=bank[:].rearrange("p t m -> p (t m)"),
-                        lhsT=picked(field, chunk * P, P).bitcast(FP8X4),
-                        lhsT_scale=picked_scales[:, first : first + P],
-                        rhs=codes,
-                        rhs_scale=plane,
-                        start=(n == 0),
-                        stop=(n == len(fields) - 1),
-                    )
-                return bank[:].rearrange("p a b -> p (a b)").rearrange("p (m t) -> p t m", t=PACK)
+        def weights_stationary(bank, dealt_slice, moving):
             for t in range(PACK):
-                codes, plane = weights(which, t * P, (t + 1) * P)
-                for n, field in enumerate(fields):
-                    first = field * V + chunk * P
+                codes, plane = dealt_slice(t)
+                for n, (words, scales) in enumerate(moving):
                     nc.tensor.matmul_mx(
                         out=bank[:, t, :],
                         lhsT=codes,
                         lhsT_scale=plane,
-                        rhs=picked(field, chunk * P, P).bitcast(FP8X4),
-                        rhs_scale=picked_scales[:, first : first + P],
+                        rhs=words,
+                        rhs_scale=scales,
                         start=(n == 0),
-                        stop=(n == len(fields) - 1),
+                        stop=(n == len(moving) - 1),
                     )
-            return bank[:].rearrange("p t v -> p v t")
 
-        def shaped(tile, chunk):
-            if MODES[chunk] == "T":
-                return tile.rearrange("p (t m) -> p t m", t=PACK)
-            return tile.rearrange("p (v t) -> p v t", t=PACK)
+        def w1_slice(t):
+            return w1_codes[:, t * P : (t + 1) * P].bitcast(FP8X4), w1_plane[:, t * P : (t + 1) * P]
 
-        right = {}
-        left = {}
-        terms = {}
-        z_bf = {}
-        z_q = {}
-        y32 = {}
-        y_bf = {}
+        def w2_slice(t):
+            return w2_dealt[:, 2 * t * P : 2 * (t + 1) * P].bitcast(FP4X4), w2_dealt_plane[:, t * P : (t + 1) * P]
 
-        def right_factor(chunk, n):
-            bank = psum.tile([P, PACK, P], F32, name="e_bank", tag="ez", bufs=3)
-            view = project(bank, chunk, ((2,), (2, 1))[n], 2)
-            if not right:
-                word_tiles["right"] = reused.tile(
-                    [P, 2 * CHUNKS * H], F32, name="right_factors", align_bytes=64, offset=12288
-                )
+        def w3_slice(t):
+            return w3_dealt[:, 2 * t * P : 2 * (t + 1) * P].bitcast(FP4X4), w3_dealt_plane[:, t * P : (t + 1) * P]
+
+        def in_chunk_layout(flat, chunk):
+            if chunk < TURNED_CHUNKS:
+                return flat.rearrange("p (t m) -> p t m", t=PACK)
+            return flat.rearrange("p (v t) -> p v t", t=PACK)
+
+        right, left, terms, z_rounded, z_quantised, y_bank, y_values = {}, {}, {}, {}, {}, {}, {}
+
+        def right_factor(chunk, n, right_all):
+            bank = psum.tile([P, PACK, P], F32, name="right_bank", tag="scalar_read", bufs=SCALAR_READ_BANKS)
+            if chunk < TURNED_CHUNKS:
+                records_stationary(bank, chunk, RIGHT_FIELDS[n], w2_codes[:].bitcast(FP4X4), w2_plane[:])
+                view = bank[:].rearrange("p a b -> p (a b)").rearrange("p (m t) -> p t m", t=PACK)
+            else:
+                weights_stationary(bank, w2_slice, [picked(field, chunk) for field in RIGHT_FIELDS[n]])
+                view = bank[:].rearrange("p t v -> p v t")
             slot = 2 * chunk + n
-            e = word_tiles["right"][:, slot * H : (slot + 1) * H]
-            nc.scalar.copy(out=shaped(e, chunk), in_=view)
-            right[chunk, n] = e
+            right[chunk, n] = in_chunk_layout(right_all[:, slot * H : (slot + 1) * H], chunk)
+            nc.scalar.copy(out=right[chunk, n], in_=view)
 
         def left_factor(chunk, n):
-            bank = psum.tile([P, PACK, P], F32, name="h_bank", tag="hy", bufs=5)
-            left[chunk, n] = project(bank, chunk, ((1, 0)[n],), 1)
-
-        def right_factors(chunk):
-            right_factor(chunk, 0)
-            right_factor(chunk, 1)
-
-        def left_factors(chunk):
-            left_factor(chunk, 0)
-            left_factor(chunk, 1)
+            bank = psum.tile([P, PACK, P], F32, name="left_bank", tag="held", bufs=HELD_BANKS)
+            if chunk < TURNED_CHUNKS:
+                records_stationary(bank, chunk, (LEFT_FIELD[n],), w1_codes[:].bitcast(FP8X4), w1_plane[:])
+                left[chunk, n] = bank[:]
+            else:
+                weights_stationary(bank, w1_slice, [picked(LEFT_FIELD[n], chunk)])
+                left[chunk, n] = bank[:].rearrange("p t v -> p v t")
 
         def multiply(chunk, n):
             term = ring.tile([P, H], F32, name=f"term{n}")
             nc.vector.tensor_tensor(
-                out=shaped(term[:], chunk), in0=left[chunk, n], in1=shaped(right[chunk, n], chunk), op=MULT
+                out=in_chunk_layout(term[:], chunk), in0=left[chunk, n], in1=right[chunk, n], op=MULT
             )
             terms[chunk, n] = term
 
-        def add(chunk, engine):
-            z = ring.tile([P, H], BF16, name="z_bf", align_bytes=64)
-            engine.tensor_tensor(out=z[:], in0=terms[chunk, 0][:], in1=terms[chunk, 1][:], op=ADD)
-            z_bf[chunk] = z
-
         def turn_and_add(chunk):
-            bank = psum.tile([P, PACK, P], F32, name="z_bank", tag="ez", bufs=3)
+            bank = psum.tile([P, PACK, P], F32, name="z_bank", tag="scalar_read", bufs=SCALAR_READ_BANKS)
             for n in range(2):
                 for t in range(PACK):
                     nc.tensor.matmul(
@@ -227,155 +227,131 @@ def tile_picked_zfibi_none_po_kernel(
                         start=(n == 0 and t == 0),
                         stop=(n == 1 and t == PACK - 1),
                     )
-            z = ring.tile([P, H], BF16, name="z_bf", align_bytes=64)
-            nc.scalar.copy(
-                out=z[:].rearrange("p (v t) -> p v t", t=PACK), in_=bank[:].rearrange("p t v -> p v t")
-            )
-            z_bf[chunk] = z
+            z = ring.tile([P, H], BF16, name="z_rounded", align_bytes=64)
+            nc.scalar.copy(out=z[:].rearrange("p (v t) -> p v t", t=PACK), in_=bank[:].rearrange("p t v -> p v t"))
+            z_rounded[chunk] = z
+
+        def add(chunk):
+            z = ring.tile([P, H], BF16, name="z_rounded", align_bytes=64)
+            nc.vector.tensor_tensor(out=z[:], in0=terms[chunk, 0][:], in1=terms[chunk, 1][:], op=ADD)
+            z_rounded[chunk] = z
 
         def quantize_z(chunk):
             codes = ring.tile([P, P], U32, name="z_codes", align_bytes=64)
             plane = ring.tile([P, P], U8, name="z_plane", align_bytes=64)
-            nc.vector.quantize_mx(out=codes[:].bitcast(FP8X4), scales=plane[:], in_=z_bf[chunk][:])
-            z_q[chunk] = (codes, plane)
+            nc.vector.quantize_mx(out=codes[:].bitcast(FP8X4), scales=plane[:], in_=z_rounded[chunk][:])
+            z_quantised[chunk] = (codes[:].bitcast(FP8X4), plane[:])
 
         y_rows = out_0.rearrange("(p t) v -> p t v", t=PACK)
-        y_bank = {}
+        y_codes = keep.tile([P, V], I32, name="y_codes", align_bytes=64)
+        y_plane = keep.tile([P, V], U8, name="y_plane", align_bytes=64)
+        y_rounded = keep.tile([P, V * PACK], BF16, name="y_rounded", align_bytes=64)
+        y_words = out_1[0].rearrange("p v r -> p (v r)").bitcast(I32)
 
         def last_layer(chunk):
-            codes, plane = z_q[chunk]
-            bank = psum.tile([P, PACK, P], F32, name="y_bank", tag="hy", bufs=5)
-            for t in range(PACK):
-                nc.tensor.matmul_mx(
-                    out=bank[:, t, :],
-                    lhsT=w3_dealt[:, 2 * P * t : 2 * P * (t + 1)].bitcast(FP4X4),
-                    lhsT_scale=w3_dealt_plane[:, P * t : P * (t + 1)],
-                    rhs=codes[:].bitcast(FP8X4),
-                    rhs_scale=plane[:],
-                    start=True,
-                    stop=True,
-                )
+            bank = psum.tile([P, PACK, P], F32, name="y_bank", tag="held", bufs=HELD_BANKS)
+            weights_stationary(bank, w3_slice, [z_quantised[chunk]])
             y_bank[chunk] = bank
 
-        def last_layer_split(chunk):
-            codes, plane = z_q[chunk]
-            y = ring.tile([P, PACK, P], F32, name="y32")
+        def store_y(chunk):
+            y = ring.tile([P, PACK, P], F32, name="y")
+            nc.scalar.copy(out=y[:], in_=y_bank[chunk][:])
+            nc.sync.dma_start(out=y_rows[:, :, chunk * P : (chunk + 1) * P], in_=y[:])
+            y_values[chunk] = y
+
+        def last_layer_in_two_banks(chunk):
+            words, scales = z_quantised[chunk]
+            y = ring.tile([P, PACK, P], F32, name="y")
             for u, copy in enumerate((nc.vector.tensor_copy, nc.scalar.copy)):
-                bank = psum.tile([P, PACK, P], F32, name="y_bank", tag="hy", bufs=5)
+                bank = psum.tile([P, PACK, P], F32, name="y_bank", tag="held", bufs=HELD_BANKS)
                 for t in (2 * u, 2 * u + 1):
+                    codes, plane = w3_slice(t)
                     nc.tensor.matmul_mx(
-                        out=bank[:, t, :],
-                        lhsT=w3_dealt[:, 2 * P * t : 2 * P * (t + 1)].bitcast(FP4X4),
-                        lhsT_scale=w3_dealt_plane[:, P * t : P * (t + 1)],
-                        rhs=codes[:].bitcast(FP8X4),
-                        rhs_scale=plane[:],
-                        start=True,
-                        stop=True,
+                        out=bank[:, t, :], lhsT=codes, lhsT_scale=plane, rhs=words, rhs_scale=scales,
+                        start=True, stop=True,
                     )
                 copy(out=y[:, 2 * u : 2 * u + 2, :], in_=bank[:, 2 * u : 2 * u + 2, :])
             nc.sync.dma_start(out=y_rows[:, :, chunk * P : (chunk + 1) * P], in_=y[:])
-            y32[chunk] = y
+            y_values[chunk] = y
 
-        def multiply_halves(chunk, n):
-            term = ring.tile([P, H], F32, name=f"term{n}")
-            for u in range(2):
-                nc.vector.tensor_tensor(
-                    out=shaped(term[:], chunk)[:, 2 * u : 2 * u + 2, :],
-                    in0=left[chunk, n][:, 2 * u : 2 * u + 2, :],
-                    in1=shaped(right[chunk, n], chunk)[:, 2 * u : 2 * u + 2, :],
-                    op=MULT,
-                )
-            terms[chunk, n] = term
+        def round_y(chunk, copy, source):
+            copy(
+                out=y_rounded[:, chunk * H : (chunk + 1) * H].rearrange("p (v t) -> p v t", t=PACK),
+                in_=source[chunk][:].rearrange("p t v -> p v t"),
+            )
 
-        def store_y(chunk):
-            y = ring.tile([P, PACK, P], F32, name="y32")
-            nc.scalar.copy(out=y[:], in_=y_bank[chunk][:])
-            nc.sync.dma_start(out=y_rows[:, :, chunk * P : (chunk + 1) * P], in_=y[:])
-            y32[chunk] = y
-
-        y_codes = keep.tile([P, V], I32, name="y_codes", align_bytes=64)
-        y_plane = keep.tile([P, V], U8, name="y_plane", align_bytes=64)
-        y_words = out_1[0].rearrange("p v r -> p (v r)").bitcast(I32)
-
-        y_round = keep.tile([P, V * PACK], BF16, name="y_round", align_bytes=64)
-
-        def round_y(chunk, how):
-            y = y_round[:, chunk * H : (chunk + 1) * H].rearrange("p (v t) -> p v t", t=PACK)
-            if how == "vs":
-                nc.vector.tensor_copy(out=y, in_=y32[chunk][:].rearrange("p t v -> p v t"))
-            elif how == "vp":
-                nc.vector.tensor_copy(out=y, in_=y_bank[chunk][:].rearrange("p t v -> p v t"))
-            else:
-                nc.scalar.copy(out=y, in_=y_bank[chunk][:].rearrange("p t v -> p v t"))
-
-        def quantize_y(lo, hi):
-            cols = slice(lo * P, hi * P)
+        def quantize_y(first, end):
             nc.vector.quantize_mx(
-                out=y_codes[:, cols].bitcast(FP8X4),
-                scales=y_plane[:, cols],
-                in_=y_round[:, lo * H : hi * H],
+                out=y_codes[:, first * P : end * P].bitcast(FP8X4),
+                scales=y_plane[:, first * P : end * P],
+                in_=y_rounded[:, first * H : end * H],
             )
 
-        def store_codes(lo, hi):
-            nc.sync.dma_start(out=y_words[:, lo * P : hi * P], in_=y_codes[:, lo * P : hi * P])
+        def store_codes(first, end):
+            nc.sync.dma_start(out=y_words[:, first * P : end * P], in_=y_codes[:, first * P : end * P])
 
-        def store_plane(queue, q):
-            queue.dma_start(
-                out=out_2[0, 4 * q : 4 * q + 4, :].bitcast(I32), in_=y_plane[32 * q : 32 * q + 4, :].bitcast(I32)
-            )
-
-        gather_words(2, 0)
-        gather_words(1, 0)
-        gather_words(0, 0)
-        cast_w1(0)
-        cast_w1(1)
-        right_factors(0)
+        place_words(EARLY_GATHERS, "early_words", EARLY_WORDS_AT)
+        for field in (2, 1, 0):
+            gather_words(field, 0)
+        round_w1(0)
+        round_w1(1)
+        right_all = reused.tile([P, 2 * CHUNKS * H], F32, name="right_all", align_bytes=64, offset=RIGHT_FACTORS_AT)
+        right_factor(0, 0, right_all)
+        right_factor(0, 1, right_all)
         gather_words(2, 1)
         quantize_w1()
-        left_factors(0)
-        right_factors(1)
-        left_factors(1)
+        place_words(LATE_GATHERS, "late_words", LATE_WORDS_AT)
+        left_factor(0, 0)
+        left_factor(0, 1)
+        right_factor(1, 0, right_all)
+        right_factor(1, 1, right_all)
+        left_factor(1, 0)
+        left_factor(1, 1)
         gather_words(1, 1)
         gather_words(0, 1)
-        deal_plane(nc.vector, w3_dealt_plane, w3_plane)
-        right_factors(2)
+
+        right_factor(2, 0, right_all)
+        right_factor(2, 1, right_all)
         multiply(0, 0)
         left_factor(2, 0)
         multiply(0, 1)
         turn_and_add(0)
-        right_factors(3)
+        right_factor(3, 0, right_all)
+        right_factor(3, 1, right_all)
         left_factor(2, 1)
         multiply(1, 0)
         multiply(1, 1)
         turn_and_add(1)
-        left_factors(3)
+        left_factor(3, 0)
+        left_factor(3, 1)
+
         multiply(2, 0)
         quantize_z(0)
         multiply(2, 1)
         last_layer(0)
-        turn_and_add(2)
         store_y(0)
         multiply(3, 0)
         quantize_z(1)
-        multiply_halves(3, 1)
         last_layer(1)
-        turn_and_add(3)
+        store_y(1)
+        add(2)
+        multiply(3, 1)
         quantize_z(2)
         last_layer(2)
-        round_y(0, "vs")
-        store_y(1)
+        add(3)
+
+        round_y(0, nc.scalar.copy, y_bank)
         store_y(2)
         quantize_z(3)
-        round_y(1, "vs")
+        round_y(1, nc.scalar.copy, y_bank)
+        last_layer_in_two_banks(3)
         quantize_y(0, 2)
         store_codes(0, 2)
-        last_layer_split(3)
-        round_y(2, "vs")
-        quantize_y(2, 3)
-        round_y(3, "vs")
-        quantize_y(3, 4)
+        for chunk in (2, 3):
+            round_y(chunk, nc.vector.tensor_copy, y_values)
+            quantize_y(chunk, chunk + 1)
         store_codes(2, 4)
-        store_plane(nc.sync, 0)
-        store_plane(nc.scalar, 1)
-        store_plane(nc.sync, 2)
-        store_plane(nc.scalar, 3)
+        for q in range(QUADRANTS):
+            (nc.sync, nc.scalar)[q % 2].dma_start(
+                out=out_2[0, 4 * q : 4 * q + 4, :].bitcast(I32), in_=y_plane[32 * q : 32 * q + 4, :].bitcast(I32)
+            )

@@ -1,7 +1,6 @@
 from contextlib import ExitStack
 
 import concourse.mybir as mybir
-from concourse.masks import make_identity
 
 K, T, S, V, H, N = 512, 2048, 1536, 512, 512, 512
 FLOPS = 5 * 2 * K * H * V
@@ -23,19 +22,19 @@ QUADRANTS = 4
 LIST_ROWS = 16
 GATHER = 256
 CHUNKS = V // P
-TURNED_CHUNKS = 2
-SCALAR_READ_BANKS = 3
-HELD_BANKS = 5
+BANK_BYTES = 2048
 
 LEFT_FIELD = (1, 0)
 RIGHT_FIELDS = ((2,), (2, 1))
 
 SCALE_TABLE_AT = EARLY_WORDS_AT = 0
-W1_ROUNDED_AT = LATE_WORDS_AT = 4096
-W1_HALVES_AT = (8192, 12288)
-RIGHT_FACTORS_AT = W1_HALVES_AT[1]
-EARLY_GATHERS = ((2, 0), (1, 0), (0, 0), (2, 1))
-LATE_GATHERS = ((1, 1), (0, 1))
+W1_LOW_AT = 4096
+W1_HIGH_AT = 24576
+RIGHT_ALL_AT = W1_HIGH_AT - 7 * 2048 + 64
+RIGHT_10_AT = W1_HIGH_AT + 64
+WORDS_0A_AT = RIGHT_10_AT + 2048
+TERM_AT = (36864, 40960, 43008, 45056, 36864 - 2048 + 64, 36864 + 64)
+Z_AT = 47104
 
 
 def load_plane(nc, plane, rows):
@@ -77,7 +76,7 @@ def tile_picked_zfibi_none_po_kernel(
         w3_codes = keep.tile([P, 2 * N], U8, name="w3_codes", align_bytes=64)
         w3_plane = keep.tile([P, N], U8, name="w3_plane", align_bytes=64)
         w1_halves = [
-            reused.tile([P, PACK, H // 2], F32, name=f"w1_half{u}", align_bytes=64, offset=W1_HALVES_AT[u])
+            reused.tile([P, PACK, H // 2], F32, name=f"w1_half{u}", align_bytes=64, offset=(W1_LOW_AT, W1_HIGH_AT)[u])
             for u in range(2)
         ]
         w1_rows = w1.rearrange("(p j) c -> p j c", j=PACK)
@@ -87,47 +86,48 @@ def tile_picked_zfibi_none_po_kernel(
         nc.vector.memset(w2_plane[:].bitcast(I32), 0)
         nc.vector.memset(w3_plane[:].bitcast(I32), 0)
         nc.sync.dma_start(offsets[:], offs)
-        nc.sync.dma_start(out=w3_codes[:].bitcast(I32), in_=w3_words[0].bitcast(I32))
         nc.sync.dma_start(out=w2_codes[:].bitcast(I32), in_=w2_words[0].bitcast(I32))
         load_plane(nc, x_scale_table, x_scales)
         nc.sync.dma_start(out=x_word_table[:], in_=x_words[0].rearrange("p c r -> p (c r)").bitcast(I32))
-        nc.sync.dma_start(out=w1_halves[0][:], in_=w1_rows[:, :, 0 : H // 2])
         load_plane(nc, w2_plane, w2_scales)
+        nc.sync.dma_start(out=w1_halves[0][:], in_=w1_rows[:, :, 0 : H // 2])
         nc.sync.dma_start(out=w1_halves[1][:], in_=w1_rows[:, :, H // 2 : H])
+        nc.sync.dma_start(out=w3_codes[:].bitcast(I32), in_=w3_words[0].bitcast(I32))
         load_plane(nc, w3_plane, w3_scales)
-        identity = keep.tile([P, P], F32, name="identity", align_bytes=64)
-        make_identity(nc, identity[:])
 
         w2_dealt = keep.tile([P, 2 * H], U8, name="w2_dealt", align_bytes=64)
         w2_dealt_plane = keep.tile([P, H], U8, name="w2_dealt_plane", align_bytes=64)
         w3_dealt = keep.tile([P, 2 * N], U8, name="w3_dealt", align_bytes=64)
         w3_dealt_plane = keep.tile([P, N], U8, name="w3_dealt_plane", align_bytes=64)
-        picked_scales = keep.tile([P, S], U8, name="picked_scales", align_bytes=64)
+        picked_scales = {}
 
-        deal_codes(nc.vector, w3_dealt, w3_codes)
-        nc.vector.tensor_copy(picked_scales[:], x_scale_table[:].indirect(offsets[:]))
+        def gather_scales(first, end, tile):
+            entries = offsets[:, first * V // LIST_ROWS : end * V // LIST_ROWS]
+            nc.vector.tensor_copy(tile[:], x_scale_table[:].indirect(entries))
+            for field in range(first, end):
+                picked_scales[field] = tile[:, (field - first) * V : (field - first + 1) * V]
+
+        scales_12 = keep.tile([P, 2 * V], U8, name="scales_12", align_bytes=64)
+        gather_scales(1, 3, scales_12)
         deal_codes(nc.gpsimd, w2_dealt, w2_codes)
         deal_plane(nc.gpsimd, w2_dealt_plane, w2_plane)
+        deal_codes(nc.gpsimd, w3_dealt, w3_codes)
         deal_plane(nc.gpsimd, w3_dealt_plane, w3_plane)
 
         picked_words = {}
 
-        def place_words(gathers, name, offset):
-            tile = reused.tile([P, len(gathers) * GATHER], U32, name=name, align_bytes=64, offset=offset)
-            for slot, key in enumerate(gathers):
-                picked_words[key] = tile[:, slot * GATHER : (slot + 1) * GATHER]
-
-        def gather_words(field, half):
+        def gather_words(field, half, words):
             first = field * V + half * GATHER
             entries = offsets[:, first // LIST_ROWS : (first + GATHER) // LIST_ROWS]
-            nc.vector.tensor_copy(picked_words[field, half], x_word_table[:].bitcast(U32).indirect(entries))
+            nc.vector.tensor_copy(words, x_word_table[:].bitcast(U32).indirect(entries))
+            picked_words[field, half] = words
 
         def picked(field, chunk):
             half, inner = divmod(chunk * P, GATHER)
-            first = field * V + chunk * P
-            return picked_words[field, half][:, inner : inner + P].bitcast(FP8X4), picked_scales[:, first : first + P]
+            scales = picked_scales[field][:, chunk * P : (chunk + 1) * P]
+            return picked_words[field, half][:, inner : inner + P].bitcast(FP8X4), scales
 
-        w1_rounded = reused.tile([P, PACK, P, PACK], BF16, name="w1_rounded", align_bytes=64, offset=W1_ROUNDED_AT)
+        w1_rounded = keep.tile([P, PACK, P, PACK], BF16, name="w1_rounded", align_bytes=64)
         w1_codes = keep.tile([P, H], U32, name="w1_codes", align_bytes=64)
         w1_plane = keep.tile([P, H], U8, name="w1_plane", align_bytes=64)
 
@@ -144,21 +144,8 @@ def tile_picked_zfibi_none_po_kernel(
                 in_=w1_rounded[:].rearrange("p t m j -> p (t m j)"),
             )
 
-        def records_stationary(bank, chunk, fields, codes, plane):
-            for n, field in enumerate(fields):
-                words, scales = picked(field, chunk)
-                nc.tensor.matmul_mx(
-                    out=bank[:].rearrange("p a b -> p (a b)"),
-                    lhsT=words,
-                    lhsT_scale=scales,
-                    rhs=codes,
-                    rhs_scale=plane,
-                    start=(n == 0),
-                    stop=(n == len(fields) - 1),
-                )
-
-        def weights_stationary(bank, dealt_slice, moving):
-            for t in range(PACK):
+        def weights_stationary(bank, dealt_slice, moving, slices=range(PACK)):
+            for t in slices:
                 codes, plane = dealt_slice(t)
                 for n, (words, scales) in enumerate(moving):
                     nc.tensor.matmul_mx(
@@ -180,76 +167,57 @@ def tile_picked_zfibi_none_po_kernel(
         def w3_slice(t):
             return w3_dealt[:, 2 * t * P : 2 * (t + 1) * P].bitcast(FP4X4), w3_dealt_plane[:, t * P : (t + 1) * P]
 
-        def in_chunk_layout(flat, chunk):
-            if chunk < TURNED_CHUNKS:
-                return flat.rearrange("p (t m) -> p t m", t=PACK)
+        def interleaved(flat):
             return flat.rearrange("p (v t) -> p v t", t=PACK)
 
         right, left, terms, z_rounded, z_quantised, y_bank, y_values = {}, {}, {}, {}, {}, {}, {}
 
-        def right_factor(chunk, n, right_all):
-            bank = psum.tile([P, PACK, P], F32, name="right_bank", tag="scalar_read", bufs=SCALAR_READ_BANKS)
-            if chunk < TURNED_CHUNKS:
-                records_stationary(bank, chunk, RIGHT_FIELDS[n], w2_codes[:].bitcast(FP4X4), w2_plane[:])
-                view = bank[:].rearrange("p a b -> p (a b)").rearrange("p (m t) -> p t m", t=PACK)
-            else:
-                weights_stationary(bank, w2_slice, [picked(field, chunk) for field in RIGHT_FIELDS[n]])
-                view = bank[:].rearrange("p t v -> p v t")
-            slot = 2 * chunk + n
-            right[chunk, n] = in_chunk_layout(right_all[:, slot * H : (slot + 1) * H], chunk)
-            nc.scalar.copy(out=right[chunk, n], in_=view)
+        def bank_at(name, index):
+            return psum.tile([P, PACK, P], F32, name=name, offset=index * BANK_BYTES)
 
-        def left_factor(chunk, n):
-            bank = psum.tile([P, PACK, P], F32, name="left_bank", tag="held", bufs=HELD_BANKS)
-            if chunk < TURNED_CHUNKS:
-                records_stationary(bank, chunk, (LEFT_FIELD[n],), w1_codes[:].bitcast(FP8X4), w1_plane[:])
-                left[chunk, n] = bank[:]
-            else:
-                weights_stationary(bank, w1_slice, [picked(LEFT_FIELD[n], chunk)])
-                left[chunk, n] = bank[:].rearrange("p t v -> p v t")
+        right_bank = {}
 
-        def multiply(chunk, n):
-            term = ring.tile([P, H], F32, name=f"term{n}")
-            nc.vector.tensor_tensor(
-                out=in_chunk_layout(term[:], chunk), in0=left[chunk, n], in1=right[chunk, n], op=MULT
-            )
+        def right_factor(chunk, n, index):
+            bank = bank_at(f"right_bank{chunk}{n}", index)
+            weights_stationary(bank, w2_slice, [picked(field, chunk) for field in RIGHT_FIELDS[n]])
+            right_bank[chunk, n] = bank
+
+        def copy_right(chunk, n, place):
+            right[chunk, n] = interleaved(place)
+            nc.scalar.copy(out=right[chunk, n], in_=right_bank[chunk, n][:].rearrange("p t v -> p v t"))
+
+        def left_factor(chunk, n, index):
+            bank = bank_at(f"left_bank{chunk}{n}", index)
+            weights_stationary(bank, w1_slice, [picked(LEFT_FIELD[n], chunk)])
+            left[chunk, n] = bank[:].rearrange("p t v -> p v t")
+
+        def multiply(chunk, n, term):
+            nc.vector.tensor_tensor(out=interleaved(term[:]), in0=left[chunk, n], in1=right[chunk, n], op=MULT)
             terms[chunk, n] = term
 
-        def turn_and_add(chunk):
-            bank = psum.tile([P, PACK, P], F32, name="z_bank", tag="scalar_read", bufs=SCALAR_READ_BANKS)
-            for n in range(2):
-                for t in range(PACK):
-                    nc.tensor.matmul(
-                        out=bank[:, t, :],
-                        lhsT=terms[chunk, n][:, t * P : (t + 1) * P],
-                        rhs=identity[:],
-                        is_transpose=True,
-                        start=(n == 0 and t == 0),
-                        stop=(n == 1 and t == PACK - 1),
-                    )
-            z = ring.tile([P, H], BF16, name="z_rounded", align_bytes=64)
-            nc.scalar.copy(out=z[:].rearrange("p (v t) -> p v t", t=PACK), in_=bank[:].rearrange("p t v -> p v t"))
-            z_rounded[chunk] = z
+        def new_term(n):
+            return ring.tile([P, H], F32, name=f"term{n}")
 
-        def add(chunk):
-            z = ring.tile([P, H], BF16, name="z_rounded", align_bytes=64)
-            nc.vector.tensor_tensor(out=z[:], in0=terms[chunk, 0][:], in1=terms[chunk, 1][:], op=ADD)
-            z_rounded[chunk] = z
+        def placed_term(chunk, n, slot):
+            return reused.tile([P, H], F32, name=f"term_{chunk}{n}", align_bytes=64, offset=TERM_AT[slot])
 
-        def quantize_z(chunk):
-            codes = ring.tile([P, P], U32, name="z_codes", align_bytes=64)
-            plane = ring.tile([P, P], U8, name="z_plane", align_bytes=64)
-            nc.vector.quantize_mx(out=codes[:].bitcast(FP8X4), scales=plane[:], in_=z_rounded[chunk][:])
-            z_quantised[chunk] = (codes[:].bitcast(FP8X4), plane[:])
+        def add(chunk, engine, z):
+            engine.tensor_tensor(out=z, in0=terms[chunk, 0][:], in1=terms[chunk, 1][:], op=ADD)
+
+        def quantize_z(first, end, z):
+            codes = keep.tile([P, (end - first) * P], U32, name=f"z_codes{first}", align_bytes=64)
+            plane = keep.tile([P, (end - first) * P], U8, name=f"z_plane{first}", align_bytes=64)
+            nc.vector.quantize_mx(out=codes[:].bitcast(FP8X4), scales=plane[:], in_=z)
+            for n in range(end - first):
+                z_quantised[first + n] = (codes[:, n * P : (n + 1) * P].bitcast(FP8X4), plane[:, n * P : (n + 1) * P])
 
         y_rows = out_0.rearrange("(p t) v -> p t v", t=PACK)
-        y_codes = keep.tile([P, V], I32, name="y_codes", align_bytes=64)
         y_plane = keep.tile([P, V], U8, name="y_plane", align_bytes=64)
         y_rounded = keep.tile([P, V * PACK], BF16, name="y_rounded", align_bytes=64)
         y_words = out_1[0].rearrange("p v r -> p (v r)").bitcast(I32)
 
-        def last_layer(chunk):
-            bank = psum.tile([P, PACK, P], F32, name="y_bank", tag="held", bufs=HELD_BANKS)
+        def last_layer(chunk, index):
+            bank = bank_at(f"y_bank{chunk}{index}", index)
             weights_stationary(bank, w3_slice, [z_quantised[chunk]])
             y_bank[chunk] = bank
 
@@ -259,25 +227,10 @@ def tile_picked_zfibi_none_po_kernel(
             nc.sync.dma_start(out=y_rows[:, :, chunk * P : (chunk + 1) * P], in_=y[:])
             y_values[chunk] = y
 
-        def last_layer_in_two_banks(chunk):
-            words, scales = z_quantised[chunk]
-            y = ring.tile([P, PACK, P], F32, name="y")
-            for u, copy in enumerate((nc.vector.tensor_copy, nc.scalar.copy)):
-                bank = psum.tile([P, PACK, P], F32, name="y_bank", tag="held", bufs=HELD_BANKS)
-                for t in (2 * u, 2 * u + 1):
-                    codes, plane = w3_slice(t)
-                    nc.tensor.matmul_mx(
-                        out=bank[:, t, :], lhsT=codes, lhsT_scale=plane, rhs=words, rhs_scale=scales,
-                        start=True, stop=True,
-                    )
-                copy(out=y[:, 2 * u : 2 * u + 2, :], in_=bank[:, 2 * u : 2 * u + 2, :])
-            nc.sync.dma_start(out=y_rows[:, :, chunk * P : (chunk + 1) * P], in_=y[:])
-            y_values[chunk] = y
-
-        def round_y(chunk, copy, source):
+        def round_y(chunk, copy, source, t0=0, t1=PACK):
             copy(
-                out=y_rounded[:, chunk * H : (chunk + 1) * H].rearrange("p (v t) -> p v t", t=PACK),
-                in_=source[chunk][:].rearrange("p t v -> p v t"),
+                out=interleaved(y_rounded[:, chunk * H : (chunk + 1) * H])[:, :, t0:t1],
+                in_=source[:].rearrange("p t v -> p v t")[:, :, t0:t1],
             )
 
         def quantize_y(first, end):
@@ -290,66 +243,92 @@ def tile_picked_zfibi_none_po_kernel(
         def store_codes(first, end):
             nc.sync.dma_start(out=y_words[:, first * P : end * P], in_=y_codes[:, first * P : end * P])
 
-        place_words(EARLY_GATHERS, "early_words", EARLY_WORDS_AT)
-        for field in (2, 1, 0):
-            gather_words(field, 0)
+        early_words = keep.tile([P, 4 * GATHER], U32, name="early_words", align_bytes=64)
+        for n, (field, half) in enumerate(((2, 0), (1, 0), (2, 1), (1, 1))):
+            gather_words(field, half, early_words[:, n * GATHER : (n + 1) * GATHER])
         round_w1(0)
         round_w1(1)
-        right_all = reused.tile([P, 2 * CHUNKS * H], F32, name="right_all", align_bytes=64, offset=RIGHT_FACTORS_AT)
-        right_factor(0, 0, right_all)
-        right_factor(0, 1, right_all)
-        gather_words(2, 1)
+        scales_0 = reused.tile([P, V], U8, name="scales_0", align_bytes=64, offset=W1_LOW_AT)
+        gather_scales(0, 1, scales_0)
         quantize_w1()
-        place_words(LATE_GATHERS, "late_words", LATE_WORDS_AT)
-        left_factor(0, 0)
-        left_factor(0, 1)
-        right_factor(1, 0, right_all)
-        right_factor(1, 1, right_all)
-        left_factor(1, 0)
-        left_factor(1, 1)
-        gather_words(1, 1)
-        gather_words(0, 1)
+        words_0a = reused.tile([P, GATHER], U32, name="words_0a", align_bytes=64, offset=WORDS_0A_AT)
+        gather_words(0, 0, words_0a[:])
+        right_all = reused.tile([P, 7 * H], F32, name="right_all", align_bytes=64, offset=RIGHT_ALL_AT)
+        right_10 = reused.tile([P, H], F32, name="right_10", align_bytes=64, offset=RIGHT_10_AT)
 
-        right_factor(2, 0, right_all)
-        right_factor(2, 1, right_all)
-        multiply(0, 0)
-        left_factor(2, 0)
-        multiply(0, 1)
-        turn_and_add(0)
-        right_factor(3, 0, right_all)
-        right_factor(3, 1, right_all)
-        left_factor(2, 1)
-        multiply(1, 0)
-        multiply(1, 1)
-        turn_and_add(1)
-        left_factor(3, 0)
-        left_factor(3, 1)
+        def place(slot):
+            return right_all[:, slot * H : (slot + 1) * H]
 
-        multiply(2, 0)
-        quantize_z(0)
-        multiply(2, 1)
-        last_layer(0)
+        right_factor(0, 0, 0)
+        right_factor(1, 0, 1)
+        right_factor(0, 1, 2)
+        right_factor(1, 1, 3)
+        right_factor(2, 0, 4)
+        right_factor(2, 1, 5)
+        copy_right(0, 0, place(0))
+        copy_right(0, 1, place(1))
+        copy_right(1, 0, right_10[:])
+        copy_right(1, 1, place(2))
+        copy_right(2, 0, place(3))
+        copy_right(2, 1, place(4))
+        left_factor(0, 0, 6)
+        left_factor(0, 1, 7)
+        left_factor(1, 0, 0)
+        left_factor(1, 1, 2)
+        right_factor(3, 0, 1)
+        z_first = reused.tile([P, H], BF16, name="z_first", align_bytes=64, offset=Z_AT)
+        multiply(0, 0, placed_term(0, 0, 0))
+        multiply(0, 1, placed_term(0, 1, 1))
+        add(0, nc.gpsimd, z_first[:])
+        left_factor(2, 0, 6)
+        right_factor(3, 1, 3)
+        left_factor(3, 0, 7)
+        copy_right(3, 0, place(5))
+        copy_right(3, 1, place(6))
+        multiply(1, 0, placed_term(1, 0, 2))
+        multiply(1, 1, placed_term(1, 1, 3))
+        words_0b = reused.tile([P, GATHER], U32, name="words_0b", align_bytes=64, offset=RIGHT_10_AT)
+        gather_words(0, 1, words_0b[:])
+        quantize_z(0, 1, z_first[:])
+        z_second = reused.tile([P, H], BF16, name="z_second", align_bytes=64, offset=Z_AT)
+        add(1, nc.gpsimd, z_second[:])
+        left_factor(2, 1, 4)
+        last_layer(0, 0)
+        left_factor(3, 1, 5)
         store_y(0)
-        multiply(3, 0)
-        quantize_z(1)
-        last_layer(1)
+        round_y(0, nc.scalar.copy, y_bank[0])
+        multiply(2, 0, placed_term(2, 0, 4))
+        multiply(2, 1, placed_term(2, 1, 1))
+        multiply(3, 0, placed_term(3, 0, 5))
+        quantize_z(1, 2, z_second[:])
+        last_layer(1, 2)
         store_y(1)
-        add(2)
-        multiply(3, 1)
-        quantize_z(2)
-        last_layer(2)
-        add(3)
-
-        round_y(0, nc.scalar.copy, y_bank)
+        round_y(1, nc.scalar.copy, y_bank[1])
+        z_late = reused.tile([P, 2 * H], BF16, name="z_late", align_bytes=64, offset=TERM_AT[2])
+        add(2, nc.vector, z_late[:, :H])
+        multiply(3, 1, placed_term(3, 1, 3))
+        quantize_z(2, 3, z_late[:, :H])
+        add(3, nc.vector, z_late[:, H:])
+        quantize_z(3, 4, z_late[:, H:])
+        last_layer(2, 1)
         store_y(2)
-        quantize_z(3)
-        round_y(1, nc.scalar.copy, y_bank)
-        last_layer_in_two_banks(3)
+        last_layer(2, 4)
+        round_y(2, nc.scalar.copy, y_bank[2])
+        low = bank_at("y_low", 3)
+        high = bank_at("y_high", 6)
+        weights_stationary(low, w3_slice, [z_quantised[3]], range(0, 2))
+        weights_stationary(high, w3_slice, [z_quantised[3]], range(2, 4))
+        y_codes = reused.tile([P, V], I32, name="y_codes", align_bytes=64, offset=TERM_AT[5])
         quantize_y(0, 2)
         store_codes(0, 2)
-        for chunk in (2, 3):
-            round_y(chunk, nc.vector.tensor_copy, y_values)
-            quantize_y(chunk, chunk + 1)
+        y = ring.tile([P, PACK, P], F32, name="y")
+        round_y(3, nc.vector.tensor_copy, low, 0, 2)
+        nc.scalar.copy(out=y[:, 2:4, :], in_=high[:, 2:4, :])
+        quantize_y(2, 3)
+        round_y(3, nc.vector.tensor_copy, high, 2, 4)
+        nc.scalar.copy(out=y[:, 0:2, :], in_=low[:, 0:2, :])
+        nc.sync.dma_start(out=y_rows[:, :, 3 * P : 4 * P], in_=y[:])
+        quantize_y(3, 4)
         store_codes(2, 4)
         for q in range(QUADRANTS):
             (nc.sync, nc.scalar)[q % 2].dma_start(

@@ -33,14 +33,14 @@ W1_HIGH_AT = 24576
 RIGHT_ALL_AT = W1_HIGH_AT - 7 * 2048 + 64
 RIGHT_10_AT = W1_HIGH_AT + 64
 WORDS_0A_AT = RIGHT_10_AT + 2048
-TERM_AT = (36864, 40960, 43008, 45056, 36864 - 2048 + 64, 36864 + 64)
-Z_AT = 47104
+TERM_AT = (36864, 40960, 45056, 47104, 40960 - 2048 + 64, 36864, 51200, 40960 + 64)
+Z_AT = 49152
 
 
-def load_plane(nc, plane, rows):
+def load_plane(nc, plane, rows, queues=None):
     for q in range(QUADRANTS):
-        nc.sync.dma_start(
-            out=plane[32 * q : 32 * q + 4, :].bitcast(I32), in_=rows[0, 4 * q : 4 * q + 4, :].bitcast(I32)
+        (queues[q % 2] if queues else nc.sync).dma_start(
+            out=plane[q:P:32, :].bitcast(I32), in_=rows[0, q:16:4, :].bitcast(I32)
         )
 
 
@@ -87,7 +87,7 @@ def tile_picked_zfibi_none_po_kernel(
         nc.vector.memset(w3_plane[:].bitcast(I32), 0)
         nc.sync.dma_start(offsets[:], offs)
         nc.sync.dma_start(out=w2_codes[:].bitcast(I32), in_=w2_words[0].bitcast(I32))
-        load_plane(nc, x_scale_table, x_scales)
+        load_plane(nc, x_scale_table, x_scales, (nc.sync, nc.scalar))
         nc.sync.dma_start(out=x_word_table[:], in_=x_words[0].rearrange("p c r -> p (c r)").bitcast(I32))
         load_plane(nc, w2_plane, w2_scales)
         nc.sync.dma_start(out=w1_halves[0][:], in_=w1_rows[:, :, 0 : H // 2])
@@ -250,9 +250,11 @@ def tile_picked_zfibi_none_po_kernel(
         round_w1(1)
         scales_0 = reused.tile([P, V], U8, name="scales_0", align_bytes=64, offset=W1_LOW_AT)
         gather_scales(0, 1, scales_0)
-        quantize_w1()
-        words_0a = reused.tile([P, GATHER], U32, name="words_0a", align_bytes=64, offset=WORDS_0A_AT)
+        words_0a = reused.tile([P, GATHER], U32, name="words_0a", align_bytes=64, offset=W1_LOW_AT + 1024)
         gather_words(0, 0, words_0a[:])
+        quantize_w1()
+        words_0b = reused.tile([P, GATHER], U32, name="words_0b", align_bytes=64, offset=WORDS_0A_AT)
+        gather_words(0, 1, words_0b[:])
         right_all = reused.tile([P, 7 * H], F32, name="right_all", align_bytes=64, offset=RIGHT_ALL_AT)
         right_10 = reused.tile([P, H], F32, name="right_10", align_bytes=64, offset=RIGHT_10_AT)
 
@@ -287,8 +289,7 @@ def tile_picked_zfibi_none_po_kernel(
         copy_right(3, 1, place(6))
         multiply(1, 0, placed_term(1, 0, 2))
         multiply(1, 1, placed_term(1, 1, 3))
-        words_0b = reused.tile([P, GATHER], U32, name="words_0b", align_bytes=64, offset=RIGHT_10_AT)
-        gather_words(0, 1, words_0b[:])
+        multiply(2, 0, placed_term(2, 0, 6))
         quantize_z(0, 1, z_first[:])
         z_second = reused.tile([P, H], BF16, name="z_second", align_bytes=64, offset=Z_AT)
         add(1, nc.gpsimd, z_second[:])
@@ -297,23 +298,21 @@ def tile_picked_zfibi_none_po_kernel(
         left_factor(3, 1, 5)
         store_y(0)
         round_y(0, nc.scalar.copy, y_bank[0])
-        multiply(2, 0, placed_term(2, 0, 4))
-        multiply(2, 1, placed_term(2, 1, 1))
+        multiply(2, 1, placed_term(2, 1, 4))
         multiply(3, 0, placed_term(3, 0, 5))
+        multiply(3, 1, placed_term(3, 1, 7))
         quantize_z(1, 2, z_second[:])
         last_layer(1, 2)
         store_y(1)
+        last_layer(1, 4)
         round_y(1, nc.scalar.copy, y_bank[1])
         z_late = reused.tile([P, 2 * H], BF16, name="z_late", align_bytes=64, offset=TERM_AT[2])
         add(2, nc.vector, z_late[:, :H])
-        multiply(3, 1, placed_term(3, 1, 3))
-        quantize_z(2, 3, z_late[:, :H])
         add(3, nc.vector, z_late[:, H:])
+        quantize_z(2, 3, z_late[:, :H])
         quantize_z(3, 4, z_late[:, H:])
         last_layer(2, 1)
         store_y(2)
-        last_layer(2, 4)
-        round_y(2, nc.scalar.copy, y_bank[2])
         low = bank_at("y_low", 3)
         high = bank_at("y_high", 6)
         weights_stationary(low, w3_slice, [z_quantised[3]], range(0, 2))
@@ -321,13 +320,14 @@ def tile_picked_zfibi_none_po_kernel(
         y_codes = reused.tile([P, V], I32, name="y_codes", align_bytes=64, offset=TERM_AT[5])
         quantize_y(0, 2)
         store_codes(0, 2)
+        round_y(2, nc.vector.tensor_copy, y_values[2])
         y = ring.tile([P, PACK, P], F32, name="y")
-        round_y(3, nc.vector.tensor_copy, low, 0, 2)
+        nc.vector.tensor_copy(out=y[:, 0:2, :], in_=low[:, 0:2, :])
         nc.scalar.copy(out=y[:, 2:4, :], in_=high[:, 2:4, :])
-        quantize_y(2, 3)
-        round_y(3, nc.vector.tensor_copy, high, 2, 4)
-        nc.scalar.copy(out=y[:, 0:2, :], in_=low[:, 0:2, :])
         nc.sync.dma_start(out=y_rows[:, :, 3 * P : 4 * P], in_=y[:])
+        round_y(3, nc.vector.tensor_copy, low, 0, 2)
+        round_y(3, nc.scalar.copy, high, 2, 4)
+        quantize_y(2, 3)
         quantize_y(3, 4)
         store_codes(2, 4)
         for q in range(QUADRANTS):

@@ -87,7 +87,7 @@ def tile_picked_zfibi_none_po_kernel(
         nc.vector.memset(w3_plane[:].bitcast(I32), 0)
         nc.sync.dma_start(offsets[:], offs)
         nc.sync.dma_start(out=w2_codes[:].bitcast(I32), in_=w2_words[0].bitcast(I32))
-        load_plane(nc, x_scale_table, x_scales, (nc.sync, nc.scalar))
+        load_plane(nc, x_scale_table, x_scales)
         nc.sync.dma_start(out=x_word_table[:], in_=x_words[0].rearrange("p c r -> p (c r)").bitcast(I32))
         load_plane(nc, w2_plane, w2_scales)
         nc.sync.dma_start(out=w1_halves[0][:], in_=w1_rows[:, :, 0 : H // 2])

@@ -40,7 +40,7 @@ Z_AT = 49152
 def load_plane(nc, plane, rows, queues=None):
     for q in range(QUADRANTS):
         (queues[q % 2] if queues else nc.sync).dma_start(
-            out=plane[q:P:32, :].bitcast(I32), in_=rows[0, q:16:4, :].bitcast(I32)
+            out=plane[32 * q : 32 * q + 4, :].bitcast(I32), in_=rows[0, 4 * q : 4 * q + 4, :].bitcast(I32)
         )
 
 
@@ -266,15 +266,15 @@ def tile_picked_zfibi_none_po_kernel(
         right_factor(0, 1, 2)
         right_factor(1, 1, 3)
         right_factor(2, 0, 4)
-        right_factor(2, 1, 5)
         copy_right(0, 0, place(0))
         copy_right(0, 1, place(1))
         copy_right(1, 0, right_10[:])
         copy_right(1, 1, place(2))
         copy_right(2, 0, place(3))
-        copy_right(2, 1, place(4))
         left_factor(0, 0, 6)
         left_factor(0, 1, 7)
+        right_factor(2, 1, 5)
+        copy_right(2, 1, place(4))
         left_factor(1, 0, 0)
         left_factor(1, 1, 2)
         right_factor(3, 0, 1)
@@ -320,13 +320,12 @@ def tile_picked_zfibi_none_po_kernel(
         y_codes = reused.tile([P, V], I32, name="y_codes", align_bytes=64, offset=TERM_AT[5])
         quantize_y(0, 2)
         store_codes(0, 2)
-        round_y(2, nc.vector.tensor_copy, y_values[2])
         y = ring.tile([P, PACK, P], F32, name="y")
         nc.vector.tensor_copy(out=y[:, 0:2, :], in_=low[:, 0:2, :])
         nc.scalar.copy(out=y[:, 2:4, :], in_=high[:, 2:4, :])
         nc.sync.dma_start(out=y_rows[:, :, 3 * P : 4 * P], in_=y[:])
-        round_y(3, nc.vector.tensor_copy, low, 0, 2)
-        round_y(3, nc.scalar.copy, high, 2, 4)
+        round_y(2, nc.vector.tensor_copy, y_values[2])
+        round_y(3, nc.vector.tensor_copy, y)
         quantize_y(2, 3)
         quantize_y(3, 4)
         store_codes(2, 4)

@@ -30,16 +30,18 @@ RIGHT_FIELDS = ((2,), (2, 1))
 SCALE_TABLE_AT = EARLY_WORDS_AT = 0
 W1_LOW_AT = 4096
 W1_HIGH_AT = 24576
-RIGHT_ALL_AT = W1_HIGH_AT - 7 * 2048 + 64
-RIGHT_10_AT = W1_HIGH_AT + 64
-WORDS_0A_AT = RIGHT_10_AT + 2048
+RIGHT_ALL_AT = W1_HIGH_AT - 8 * 2048 + 64
+WORDS_0A_AT = W1_HIGH_AT + 64
 TERM_AT = (36864, 40960, 45056, 47104, 40960 - 2048 + 64, 36864, 51200, 40960 + 64)
 Z_AT = 49152
+WORDS_AT = 53248
+W1_ROUNDED_AT = 59392
+W1_PARTS = ((0, 32, 2048), (32, 80, 4096), (80, 128, W1_HIGH_AT))
 
 
-def load_plane(nc, plane, rows, queues=None):
-    for q in range(QUADRANTS):
-        (queues[q % 2] if queues else nc.sync).dma_start(
+def load_plane(nc, plane, rows, quadrants=range(QUADRANTS)):
+    for q in quadrants:
+        nc.sync.dma_start(
             out=plane[32 * q : 32 * q + 4, :].bitcast(I32), in_=rows[0, 4 * q : 4 * q + 4, :].bitcast(I32)
         )
 
@@ -75,9 +77,9 @@ def tile_picked_zfibi_none_po_kernel(
         w2_plane = keep.tile([P, H], U8, name="w2_plane", align_bytes=64)
         w3_codes = keep.tile([P, 2 * N], U8, name="w3_codes", align_bytes=64)
         w3_plane = keep.tile([P, N], U8, name="w3_plane", align_bytes=64)
-        w1_halves = [
-            reused.tile([P, PACK, H // 2], F32, name=f"w1_half{u}", align_bytes=64, offset=(W1_LOW_AT, W1_HIGH_AT)[u])
-            for u in range(2)
+        w1_parts = [
+            reused.tile([P, PACK, PACK * (end - first)], F32, name=f"w1_part{first}", align_bytes=64, offset=at)
+            for first, end, at in W1_PARTS
         ]
         w1_rows = w1.rearrange("(p j) c -> p j c", j=PACK)
 
@@ -85,20 +87,25 @@ def tile_picked_zfibi_none_po_kernel(
         nc.gpsimd.memset(x_scale_table[:, T // 2 :].bitcast(I32), 0)
         nc.vector.memset(w2_plane[:].bitcast(I32), 0)
         nc.vector.memset(w3_plane[:].bitcast(I32), 0)
+        def load_w1(u):
+            first, end, at = W1_PARTS[u]
+            nc.sync.dma_start(out=w1_parts[u][:], in_=w1_rows[:, :, PACK * first : PACK * end])
+
         nc.sync.dma_start(offsets[:], offs)
         nc.sync.dma_start(out=w2_codes[:].bitcast(I32), in_=w2_words[0].bitcast(I32))
-        load_plane(nc, x_scale_table, x_scales)
-        nc.sync.dma_start(out=x_word_table[:], in_=x_words[0].rearrange("p c r -> p (c r)").bitcast(I32))
-        load_plane(nc, w2_plane, w2_scales)
-        nc.sync.dma_start(out=w1_halves[0][:], in_=w1_rows[:, :, 0 : H // 2])
-        nc.sync.dma_start(out=w1_halves[1][:], in_=w1_rows[:, :, H // 2 : H])
         nc.sync.dma_start(out=w3_codes[:].bitcast(I32), in_=w3_words[0].bitcast(I32))
+        load_plane(nc, x_scale_table, x_scales)
+        load_plane(nc, w2_plane, w2_scales, range(0, 1))
+        load_w1(0)
+        nc.sync.dma_start(out=x_word_table[:], in_=x_words[0].rearrange("p c r -> p (c r)").bitcast(I32))
+        load_plane(nc, w2_plane, w2_scales, range(1, 4))
+        load_w1(1)
+        load_w1(2)
         load_plane(nc, w3_plane, w3_scales)
 
         w2_dealt = keep.tile([P, 2 * H], U8, name="w2_dealt", align_bytes=64)
         w2_dealt_plane = keep.tile([P, H], U8, name="w2_dealt_plane", align_bytes=64)
         w3_dealt = keep.tile([P, 2 * N], U8, name="w3_dealt", align_bytes=64)
-        w3_dealt_plane = keep.tile([P, N], U8, name="w3_dealt_plane", align_bytes=64)
         picked_scales = {}
 
         def gather_scales(first, end, tile):
@@ -107,12 +114,11 @@ def tile_picked_zfibi_none_po_kernel(
             for field in range(first, end):
                 picked_scales[field] = tile[:, (field - first) * V : (field - first + 1) * V]
 
-        scales_12 = keep.tile([P, 2 * V], U8, name="scales_12", align_bytes=64)
-        gather_scales(1, 3, scales_12)
+        scales_all = keep.tile([P, 3 * V], U8, name="scales_all", align_bytes=64)
+        gather_scales(0, 3, scales_all)
         deal_codes(nc.gpsimd, w2_dealt, w2_codes)
         deal_plane(nc.gpsimd, w2_dealt_plane, w2_plane)
         deal_codes(nc.gpsimd, w3_dealt, w3_codes)
-        deal_plane(nc.gpsimd, w3_dealt_plane, w3_plane)
 
         picked_words = {}
 
@@ -127,14 +133,14 @@ def tile_picked_zfibi_none_po_kernel(
             scales = picked_scales[field][:, chunk * P : (chunk + 1) * P]
             return picked_words[field, half][:, inner : inner + P].bitcast(FP8X4), scales
 
-        w1_rounded = keep.tile([P, PACK, P, PACK], BF16, name="w1_rounded", align_bytes=64)
+        w1_rounded = reused.tile([P, PACK, P, PACK], BF16, name="w1_rounded", align_bytes=64, offset=W1_ROUNDED_AT)
         w1_codes = keep.tile([P, H], U32, name="w1_codes", align_bytes=64)
         w1_plane = keep.tile([P, H], U8, name="w1_plane", align_bytes=64)
 
         def round_w1(u):
             nc.scalar.copy(
-                out=w1_rounded[:, :, u * (P // 2) : (u + 1) * (P // 2), :].rearrange("p t m j -> p m j t"),
-                in_=w1_halves[u][:].rearrange("p j (m t) -> p m j t", t=PACK),
+                out=w1_rounded[:, :, W1_PARTS[u][0] : W1_PARTS[u][1], :].rearrange("p t m j -> p m j t"),
+                in_=w1_parts[u][:].rearrange("p j (m t) -> p m j t", t=PACK),
             )
 
         def quantize_w1():
@@ -243,20 +249,18 @@ def tile_picked_zfibi_none_po_kernel(
         def store_codes(first, end):
             nc.sync.dma_start(out=y_words[:, first * P : end * P], in_=y_codes[:, first * P : end * P])
 
-        early_words = keep.tile([P, 4 * GATHER], U32, name="early_words", align_bytes=64)
-        for n, (field, half) in enumerate(((2, 0), (1, 0), (2, 1), (1, 1))):
-            gather_words(field, half, early_words[:, n * GATHER : (n + 1) * GATHER])
+        all_words = reused.tile([P, 5 * GATHER], U32, name="all_words", align_bytes=64, offset=WORDS_AT)
+        for n, (field, half) in enumerate(((2, 0), (1, 0), (2, 1), (1, 1), (0, 0))):
+            gather_words(field, half, all_words[:, n * GATHER : (n + 1) * GATHER])
         round_w1(0)
         round_w1(1)
-        scales_0 = reused.tile([P, V], U8, name="scales_0", align_bytes=64, offset=W1_LOW_AT)
-        gather_scales(0, 1, scales_0)
-        words_0a = reused.tile([P, GATHER], U32, name="words_0a", align_bytes=64, offset=W1_LOW_AT + 1024)
-        gather_words(0, 0, words_0a[:])
+        round_w1(2)
         quantize_w1()
-        words_0b = reused.tile([P, GATHER], U32, name="words_0b", align_bytes=64, offset=WORDS_0A_AT)
-        gather_words(0, 1, words_0b[:])
-        right_all = reused.tile([P, 7 * H], F32, name="right_all", align_bytes=64, offset=RIGHT_ALL_AT)
-        right_10 = reused.tile([P, H], F32, name="right_10", align_bytes=64, offset=RIGHT_10_AT)
+        w3_dealt_plane = reused.tile([P, N], U8, name="w3_dealt_plane", align_bytes=64, offset=W1_ROUNDED_AT)
+        deal_plane(nc.gpsimd, w3_dealt_plane, w3_plane)
+        late_words = reused.tile([P, GATHER], U32, name="late_words", align_bytes=64, offset=WORDS_0A_AT)
+        gather_words(0, 1, late_words[:])
+        right_all = reused.tile([P, 8 * H], F32, name="right_all", align_bytes=64, offset=RIGHT_ALL_AT)
 
         def place(slot):
             return right_all[:, slot * H : (slot + 1) * H]
@@ -265,26 +269,26 @@ def tile_picked_zfibi_none_po_kernel(
         right_factor(1, 0, 1)
         right_factor(0, 1, 2)
         right_factor(1, 1, 3)
-        right_factor(2, 0, 4)
         copy_right(0, 0, place(0))
         copy_right(0, 1, place(1))
-        copy_right(1, 0, right_10[:])
+        copy_right(1, 0, place(7))
         copy_right(1, 1, place(2))
-        copy_right(2, 0, place(3))
         left_factor(0, 0, 6)
         left_factor(0, 1, 7)
-        right_factor(2, 1, 5)
+        left_factor(1, 0, 4)
+        left_factor(1, 1, 5)
+        right_factor(2, 0, 0)
+        right_factor(2, 1, 2)
+        copy_right(2, 0, place(3))
         copy_right(2, 1, place(4))
-        left_factor(1, 0, 0)
-        left_factor(1, 1, 2)
-        right_factor(3, 0, 1)
         z_first = reused.tile([P, H], BF16, name="z_first", align_bytes=64, offset=Z_AT)
         multiply(0, 0, placed_term(0, 0, 0))
         multiply(0, 1, placed_term(0, 1, 1))
         add(0, nc.gpsimd, z_first[:])
         left_factor(2, 0, 6)
+        right_factor(3, 0, 1)
+        left_factor(2, 1, 7)
         right_factor(3, 1, 3)
-        left_factor(3, 0, 7)
         copy_right(3, 0, place(5))
         copy_right(3, 1, place(6))
         multiply(1, 0, placed_term(1, 0, 2))
@@ -293,9 +297,9 @@ def tile_picked_zfibi_none_po_kernel(
         quantize_z(0, 1, z_first[:])
         z_second = reused.tile([P, H], BF16, name="z_second", align_bytes=64, offset=Z_AT)
         add(1, nc.gpsimd, z_second[:])
-        left_factor(2, 1, 4)
-        last_layer(0, 0)
+        left_factor(3, 0, 4)
         left_factor(3, 1, 5)
+        last_layer(0, 0)
         store_y(0)
         round_y(0, nc.scalar.copy, y_bank[0])
         multiply(2, 1, placed_term(2, 1, 4))
@@ -304,7 +308,7 @@ def tile_picked_zfibi_none_po_kernel(
         quantize_z(1, 2, z_second[:])
         last_layer(1, 2)
         store_y(1)
-        last_layer(1, 4)
+        last_layer(1, 6)
         round_y(1, nc.scalar.copy, y_bank[1])
         z_late = reused.tile([P, 2 * H], BF16, name="z_late", align_bytes=64, offset=TERM_AT[2])
         add(2, nc.vector, z_late[:, :H])
@@ -314,7 +318,7 @@ def tile_picked_zfibi_none_po_kernel(
         last_layer(2, 1)
         store_y(2)
         low = bank_at("y_low", 3)
-        high = bank_at("y_high", 6)
+        high = bank_at("y_high", 7)
         weights_stationary(low, w3_slice, [z_quantised[3]], range(0, 2))
         weights_stationary(high, w3_slice, [z_quantised[3]], range(2, 4))
         y_codes = reused.tile([P, V], I32, name="y_codes", align_bytes=64, offset=TERM_AT[5])

@@ -20,44 +20,63 @@ P = 128
 PACK = 4
 QUADRANTS = 4
 LIST_ROWS = 16
-GATHER = 256
+HALF = V // 2
 CHUNKS = V // P
 BANK_BYTES = 2048
+ALIGN = 64
 
 LEFT_FIELD = (1, 0)
 RIGHT_FIELDS = ((2,), (2, 1))
 
-SCALE_TABLE_AT = EARLY_WORDS_AT = 0
-W1_LOW_AT = 4096
-W1_HIGH_AT = 24576
-RIGHT_ALL_AT = W1_HIGH_AT - 8 * 2048 + 64
-WORDS_0A_AT = W1_HIGH_AT + 64
-TERM_AT = (36864, 40960, 45056, 47104, 40960 - 2048 + 64, 36864, 51200, 40960 + 64)
-Z_AT = 49152
-WORDS_AT = 53248
-W1_ROUNDED_AT = 59392
-W1_PARTS = ((0, 32, 2048), (32, 80, 4096), (80, 128, W1_HIGH_AT))
+W1_CUTS = (0, 32, 80, 128)
+
+TERM_BYTES = 4 * H
+W1_FIRST_AT = 0
+RIGHT_AT = 2048
+W1_LAST_AT = RIGHT_AT + 2 * CHUNKS * TERM_BYTES - ALIGN
+LAST_WORDS_AT = W1_LAST_AT + ALIGN
+W1_ROUNDED_AT = W1_LAST_AT + 4096 + ALIGN
+TERM_00_AT = W1_ROUNDED_AT + 4096
+TERM_01_AT = TERM_00_AT + 2 * TERM_BYTES
+TERM_10_AT = TERM_01_AT + 2 * TERM_BYTES
+Z_EARLY_AT = TERM_10_AT + TERM_BYTES
+PLACED_TERMS = {
+    (0, 0): TERM_00_AT,
+    (0, 1): TERM_01_AT,
+    (1, 0): TERM_10_AT,
+    (2, 1): TERM_01_AT - TERM_BYTES + ALIGN,
+    (3, 0): TERM_00_AT,
+    (3, 1): TERM_01_AT + ALIGN,
+}
 
 
-def load_plane(nc, plane, rows, quadrants=range(QUADRANTS)):
+def load_plane(nc, plane, rows, quadrants):
     for q in quadrants:
         nc.sync.dma_start(
             out=plane[32 * q : 32 * q + 4, :].bitcast(I32), in_=rows[0, 4 * q : 4 * q + 4, :].bitcast(I32)
         )
 
 
-def deal_codes(engine, dealt, codes):
-    engine.tensor_copy(
+def deal_codes(nc, dealt, codes):
+    nc.gpsimd.tensor_copy(
         out=dealt[:].rearrange("k (t p b) -> k t p b", t=PACK, b=2),
         in_=codes[:].rearrange("k (p t b) -> k t p b", t=PACK, b=2),
     )
 
 
-def deal_plane(engine, dealt, plane):
-    engine.tensor_copy(
+def deal_plane(nc, dealt, plane):
+    nc.gpsimd.tensor_copy(
         out=dealt[:].rearrange("k (t p) -> k t p", t=PACK),
         in_=plane[:].rearrange("k (p t) -> k t p", t=PACK),
     )
+
+
+def as_words(flat):
+    return flat.rearrange("p (v t) -> p v t", t=PACK)
+
+
+def slices_as_words(slices):
+    return slices.rearrange("p t v -> p v t")
 
 
 def tile_picked_zfibi_none_po_kernel(
@@ -66,91 +85,90 @@ def tile_picked_zfibi_none_po_kernel(
     nc = tc.nc
     with ExitStack() as ctx:
         keep = ctx.enter_context(tc.tile_pool(name="keep", bufs=1))
-        ring = ctx.enter_context(tc.tile_pool(name="ring", bufs=CHUNKS))
         reused = ctx.enter_context(tc.tile_pool(name="reused", bufs=1))
         psum = ctx.enter_context(tc.psum_pool(name="psum", bufs=1))
 
+        def kept(name, shape, dtype):
+            return keep.tile(shape, dtype, name=name, align_bytes=ALIGN)
+
+        def placed(name, shape, dtype, offset):
+            return reused.tile(shape, dtype, name=name, align_bytes=ALIGN, offset=offset)
+
+        def bank_at(name, index):
+            return psum.tile([P, PACK, P], F32, name=name, offset=index * BANK_BYTES)
+
         offsets = keep.tile([P, S // LIST_ROWS], U16, name="offsets")
-        x_scale_table = reused.tile([P, T], U8, name="x_scale_table", align_bytes=64, offset=SCALE_TABLE_AT)
-        x_word_table = keep.tile([P, T], I32, name="x_word_table", align_bytes=64)
-        w2_codes = keep.tile([P, 2 * H], U8, name="w2_codes", align_bytes=64)
-        w2_plane = keep.tile([P, H], U8, name="w2_plane", align_bytes=64)
-        w3_codes = keep.tile([P, 2 * N], U8, name="w3_codes", align_bytes=64)
-        w3_plane = keep.tile([P, N], U8, name="w3_plane", align_bytes=64)
-        w1_parts = [
-            reused.tile([P, PACK, PACK * (end - first)], F32, name=f"w1_part{first}", align_bytes=64, offset=at)
-            for first, end, at in W1_PARTS
+        x_scale_table = kept("x_scale_table", [P, T], U8)
+        x_word_table = kept("x_word_table", [P, T], I32)
+        w2_codes = kept("w2_codes", [P, 2 * H], U8)
+        w2_plane = kept("w2_plane", [P, H], U8)
+        w3_codes = kept("w3_codes", [P, 2 * N], U8)
+        w3_plane = kept("w3_plane", [P, N], U8)
+        w1_widths = [PACK * (W1_CUTS[u + 1] - W1_CUTS[u]) for u in range(3)]
+        w1_pieces = [
+            placed("w1_first", [P, PACK, w1_widths[0]], F32, W1_FIRST_AT),
+            kept("w1_middle", [P, PACK, w1_widths[1]], F32),
+            placed("w1_last", [P, PACK, w1_widths[2]], F32, W1_LAST_AT),
         ]
         w1_rows = w1.rearrange("(p j) c -> p j c", j=PACK)
 
-        nc.vector.memset(x_scale_table[:, : T // 2].bitcast(I32), 0)
-        nc.gpsimd.memset(x_scale_table[:, T // 2 :].bitcast(I32), 0)
+        nc.vector.memset(x_scale_table[:].bitcast(I32), 0)
         nc.vector.memset(w2_plane[:].bitcast(I32), 0)
         nc.vector.memset(w3_plane[:].bitcast(I32), 0)
-        def load_w1(u):
-            first, end, at = W1_PARTS[u]
-            nc.sync.dma_start(out=w1_parts[u][:], in_=w1_rows[:, :, PACK * first : PACK * end])
-
         nc.sync.dma_start(offsets[:], offs)
         nc.sync.dma_start(out=w2_codes[:].bitcast(I32), in_=w2_words[0].bitcast(I32))
         nc.sync.dma_start(out=w3_codes[:].bitcast(I32), in_=w3_words[0].bitcast(I32))
-        load_plane(nc, x_scale_table, x_scales)
+        load_plane(nc, x_scale_table, x_scales, range(QUADRANTS))
         load_plane(nc, w2_plane, w2_scales, range(0, 1))
-        load_w1(0)
         nc.sync.dma_start(out=x_word_table[:], in_=x_words[0].rearrange("p c r -> p (c r)").bitcast(I32))
-        load_plane(nc, w2_plane, w2_scales, range(1, 4))
-        load_w1(1)
-        load_w1(2)
-        load_plane(nc, w3_plane, w3_scales)
+        load_plane(nc, w2_plane, w2_scales, range(1, QUADRANTS))
+        for u in range(3):
+            nc.sync.dma_start(out=w1_pieces[u][:], in_=w1_rows[:, :, PACK * W1_CUTS[u] : PACK * W1_CUTS[u + 1]])
+        load_plane(nc, w3_plane, w3_scales, range(QUADRANTS))
 
-        w2_dealt = keep.tile([P, 2 * H], U8, name="w2_dealt", align_bytes=64)
-        w2_dealt_plane = keep.tile([P, H], U8, name="w2_dealt_plane", align_bytes=64)
-        w3_dealt = keep.tile([P, 2 * N], U8, name="w3_dealt", align_bytes=64)
-        picked_scales = {}
+        picked_scales, picked_words = {}, {}
 
-        def gather_scales(first, end, tile):
-            entries = offsets[:, first * V // LIST_ROWS : end * V // LIST_ROWS]
-            nc.vector.tensor_copy(tile[:], x_scale_table[:].indirect(entries))
-            for field in range(first, end):
-                picked_scales[field] = tile[:, (field - first) * V : (field - first + 1) * V]
+        def gather(picked, table, field, half, halves, tile):
+            first = field * V + half * HALF
+            entries = offsets[:, first // LIST_ROWS : (first + halves * HALF) // LIST_ROWS]
+            nc.vector.tensor_copy(tile, table.indirect(entries))
+            for n in range(halves):
+                picked[divmod(2 * field + half + n, 2)] = tile[:, n * HALF : (n + 1) * HALF]
 
-        scales_all = keep.tile([P, 3 * V], U8, name="scales_all", align_bytes=64)
-        gather_scales(0, 3, scales_all)
-        deal_codes(nc.gpsimd, w2_dealt, w2_codes)
-        deal_plane(nc.gpsimd, w2_dealt_plane, w2_plane)
-        deal_codes(nc.gpsimd, w3_dealt, w3_codes)
+        def gather_scales(field, half, halves, tile):
+            gather(picked_scales, x_scale_table[:], field, half, halves, tile)
 
-        picked_words = {}
+        def gather_words(field, half, halves, tile):
+            gather(picked_words, x_word_table[:].bitcast(U32), field, half, halves, tile)
 
-        def gather_words(field, half, words):
-            first = field * V + half * GATHER
-            entries = offsets[:, first // LIST_ROWS : (first + GATHER) // LIST_ROWS]
-            nc.vector.tensor_copy(words, x_word_table[:].bitcast(U32).indirect(entries))
-            picked_words[field, half] = words
+        def picked_operand(field, chunk):
+            half, first = divmod(chunk * P, HALF)
+            words = picked_words[field, half][:, first : first + P]
+            return words.bitcast(FP8X4), picked_scales[field, half][:, first : first + P]
 
-        def picked(field, chunk):
-            half, inner = divmod(chunk * P, GATHER)
-            scales = picked_scales[field][:, chunk * P : (chunk + 1) * P]
-            return picked_words[field, half][:, inner : inner + P].bitcast(FP8X4), scales
-
-        w1_rounded = reused.tile([P, PACK, P, PACK], BF16, name="w1_rounded", align_bytes=64, offset=W1_ROUNDED_AT)
-        w1_codes = keep.tile([P, H], U32, name="w1_codes", align_bytes=64)
-        w1_plane = keep.tile([P, H], U8, name="w1_plane", align_bytes=64)
+        w2_dealt = kept("w2_dealt", [P, 2 * H], U8)
+        w2_dealt_plane = kept("w2_dealt_plane", [P, H], U8)
+        w3_dealt = kept("w3_dealt", [P, 2 * N], U8)
+        w1_rounded = placed("w1_rounded", [P, PACK, P, PACK], BF16, W1_ROUNDED_AT)
+        w1_codes = kept("w1_codes", [P, H], U32)
+        w1_plane = kept("w1_plane", [P, H], U8)
 
         def round_w1(u):
             nc.scalar.copy(
-                out=w1_rounded[:, :, W1_PARTS[u][0] : W1_PARTS[u][1], :].rearrange("p t m j -> p m j t"),
-                in_=w1_parts[u][:].rearrange("p j (m t) -> p m j t", t=PACK),
+                out=w1_rounded[:, :, W1_CUTS[u] : W1_CUTS[u + 1], :].rearrange("p t m j -> p m j t"),
+                in_=w1_pieces[u][:].rearrange("p j (m t) -> p m j t", t=PACK),
             )
 
-        def quantize_w1():
-            nc.vector.quantize_mx(
-                out=w1_codes[:].bitcast(FP8X4),
-                scales=w1_plane[:],
-                in_=w1_rounded[:].rearrange("p t m j -> p (t m j)"),
-            )
+        def w1_slice(t):
+            return w1_codes[:, t * P : (t + 1) * P].bitcast(FP8X4), w1_plane[:, t * P : (t + 1) * P]
 
-        def weights_stationary(bank, dealt_slice, moving, slices=range(PACK)):
+        def w2_slice(t):
+            return w2_dealt[:, 2 * t * P : 2 * (t + 1) * P].bitcast(FP4X4), w2_dealt_plane[:, t * P : (t + 1) * P]
+
+        def w3_slice(t):
+            return w3_dealt[:, 2 * t * P : 2 * (t + 1) * P].bitcast(FP4X4), w3_dealt_plane[:, t * P : (t + 1) * P]
+
+        def project(bank, dealt_slice, moving, slices):
             for t in slices:
                 codes, plane = dealt_slice(t)
                 for n, (words, scales) in enumerate(moving):
@@ -164,80 +182,58 @@ def tile_picked_zfibi_none_po_kernel(
                         stop=(n == len(moving) - 1),
                     )
 
-        def w1_slice(t):
-            return w1_codes[:, t * P : (t + 1) * P].bitcast(FP8X4), w1_plane[:, t * P : (t + 1) * P]
+        right_bank, left_bank, right, terms, z_quantised = {}, {}, {}, {}, {}
 
-        def w2_slice(t):
-            return w2_dealt[:, 2 * t * P : 2 * (t + 1) * P].bitcast(FP4X4), w2_dealt_plane[:, t * P : (t + 1) * P]
-
-        def w3_slice(t):
-            return w3_dealt[:, 2 * t * P : 2 * (t + 1) * P].bitcast(FP4X4), w3_dealt_plane[:, t * P : (t + 1) * P]
-
-        def interleaved(flat):
-            return flat.rearrange("p (v t) -> p v t", t=PACK)
-
-        right, left, terms, z_rounded, z_quantised, y_bank, y_values = {}, {}, {}, {}, {}, {}, {}
-
-        def bank_at(name, index):
-            return psum.tile([P, PACK, P], F32, name=name, offset=index * BANK_BYTES)
-
-        right_bank = {}
-
-        def right_factor(chunk, n, index):
-            bank = bank_at(f"right_bank{chunk}{n}", index)
-            weights_stationary(bank, w2_slice, [picked(field, chunk) for field in RIGHT_FIELDS[n]])
+        def right_factor(chunk, n, bank_index):
+            bank = bank_at(f"right_bank{chunk}{n}", bank_index)
+            project(bank, w2_slice, [picked_operand(field, chunk) for field in RIGHT_FIELDS[n]], range(PACK))
             right_bank[chunk, n] = bank
 
-        def copy_right(chunk, n, place):
-            right[chunk, n] = interleaved(place)
-            nc.scalar.copy(out=right[chunk, n], in_=right_bank[chunk, n][:].rearrange("p t v -> p v t"))
+        def copy_right(chunk, n):
+            first = (2 * chunk + n) * H
+            right[chunk, n] = as_words(right_all[:, first : first + H])
+            nc.scalar.copy(out=right[chunk, n], in_=slices_as_words(right_bank[chunk, n][:]))
 
-        def left_factor(chunk, n, index):
-            bank = bank_at(f"left_bank{chunk}{n}", index)
-            weights_stationary(bank, w1_slice, [picked(LEFT_FIELD[n], chunk)])
-            left[chunk, n] = bank[:].rearrange("p t v -> p v t")
+        def left_factor(chunk, n, bank_index):
+            bank = bank_at(f"left_bank{chunk}{n}", bank_index)
+            project(bank, w1_slice, [picked_operand(LEFT_FIELD[n], chunk)], range(PACK))
+            left_bank[chunk, n] = bank
 
-        def multiply(chunk, n, term):
-            nc.vector.tensor_tensor(out=interleaved(term[:]), in0=left[chunk, n], in1=right[chunk, n], op=MULT)
+        def multiply(chunk, n):
+            if (chunk, n) in PLACED_TERMS:
+                term = placed(f"term{chunk}{n}", [P, H], F32, PLACED_TERMS[chunk, n])
+            else:
+                term = kept(f"term{chunk}{n}", [P, H], F32)
+            nc.vector.tensor_tensor(
+                out=as_words(term[:]), in0=slices_as_words(left_bank[chunk, n][:]), in1=right[chunk, n], op=MULT
+            )
             terms[chunk, n] = term
 
-        def new_term(n):
-            return ring.tile([P, H], F32, name=f"term{n}")
-
-        def placed_term(chunk, n, slot):
-            return reused.tile([P, H], F32, name=f"term_{chunk}{n}", align_bytes=64, offset=TERM_AT[slot])
-
-        def add(chunk, engine, z):
+        def add_terms(engine, chunk, z):
             engine.tensor_tensor(out=z, in0=terms[chunk, 0][:], in1=terms[chunk, 1][:], op=ADD)
 
-        def quantize_z(first, end, z):
-            codes = keep.tile([P, (end - first) * P], U32, name=f"z_codes{first}", align_bytes=64)
-            plane = keep.tile([P, (end - first) * P], U8, name=f"z_plane{first}", align_bytes=64)
+        def quantize_z(chunk, z):
+            codes = kept(f"z_codes{chunk}", [P, P], U32)
+            plane = kept(f"z_plane{chunk}", [P, P], U8)
             nc.vector.quantize_mx(out=codes[:].bitcast(FP8X4), scales=plane[:], in_=z)
-            for n in range(end - first):
-                z_quantised[first + n] = (codes[:, n * P : (n + 1) * P].bitcast(FP8X4), plane[:, n * P : (n + 1) * P])
+            z_quantised[chunk] = (codes[:].bitcast(FP8X4), plane[:])
 
         y_rows = out_0.rearrange("(p t) v -> p t v", t=PACK)
-        y_plane = keep.tile([P, V], U8, name="y_plane", align_bytes=64)
-        y_rounded = keep.tile([P, V * PACK], BF16, name="y_rounded", align_bytes=64)
         y_words = out_1[0].rearrange("p v r -> p (v r)").bitcast(I32)
+        y_plane = kept("y_plane", [P, V], U8)
+        y_rounded = kept("y_rounded", [P, V * PACK], BF16)
+        y_values = [kept(f"y{chunk}", [P, PACK, P], F32) for chunk in range(CHUNKS)]
 
-        def last_layer(chunk, index):
-            bank = bank_at(f"y_bank{chunk}{index}", index)
-            weights_stationary(bank, w3_slice, [z_quantised[chunk]])
-            y_bank[chunk] = bank
+        def last_layer(name, chunk, bank_index, slices):
+            bank = bank_at(name, bank_index)
+            project(bank, w3_slice, [z_quantised[chunk]], slices)
+            return bank
 
-        def store_y(chunk):
-            y = ring.tile([P, PACK, P], F32, name="y")
-            nc.scalar.copy(out=y[:], in_=y_bank[chunk][:])
-            nc.sync.dma_start(out=y_rows[:, :, chunk * P : (chunk + 1) * P], in_=y[:])
-            y_values[chunk] = y
+        def store_y(queue, chunk):
+            queue.dma_start(out=y_rows[:, :, chunk * P : (chunk + 1) * P], in_=y_values[chunk][:])
 
-        def round_y(chunk, copy, source, t0=0, t1=PACK):
-            copy(
-                out=interleaved(y_rounded[:, chunk * H : (chunk + 1) * H])[:, :, t0:t1],
-                in_=source[:].rearrange("p t v -> p v t")[:, :, t0:t1],
-            )
+        def round_y(copy, chunk, source):
+            copy(out=as_words(y_rounded[:, chunk * H : (chunk + 1) * H]), in_=slices_as_words(source[:]))
 
         def quantize_y(first, end):
             nc.vector.quantize_mx(
@@ -249,87 +245,95 @@ def tile_picked_zfibi_none_po_kernel(
         def store_codes(first, end):
             nc.sync.dma_start(out=y_words[:, first * P : end * P], in_=y_codes[:, first * P : end * P])
 
-        all_words = reused.tile([P, 5 * GATHER], U32, name="all_words", align_bytes=64, offset=WORDS_AT)
-        for n, (field, half) in enumerate(((2, 0), (1, 0), (2, 1), (1, 1), (0, 0))):
-            gather_words(field, half, all_words[:, n * GATHER : (n + 1) * GATHER])
+        gather_scales(1, 0, 4, kept("scales_12", [P, 4 * HALF], U8)[:])
+        gather_scales(0, 0, 1, kept("scales_0_low", [P, HALF], U8)[:])
+        deal_codes(nc, w2_dealt, w2_codes)
+        deal_plane(nc, w2_dealt_plane, w2_plane)
+        deal_codes(nc, w3_dealt, w3_codes)
+        words_12 = kept("words_12", [P, 4 * HALF], U32)
+        gather_words(2, 0, 1, words_12[:, 0:HALF])
+        gather_words(1, 0, 2, words_12[:, HALF : 3 * HALF])
+        gather_words(2, 1, 1, words_12[:, 3 * HALF : 4 * HALF])
         round_w1(0)
+        gather_scales(0, 1, 1, placed("scales_0_high", [P, HALF], U8, W1_FIRST_AT)[:])
+        gather_words(0, 0, 1, placed("words_0_low", [P, HALF], U32, W1_FIRST_AT + 4 * HALF)[:])
         round_w1(1)
         round_w1(2)
-        quantize_w1()
-        w3_dealt_plane = reused.tile([P, N], U8, name="w3_dealt_plane", align_bytes=64, offset=W1_ROUNDED_AT)
-        deal_plane(nc.gpsimd, w3_dealt_plane, w3_plane)
-        late_words = reused.tile([P, GATHER], U32, name="late_words", align_bytes=64, offset=WORDS_0A_AT)
-        gather_words(0, 1, late_words[:])
-        right_all = reused.tile([P, 8 * H], F32, name="right_all", align_bytes=64, offset=RIGHT_ALL_AT)
-
-        def place(slot):
-            return right_all[:, slot * H : (slot + 1) * H]
+        nc.vector.quantize_mx(
+            out=w1_codes[:].bitcast(FP8X4), scales=w1_plane[:], in_=w1_rounded[:].rearrange("p t m j -> p (t m j)")
+        )
+        w3_dealt_plane = placed("w3_dealt_plane", [P, N], U8, W1_ROUNDED_AT)
+        deal_plane(nc, w3_dealt_plane, w3_plane)
+        gather_words(0, 1, 1, placed("words_0_high", [P, HALF], U32, LAST_WORDS_AT)[:])
+        right_all = placed("right_all", [P, 2 * CHUNKS * H], F32, RIGHT_AT)
 
         right_factor(0, 0, 0)
         right_factor(1, 0, 1)
         right_factor(0, 1, 2)
         right_factor(1, 1, 3)
-        copy_right(0, 0, place(0))
-        copy_right(0, 1, place(1))
-        copy_right(1, 0, place(7))
-        copy_right(1, 1, place(2))
+        right_factor(2, 0, 4)
+        for chunk in (0, 1):
+            copy_right(chunk, 0)
+            copy_right(chunk, 1)
         left_factor(0, 0, 6)
         left_factor(0, 1, 7)
-        left_factor(1, 0, 4)
-        left_factor(1, 1, 5)
-        right_factor(2, 0, 0)
+        left_factor(1, 0, 5)
+        left_factor(1, 1, 0)
         right_factor(2, 1, 2)
-        copy_right(2, 0, place(3))
-        copy_right(2, 1, place(4))
-        z_first = reused.tile([P, H], BF16, name="z_first", align_bytes=64, offset=Z_AT)
-        multiply(0, 0, placed_term(0, 0, 0))
-        multiply(0, 1, placed_term(0, 1, 1))
-        add(0, nc.gpsimd, z_first[:])
+        copy_right(2, 0)
+        copy_right(2, 1)
+
+        z_0 = placed("z_0", [P, H], BF16, Z_EARLY_AT)
+        multiply(0, 0)
+        multiply(0, 1)
+        add_terms(nc.gpsimd, 0, z_0[:])
         left_factor(2, 0, 6)
-        right_factor(3, 0, 1)
         left_factor(2, 1, 7)
+        right_factor(3, 0, 1)
         right_factor(3, 1, 3)
-        copy_right(3, 0, place(5))
-        copy_right(3, 1, place(6))
-        multiply(1, 0, placed_term(1, 0, 2))
-        multiply(1, 1, placed_term(1, 1, 3))
-        multiply(2, 0, placed_term(2, 0, 6))
-        quantize_z(0, 1, z_first[:])
-        z_second = reused.tile([P, H], BF16, name="z_second", align_bytes=64, offset=Z_AT)
-        add(1, nc.gpsimd, z_second[:])
-        left_factor(3, 0, 4)
-        left_factor(3, 1, 5)
-        last_layer(0, 0)
-        store_y(0)
-        round_y(0, nc.scalar.copy, y_bank[0])
-        multiply(2, 1, placed_term(2, 1, 4))
-        multiply(3, 0, placed_term(3, 0, 5))
-        multiply(3, 1, placed_term(3, 1, 7))
-        quantize_z(1, 2, z_second[:])
-        last_layer(1, 2)
-        store_y(1)
-        last_layer(1, 6)
-        round_y(1, nc.scalar.copy, y_bank[1])
-        z_late = reused.tile([P, 2 * H], BF16, name="z_late", align_bytes=64, offset=TERM_AT[2])
-        add(2, nc.vector, z_late[:, :H])
-        add(3, nc.vector, z_late[:, H:])
-        quantize_z(2, 3, z_late[:, :H])
-        quantize_z(3, 4, z_late[:, H:])
-        last_layer(2, 1)
-        store_y(2)
-        low = bank_at("y_low", 3)
-        high = bank_at("y_high", 7)
-        weights_stationary(low, w3_slice, [z_quantised[3]], range(0, 2))
-        weights_stationary(high, w3_slice, [z_quantised[3]], range(2, 4))
-        y_codes = reused.tile([P, V], I32, name="y_codes", align_bytes=64, offset=TERM_AT[5])
+        copy_right(3, 0)
+        copy_right(3, 1)
+        multiply(1, 0)
+        multiply(1, 1)
+        multiply(2, 0)
+        quantize_z(0, z_0[:])
+        z_1 = placed("z_1", [P, H], BF16, Z_EARLY_AT)
+        add_terms(nc.gpsimd, 1, z_1[:])
+        left_factor(3, 0, 5)
+        left_factor(3, 1, 0)
+
+        y_bank = last_layer("y_bank0", 0, 4, range(PACK))
+        nc.scalar.copy(out=y_values[0][:], in_=y_bank[:])
+        store_y(nc.sync, 0)
+        round_y(nc.scalar.copy, 0, y_bank)
+        multiply(2, 1)
+        multiply(3, 0)
+        multiply(3, 1)
+        quantize_z(1, z_1[:])
+        y_bank = last_layer("y_bank1", 1, 2, range(PACK))
+        nc.scalar.copy(out=y_values[1][:], in_=y_bank[:])
+        store_y(nc.sync, 1)
+        round_y(nc.scalar.copy, 1, y_bank)
+
+        z_late = placed("z_late", [P, 2 * H], BF16, TERM_10_AT)
+        add_terms(nc.vector, 2, z_late[:, :H])
+        add_terms(nc.vector, 3, z_late[:, H:])
+        quantize_z(2, z_late[:, :H])
+        quantize_z(3, z_late[:, H:])
+        y_bank = last_layer("y_bank2", 2, 1, range(PACK))
+        nc.scalar.copy(out=y_values[2][:], in_=y_bank[:])
+        store_y(nc.sync, 2)
+
+        y_low = last_layer("y_low", 3, 3, range(0, 2))
+        y_high = last_layer("y_high", 3, 7, range(2, 4))
+        y_codes = placed("y_codes", [P, V], I32, TERM_00_AT)
         quantize_y(0, 2)
         store_codes(0, 2)
-        y = ring.tile([P, PACK, P], F32, name="y")
-        nc.vector.tensor_copy(out=y[:, 0:2, :], in_=low[:, 0:2, :])
-        nc.scalar.copy(out=y[:, 2:4, :], in_=high[:, 2:4, :])
-        nc.sync.dma_start(out=y_rows[:, :, 3 * P : 4 * P], in_=y[:])
-        round_y(2, nc.vector.tensor_copy, y_values[2])
-        round_y(3, nc.vector.tensor_copy, y)
+        nc.vector.tensor_copy(out=y_values[3][:, 0:2, :], in_=y_low[:, 0:2, :])
+        nc.scalar.copy(out=y_values[3][:, 2:4, :], in_=y_high[:, 2:4, :])
+        store_y(nc.scalar, 3)
+        round_y(nc.vector.tensor_copy, 2, y_values[2])
+        round_y(nc.vector.tensor_copy, 3, y_values[3])
         quantize_y(2, 3)
         quantize_y(3, 4)
         store_codes(2, 4)

@@ -308,6 +308,7 @@ def tile_picked_zfibi_none_po_kernel(
         round_y(nc.scalar.copy, 0, y_bank)
         multiply(2, 1)
         multiply(3, 0)
+        last_layer("warm_up", 0, 5, range(PACK))
         multiply(3, 1)
         quantize_z(1, z_1[:])
         y_bank = last_layer("y_bank1", 1, 2, range(PACK))

@@ -29,6 +29,7 @@ LEFT_FIELD = (1, 0)
 RIGHT_FIELDS = ((2,), (2, 1))
 
 W1_CUTS = (0, 32, 80, 128)
+W1_GPSIMD = (0, 16, 18)
 
 TERM_BYTES = 4 * H
 W1_FIRST_AT = 0
@@ -57,7 +58,14 @@ def load_plane(nc, plane, rows, quadrants):
         )
 
 
-def deal_codes(nc, dealt, codes):
+def deal_codes_as_words(nc, dealt, codes):
+    nc.scalar.copy(
+        out=dealt[:].bitcast(U16).rearrange("k (t p) -> k t p", t=PACK),
+        in_=codes[:].bitcast(U16).rearrange("k (p t) -> k t p", t=PACK),
+    )
+
+
+def deal_codes_as_bytes(nc, dealt, codes):
     nc.gpsimd.tensor_copy(
         out=dealt[:].rearrange("k (t p b) -> k t p b", t=PACK, b=2),
         in_=codes[:].rearrange("k (p t b) -> k t p b", t=PACK, b=2),
@@ -117,29 +125,31 @@ def tile_picked_zfibi_none_po_kernel(
         nc.vector.memset(w3_plane[:].bitcast(I32), 0)
         nc.sync.dma_start(offsets[:], offs)
         nc.sync.dma_start(out=w2_codes[:].bitcast(I32), in_=w2_words[0].bitcast(I32))
-        nc.sync.dma_start(out=w3_codes[:].bitcast(I32), in_=w3_words[0].bitcast(I32))
         load_plane(nc, x_scale_table, x_scales, range(QUADRANTS))
-        load_plane(nc, w2_plane, w2_scales, range(0, 1))
+        load_plane(nc, w2_plane, w2_scales, range(0, 2))
         nc.sync.dma_start(out=x_word_table[:], in_=x_words[0].rearrange("p c r -> p (c r)").bitcast(I32))
-        load_plane(nc, w2_plane, w2_scales, range(1, QUADRANTS))
+        load_plane(nc, w2_plane, w2_scales, range(2, QUADRANTS))
+        nc.sync.dma_start(out=w3_codes[:].bitcast(I32), in_=w3_words[0].bitcast(I32))
         for u in range(3):
             nc.sync.dma_start(out=w1_pieces[u][:], in_=w1_rows[:, :, PACK * W1_CUTS[u] : PACK * W1_CUTS[u + 1]])
         load_plane(nc, w3_plane, w3_scales, range(QUADRANTS))
 
         picked_scales, picked_words = {}, {}
 
-        def gather(picked, table, field, half, halves, tile):
-            first = field * V + half * HALF
-            entries = offsets[:, first // LIST_ROWS : (first + halves * HALF) // LIST_ROWS]
-            nc.vector.tensor_copy(tile, table.indirect(entries))
+        def gather(picked, table, field, half, halves, tile, calls):
+            width = halves * HALF // calls
+            for call in range(calls):
+                first = field * V + half * HALF + call * width
+                entries = offsets[:, first // LIST_ROWS : (first + width) // LIST_ROWS]
+                nc.vector.tensor_copy(tile[:, call * width : (call + 1) * width], table.indirect(entries))
             for n in range(halves):
                 picked[divmod(2 * field + half + n, 2)] = tile[:, n * HALF : (n + 1) * HALF]
 
         def gather_scales(field, half, halves, tile):
-            gather(picked_scales, x_scale_table[:], field, half, halves, tile)
+            gather(picked_scales, x_scale_table[:], field, half, halves, tile, 1)
 
-        def gather_words(field, half, halves, tile):
-            gather(picked_words, x_word_table[:].bitcast(U32), field, half, halves, tile)
+        def gather_words(field, half, halves, tile, calls=1):
+            gather(picked_words, x_word_table[:].bitcast(U32), field, half, halves, tile, calls)
 
         def picked_operand(field, chunk):
             half, first = divmod(chunk * P, HALF)
@@ -153,11 +163,18 @@ def tile_picked_zfibi_none_po_kernel(
         w1_codes = kept("w1_codes", [P, H], U32)
         w1_plane = kept("w1_plane", [P, H], U8)
 
-        def round_w1(u):
-            nc.scalar.copy(
-                out=w1_rounded[:, :, W1_CUTS[u] : W1_CUTS[u + 1], :].rearrange("p t m j -> p m j t"),
-                in_=w1_pieces[u][:].rearrange("p j (m t) -> p m j t", t=PACK),
+        def round_groups(copy, walk, u, first, end):
+            piece = w1_pieces[u][:].rearrange("p j (m t) -> " + walk, t=PACK)
+            copy(
+                out=w1_rounded[:, :, first:end, :].rearrange("p t m j -> " + walk),
+                in_=piece[:, first - W1_CUTS[u] : end - W1_CUTS[u], :, :],
             )
+
+        def round_w1(u):
+            cut = W1_CUTS[u + 1] - W1_GPSIMD[u]
+            round_groups(nc.scalar.copy, "p m j t", u, W1_CUTS[u], cut)
+            if W1_GPSIMD[u]:
+                round_groups(nc.gpsimd.tensor_copy, "p m t j", u, cut, W1_CUTS[u + 1])
 
         def w1_slice(t):
             return w1_codes[:, t * P : (t + 1) * P].bitcast(FP8X4), w1_plane[:, t * P : (t + 1) * P]
@@ -247,11 +264,11 @@ def tile_picked_zfibi_none_po_kernel(
 
         gather_scales(1, 0, 4, kept("scales_12", [P, 4 * HALF], U8)[:])
         gather_scales(0, 0, 1, kept("scales_0_low", [P, HALF], U8)[:])
-        deal_codes(nc, w2_dealt, w2_codes)
+        deal_codes_as_bytes(nc, w2_dealt, w2_codes)
         deal_plane(nc, w2_dealt_plane, w2_plane)
-        deal_codes(nc, w3_dealt, w3_codes)
+        deal_codes_as_words(nc, w3_dealt, w3_codes)
         words_12 = kept("words_12", [P, 4 * HALF], U32)
-        gather_words(2, 0, 1, words_12[:, 0:HALF])
+        gather_words(2, 0, 1, words_12[:, 0:HALF], calls=2)
         gather_words(1, 0, 2, words_12[:, HALF : 3 * HALF])
         gather_words(2, 1, 1, words_12[:, 3 * HALF : 4 * HALF])
         round_w1(0)

@@ -28,8 +28,8 @@ ALIGN = 64
 LEFT_FIELD = (1, 0)
 RIGHT_FIELDS = ((2,), (2, 1))
 
-W1_CUTS = (0, 32, 80, 128)
-W1_GPSIMD = (0, 16, 18)
+W1_CUTS = (0, 32, 96, 128)
+W1_GPSIMD = (0, 24, 12)
 
 TERM_BYTES = 4 * H
 W1_FIRST_AT = 0
@@ -129,9 +129,9 @@ def tile_picked_zfibi_none_po_kernel(
         load_plane(nc, w2_plane, w2_scales, range(0, 2))
         nc.sync.dma_start(out=x_word_table[:], in_=x_words[0].rearrange("p c r -> p (c r)").bitcast(I32))
         load_plane(nc, w2_plane, w2_scales, range(2, QUADRANTS))
-        nc.sync.dma_start(out=w3_codes[:].bitcast(I32), in_=w3_words[0].bitcast(I32))
         for u in range(3):
             nc.sync.dma_start(out=w1_pieces[u][:], in_=w1_rows[:, :, PACK * W1_CUTS[u] : PACK * W1_CUTS[u + 1]])
+        nc.sync.dma_start(out=w3_codes[:].bitcast(I32), in_=w3_words[0].bitcast(I32))
         load_plane(nc, w3_plane, w3_scales, range(QUADRANTS))
 
         picked_scales, picked_words = {}, {}
@@ -158,7 +158,6 @@ def tile_picked_zfibi_none_po_kernel(
 
         w2_dealt = kept("w2_dealt", [P, 2 * H], U8)
         w2_dealt_plane = kept("w2_dealt_plane", [P, H], U8)
-        w3_dealt = kept("w3_dealt", [P, 2 * N], U8)
         w1_rounded = placed("w1_rounded", [P, PACK, P, PACK], BF16, W1_ROUNDED_AT)
         w1_codes = kept("w1_codes", [P, H], U32)
         w1_plane = kept("w1_plane", [P, H], U8)
@@ -266,7 +265,6 @@ def tile_picked_zfibi_none_po_kernel(
         gather_scales(0, 0, 1, kept("scales_0_low", [P, HALF], U8)[:])
         deal_codes_as_bytes(nc, w2_dealt, w2_codes)
         deal_plane(nc, w2_dealt_plane, w2_plane)
-        deal_codes_as_words(nc, w3_dealt, w3_codes)
         words_12 = kept("words_12", [P, 4 * HALF], U32)
         gather_words(2, 0, 1, words_12[:, 0:HALF], calls=2)
         gather_words(1, 0, 2, words_12[:, HALF : 3 * HALF])
@@ -292,6 +290,8 @@ def tile_picked_zfibi_none_po_kernel(
         for chunk in (0, 1):
             copy_right(chunk, 0)
             copy_right(chunk, 1)
+        w3_dealt = placed("w3_dealt", [P, 2 * N], U8, W1_ROUNDED_AT + 1024)
+        deal_codes_as_words(nc, w3_dealt, w3_codes)
         left_factor(0, 0, 6)
         left_factor(0, 1, 7)
         left_factor(1, 0, 5)

@@ -51,11 +51,9 @@ PLACED_TERMS = {
 }
 
 
-def load_plane(nc, plane, rows, quadrants):
-    for q in quadrants:
-        nc.sync.dma_start(
-            out=plane[32 * q : 32 * q + 4, :].bitcast(I32), in_=rows[0, 4 * q : 4 * q + 4, :].bitcast(I32)
-        )
+def load_plane(nc, plane, rows, places):
+    for r in places:
+        nc.sync.dma_start(out=plane[r:P:32, :].bitcast(I32), in_=rows[0, r::QUADRANTS, :].bitcast(I32))
 
 
 def deal_codes_as_words(nc, dealt, codes):

@@ -124,9 +124,9 @@ def tile_picked_zfibi_none_po_kernel(
         nc.sync.dma_start(offsets[:], offs)
         nc.sync.dma_start(out=w2_codes[:].bitcast(I32), in_=w2_words[0].bitcast(I32))
         load_plane(nc, x_scale_table, x_scales, range(QUADRANTS))
-        load_plane(nc, w2_plane, w2_scales, range(0, 2))
+        load_plane(nc, w2_plane, w2_scales, range(0, 1))
         nc.sync.dma_start(out=x_word_table[:], in_=x_words[0].rearrange("p c r -> p (c r)").bitcast(I32))
-        load_plane(nc, w2_plane, w2_scales, range(2, QUADRANTS))
+        load_plane(nc, w2_plane, w2_scales, range(1, QUADRANTS))
         for u in range(3):
             nc.sync.dma_start(out=w1_pieces[u][:], in_=w1_rows[:, :, PACK * W1_CUTS[u] : PACK * W1_CUTS[u + 1]])
         nc.sync.dma_start(out=w3_codes[:].bitcast(I32), in_=w3_words[0].bitcast(I32))

@@ -1,6 +1,7 @@
 from contextlib import ExitStack
 
 import concourse.mybir as mybir
+from concourse.masks import make_identity
 
 K, T, S, V, H, N = 512, 2048, 1536, 512, 512, 512
 FLOPS = 5 * 2 * K * H * V
@@ -25,6 +26,8 @@ CHUNKS = V // P
 BANK_BYTES = 2048
 ALIGN = 64
 
+TURNED = 2
+
 LEFT_FIELD = (1, 0)
 RIGHT_FIELDS = ((2,), (2, 1))
 
@@ -40,11 +43,13 @@ W1_ROUNDED_AT = W1_LAST_AT + 4096 + ALIGN
 TERM_00_AT = W1_ROUNDED_AT + 4096
 TERM_01_AT = TERM_00_AT + 2 * TERM_BYTES
 TERM_10_AT = TERM_01_AT + 2 * TERM_BYTES
-Z_EARLY_AT = TERM_10_AT + TERM_BYTES
+TERM_11_AT = TERM_10_AT + TERM_BYTES
+Z_EARLY_AT = TERM_11_AT + TERM_BYTES
 PLACED_TERMS = {
     (0, 0): TERM_00_AT,
     (0, 1): TERM_01_AT,
     (1, 0): TERM_10_AT,
+    (1, 1): TERM_11_AT,
     (2, 1): TERM_01_AT - TERM_BYTES + ALIGN,
     (3, 0): TERM_00_AT,
     (3, 1): TERM_01_AT + ALIGN,
@@ -134,9 +139,9 @@ def tile_picked_zfibi_none_po_kernel(
 
         picked_scales, picked_words = {}, {}
 
-        def gather(picked, table, field, half, halves, tile, calls):
+        def gather(picked, table, field, half, halves, tile, calls, only=None):
             width = halves * HALF // calls
-            for call in range(calls):
+            for call in range(calls) if only is None else (only,):
                 first = field * V + half * HALF + call * width
                 entries = offsets[:, first // LIST_ROWS : (first + width) // LIST_ROWS]
                 nc.vector.tensor_copy(tile[:, call * width : (call + 1) * width], table.indirect(entries))
@@ -146,8 +151,8 @@ def tile_picked_zfibi_none_po_kernel(
         def gather_scales(field, half, halves, tile):
             gather(picked_scales, x_scale_table[:], field, half, halves, tile, 1)
 
-        def gather_words(field, half, halves, tile, calls=1):
-            gather(picked_words, x_word_table[:].bitcast(U32), field, half, halves, tile, calls)
+        def gather_words(field, half, halves, tile, calls=1, only=None):
+            gather(picked_words, x_word_table[:].bitcast(U32), field, half, halves, tile, calls, only)
 
         def picked_operand(field, chunk):
             half, first = divmod(chunk * P, HALF)
@@ -198,19 +203,48 @@ def tile_picked_zfibi_none_po_kernel(
 
         right_bank, left_bank, right, terms, z_quantised = {}, {}, {}, {}, {}
 
+        def turned_project(bank, operands, codes, plane):
+            for n, (words, scales) in enumerate(operands):
+                nc.tensor.matmul_mx(
+                    out=bank[:].rearrange("r t p -> r (t p)"),
+                    lhsT=words,
+                    lhsT_scale=scales,
+                    rhs=codes,
+                    rhs_scale=plane,
+                    start=(n == 0),
+                    stop=(n == len(operands) - 1),
+                )
+
         def right_factor(chunk, n, bank_index):
             bank = bank_at(f"right_bank{chunk}{n}", bank_index)
-            project(bank, w2_slice, [picked_operand(field, chunk) for field in RIGHT_FIELDS[n]], range(PACK))
+            operands = [picked_operand(field, chunk) for field in RIGHT_FIELDS[n]]
+            if chunk == TURNED:
+                turned_project(bank, operands, w2_codes[:].bitcast(FP4X4), w2_plane[:])
+            else:
+                project(bank, w2_slice, operands, range(PACK))
             right_bank[chunk, n] = bank
 
         def copy_right(chunk, n):
             first = (2 * chunk + n) * H
-            right[chunk, n] = as_words(right_all[:, first : first + H])
-            nc.scalar.copy(out=right[chunk, n], in_=slices_as_words(right_bank[chunk, n][:]))
+            flat = right_all[:, first : first + H]
+            bank = right_bank[chunk, n][:]
+            if chunk == TURNED:
+                right[chunk, n] = flat
+                nc.scalar.copy(
+                    out=flat.rearrange("r (t p) -> r t p", t=PACK),
+                    in_=bank.rearrange("r a b -> r (a b)").rearrange("r (p t) -> r t p", t=PACK),
+                )
+            else:
+                right[chunk, n] = as_words(flat)
+                nc.scalar.copy(out=right[chunk, n], in_=slices_as_words(bank))
 
         def left_factor(chunk, n, bank_index):
             bank = bank_at(f"left_bank{chunk}{n}", bank_index)
-            project(bank, w1_slice, [picked_operand(LEFT_FIELD[n], chunk)], range(PACK))
+            operands = [picked_operand(LEFT_FIELD[n], chunk)]
+            if chunk == TURNED:
+                turned_project(bank, operands, w1_codes[:].bitcast(FP8X4), w1_plane[:])
+            else:
+                project(bank, w1_slice, operands, range(PACK))
             left_bank[chunk, n] = bank
 
         def multiply(chunk, n):
@@ -218,19 +252,32 @@ def tile_picked_zfibi_none_po_kernel(
                 term = placed(f"term{chunk}{n}", [P, H], F32, PLACED_TERMS[chunk, n])
             else:
                 term = kept(f"term{chunk}{n}", [P, H], F32)
-            nc.vector.tensor_tensor(
-                out=as_words(term[:]), in0=slices_as_words(left_bank[chunk, n][:]), in1=right[chunk, n], op=MULT
-            )
+            bank = left_bank[chunk, n][:]
+            if chunk == TURNED:
+                out, left = term[:], bank.rearrange("r t p -> r (t p)")
+            else:
+                out, left = as_words(term[:]), slices_as_words(bank)
+            nc.vector.tensor_tensor(out=out, in0=left, in1=right[chunk, n], op=MULT)
             terms[chunk, n] = term
+
+        def turn_and_add(bank, chunk, n):
+            for t in range(PACK):
+                nc.tensor.matmul(
+                    out=bank[:, t, :],
+                    lhsT=terms[chunk, n][:, t * P : (t + 1) * P],
+                    rhs=identity[:],
+                    is_transpose=True,
+                    start=(n == 0 and t == 0),
+                    stop=(n == 1 and t == PACK - 1),
+                )
 
         def add_terms(engine, chunk, z):
             engine.tensor_tensor(out=z, in0=terms[chunk, 0][:], in1=terms[chunk, 1][:], op=ADD)
 
-        def quantize_z(chunk, z):
-            codes = kept(f"z_codes{chunk}", [P, P], U32)
-            plane = kept(f"z_plane{chunk}", [P, P], U8)
-            nc.vector.quantize_mx(out=codes[:].bitcast(FP8X4), scales=plane[:], in_=z)
-            z_quantised[chunk] = (codes[:].bitcast(FP8X4), plane[:])
+        def quantize_z(chunk, z, codes, plane):
+            nc.vector.quantize_mx(out=codes.bitcast(FP8X4), scales=plane, in_=z)
+            for n in range(codes.shape[1] // P):
+                z_quantised[chunk + n] = (codes[:, n * P : (n + 1) * P].bitcast(FP8X4), plane[:, n * P : (n + 1) * P])
 
         y_rows = out_0.rearrange("(p t) v -> p t v", t=PACK)
         y_words = out_1[0].rearrange("p v r -> p (v r)").bitcast(I32)
@@ -238,7 +285,7 @@ def tile_picked_zfibi_none_po_kernel(
         y_rounded = kept("y_rounded", [P, V * PACK], BF16)
         y_values = [kept(f"y{chunk}", [P, PACK, P], F32) for chunk in range(CHUNKS)]
 
-        def last_layer(name, chunk, bank_index, slices):
+        def last_layer(name, chunk, bank_index, slices=range(PACK)):
             bank = bank_at(name, bank_index)
             project(bank, w3_slice, [z_quantised[chunk]], slices)
             return bank
@@ -259,14 +306,19 @@ def tile_picked_zfibi_none_po_kernel(
         def store_codes(first, end):
             nc.sync.dma_start(out=y_words[:, first * P : end * P], in_=y_codes[:, first * P : end * P])
 
+        identity = kept("identity", [P, P], F32)
+        nc.vector.memset(identity[:], 0.0)
+        make_identity(nc, identity[:], nomemset=True)
         gather_scales(1, 0, 4, kept("scales_12", [P, 4 * HALF], U8)[:])
         gather_scales(0, 0, 1, kept("scales_0_low", [P, HALF], U8)[:])
         deal_codes_as_bytes(nc, w2_dealt, w2_codes)
         deal_plane(nc, w2_dealt_plane, w2_plane)
         words_12 = kept("words_12", [P, 4 * HALF], U32)
-        gather_words(2, 0, 1, words_12[:, 0:HALF], calls=2)
-        gather_words(1, 0, 2, words_12[:, HALF : 3 * HALF])
-        gather_words(2, 1, 1, words_12[:, 3 * HALF : 4 * HALF])
+        gather_words(2, 1, 1, words_12[:, 0:HALF], calls=2, only=0)
+        gather_words(1, 1, 1, words_12[:, HALF : 2 * HALF])
+        gather_words(2, 0, 1, words_12[:, 3 * HALF : 4 * HALF])
+        gather_words(1, 0, 1, words_12[:, 2 * HALF : 3 * HALF])
+        gather_words(2, 1, 1, words_12[:, 0:HALF], calls=2, only=1)
         round_w1(0)
         gather_scales(0, 1, 1, placed("scales_0_high", [P, HALF], U8, W1_FIRST_AT)[:])
         gather_words(0, 0, 1, placed("words_0_low", [P, HALF], U32, W1_FIRST_AT + 4 * HALF)[:])
@@ -280,74 +332,76 @@ def tile_picked_zfibi_none_po_kernel(
         gather_words(0, 1, 1, placed("words_0_high", [P, HALF], U32, LAST_WORDS_AT)[:])
         right_all = placed("right_all", [P, 2 * CHUNKS * H], F32, RIGHT_AT)
 
-        right_factor(0, 0, 0)
-        right_factor(1, 0, 1)
-        right_factor(0, 1, 2)
-        right_factor(1, 1, 3)
-        right_factor(2, 0, 4)
+        def z_tiles(chunk, codes_at=None):
+            name = f"z_codes{chunk}"
+            codes = kept(name, [P, P], U32) if codes_at is None else placed(name, [P, P], U32, codes_at)
+            return codes[:], kept(f"z_plane{chunk}", [P, P], U8)[:]
+
+        def copy_y(chunk, bank):
+            nc.scalar.copy(out=y_values[chunk][:], in_=bank[:])
+            store_y(nc.sync, chunk)
+
+        right_factor(2, 0, 0)
+        right_factor(2, 1, 1)
         for chunk in (0, 1):
+            right_factor(chunk, 0, 2 * chunk + 2)
+            right_factor(chunk, 1, 2 * chunk + 3)
+        for chunk in (0, 1, 2):
             copy_right(chunk, 0)
             copy_right(chunk, 1)
-        w3_dealt = placed("w3_dealt", [P, 2 * N], U8, W1_ROUNDED_AT + 1024)
-        deal_codes_as_words(nc, w3_dealt, w3_codes)
         left_factor(0, 0, 6)
         left_factor(0, 1, 7)
-        left_factor(1, 0, 5)
-        left_factor(1, 1, 0)
-        right_factor(2, 1, 2)
-        copy_right(2, 0)
-        copy_right(2, 1)
+        left_factor(1, 0, 2)
+        left_factor(1, 1, 3)
+        right_factor(3, 0, 4)
+        left_factor(2, 0, 5)
 
         z_0 = placed("z_0", [P, H], BF16, Z_EARLY_AT)
         multiply(0, 0)
         multiply(0, 1)
         add_terms(nc.gpsimd, 0, z_0[:])
-        left_factor(2, 0, 6)
-        left_factor(2, 1, 7)
-        right_factor(3, 0, 1)
-        right_factor(3, 1, 3)
+        left_factor(2, 1, 6)
+        right_factor(3, 1, 7)
+        w3_dealt = placed("w3_dealt", [P, 2 * N], U8, W1_ROUNDED_AT + 1024)
+        deal_codes_as_words(nc, w3_dealt, w3_codes)
         copy_right(3, 0)
         copy_right(3, 1)
         multiply(1, 0)
         multiply(1, 1)
+        left_factor(3, 0, 3)
+        left_factor(3, 1, 0)
         multiply(2, 0)
-        quantize_z(0, z_0[:])
+        z_bank = bank_at("z_bank", 2)
+        turn_and_add(z_bank, 2, 0)
+        quantize_z(0, z_0[:], *z_tiles(0))
         z_1 = placed("z_1", [P, H], BF16, Z_EARLY_AT)
         add_terms(nc.gpsimd, 1, z_1[:])
-        left_factor(3, 0, 5)
-        left_factor(3, 1, 0)
-
-        y_bank = last_layer("y_bank0", 0, 4, range(PACK))
-        nc.scalar.copy(out=y_values[0][:], in_=y_bank[:])
-        store_y(nc.sync, 0)
-        round_y(nc.scalar.copy, 0, y_bank)
+        y_bank = last_layer("y_bank0", 0, 1)
+        copy_y(0, y_bank)
         multiply(2, 1)
+        turn_and_add(z_bank, 2, 1)
+        z_2 = kept("z_2", [P, H], BF16)
+        nc.scalar.copy(out=as_words(z_2[:]), in_=slices_as_words(z_bank[:]))
+        round_y(nc.scalar.copy, 0, y_bank)
         multiply(3, 0)
-        last_layer("warm_up", 0, 5, range(PACK))
+        last_layer("warm_up", 0, 3)
         multiply(3, 1)
-        quantize_z(1, z_1[:])
-        y_bank = last_layer("y_bank1", 1, 2, range(PACK))
-        nc.scalar.copy(out=y_values[1][:], in_=y_bank[:])
-        store_y(nc.sync, 1)
-        round_y(nc.scalar.copy, 1, y_bank)
-
-        z_late = placed("z_late", [P, 2 * H], BF16, TERM_10_AT)
-        add_terms(nc.vector, 2, z_late[:, :H])
-        add_terms(nc.vector, 3, z_late[:, H:])
-        quantize_z(2, z_late[:, :H])
-        quantize_z(3, z_late[:, H:])
-        y_bank = last_layer("y_bank2", 2, 1, range(PACK))
-        nc.scalar.copy(out=y_values[2][:], in_=y_bank[:])
-        store_y(nc.sync, 2)
-
-        y_low = last_layer("y_low", 3, 3, range(0, 2))
+        quantize_z(1, z_1[:], *z_tiles(1))
+        copy_y(1, last_layer("y_bank1", 1, 4))
+        z_3 = placed("z_3", [P, H], BF16, TERM_10_AT)
+        add_terms(nc.vector, 3, z_3[:])
+        quantize_z(2, z_2[:], *z_tiles(2, TERM_11_AT))
+        quantize_z(3, z_3[:], *z_tiles(3))
+        copy_y(2, last_layer("y_bank2", 2, 5))
+        y_low = last_layer("y_low", 3, 6, range(0, 2))
         y_high = last_layer("y_high", 3, 7, range(2, 4))
         y_codes = placed("y_codes", [P, V], I32, TERM_00_AT)
-        quantize_y(0, 2)
-        store_codes(0, 2)
+        round_y(nc.vector.tensor_copy, 1, y_values[1])
         nc.vector.tensor_copy(out=y_values[3][:, 0:2, :], in_=y_low[:, 0:2, :])
         nc.scalar.copy(out=y_values[3][:, 2:4, :], in_=y_high[:, 2:4, :])
         store_y(nc.scalar, 3)
+        quantize_y(0, 2)
+        store_codes(0, 2)
         round_y(nc.vector.tensor_copy, 2, y_values[2])
         round_y(nc.vector.tensor_copy, 3, y_values[3])
         quantize_y(2, 3)

@@ -45,6 +45,7 @@ TERM_01_AT = TERM_00_AT + 2 * TERM_BYTES
 TERM_10_AT = TERM_01_AT + 2 * TERM_BYTES
 TERM_11_AT = TERM_10_AT + TERM_BYTES
 Z_EARLY_AT = TERM_11_AT + TERM_BYTES
+Z_CODES_3_AT = Z_EARLY_AT + 2 * H
 PLACED_TERMS = {
     (0, 0): TERM_00_AT,
     (0, 1): TERM_01_AT,
@@ -282,7 +283,7 @@ def tile_picked_zfibi_none_po_kernel(
         y_rows = out_0.rearrange("(p t) v -> p t v", t=PACK)
         y_words = out_1[0].rearrange("p v r -> p (v r)").bitcast(I32)
         y_plane = kept("y_plane", [P, V], U8)
-        y_rounded = kept("y_rounded", [P, V * PACK], BF16)
+        y_rounded = {chunk: kept(f"y_rounded{chunk}", [P, H], BF16) for chunk in (0, 3)}
         y_values = [kept(f"y{chunk}", [P, PACK, P], F32) for chunk in range(CHUNKS)]
 
         def last_layer(name, chunk, bank_index, slices=range(PACK)):
@@ -294,13 +295,13 @@ def tile_picked_zfibi_none_po_kernel(
             queue.dma_start(out=y_rows[:, :, chunk * P : (chunk + 1) * P], in_=y_values[chunk][:])
 
         def round_y(copy, chunk, source):
-            copy(out=as_words(y_rounded[:, chunk * H : (chunk + 1) * H]), in_=slices_as_words(source[:]))
+            copy(out=as_words(y_rounded[chunk][:]), in_=slices_as_words(source[:]))
 
-        def quantize_y(first, end):
+        def quantize_y(chunk):
             nc.vector.quantize_mx(
-                out=y_codes[:, first * P : end * P].bitcast(FP8X4),
-                scales=y_plane[:, first * P : end * P],
-                in_=y_rounded[:, first * H : end * H],
+                out=y_codes[:, chunk * P : (chunk + 1) * P].bitcast(FP8X4),
+                scales=y_plane[:, chunk * P : (chunk + 1) * P],
+                in_=y_rounded[chunk][:],
             )
 
         def store_codes(first, end):
@@ -371,41 +372,53 @@ def tile_picked_zfibi_none_po_kernel(
         left_factor(3, 0, 3)
         left_factor(3, 1, 0)
         multiply(2, 0)
-        z_bank = bank_at("z_bank", 2)
-        turn_and_add(z_bank, 2, 0)
         quantize_z(0, z_0[:], *z_tiles(0))
         z_1 = placed("z_1", [P, H], BF16, Z_EARLY_AT)
         add_terms(nc.gpsimd, 1, z_1[:])
         y_bank = last_layer("y_bank0", 0, 1)
         copy_y(0, y_bank)
         multiply(2, 1)
+        z_bank = bank_at("z_bank", 6)
+        turn_and_add(z_bank, 2, 0)
         turn_and_add(z_bank, 2, 1)
         z_2 = kept("z_2", [P, H], BF16)
-        nc.scalar.copy(out=as_words(z_2[:]), in_=slices_as_words(z_bank[:]))
         round_y(nc.scalar.copy, 0, y_bank)
+        nc.scalar.copy(out=as_words(z_2[:]), in_=slices_as_words(z_bank[:]))
         multiply(3, 0)
         last_layer("warm_up", 0, 3)
         multiply(3, 1)
         quantize_z(1, z_1[:], *z_tiles(1))
-        copy_y(1, last_layer("y_bank1", 1, 4))
+        y_bank = last_layer("y_bank1", 1, 4)
+        copy_y(1, y_bank)
         z_3 = placed("z_3", [P, H], BF16, TERM_10_AT)
         add_terms(nc.vector, 3, z_3[:])
         quantize_z(2, z_2[:], *z_tiles(2, TERM_11_AT))
-        quantize_z(3, z_3[:], *z_tiles(3))
-        copy_y(2, last_layer("y_bank2", 2, 5))
-        y_low = last_layer("y_low", 3, 6, range(0, 2))
-        y_high = last_layer("y_high", 3, 7, range(2, 4))
+        quantize_z(3, z_3[:], *z_tiles(3, Z_CODES_3_AT))
+        low, high = {}, {}
+        for chunk, low_bank, high_bank in ((2, 5, 2), (3, 0, 7)):
+            low[chunk] = last_layer(f"y_low{chunk}", chunk, low_bank, range(0, 2))
+            high[chunk] = last_layer(f"y_high{chunk}", chunk, high_bank, range(2, 4))
+
+        def copy_pair(copy, chunk, bank, first):
+            copy(out=y_values[chunk][:, first : first + 2, :], in_=bank[:, first : first + 2, :])
+
         y_codes = placed("y_codes", [P, V], I32, TERM_00_AT)
+        quantize_y(0)
+        copy_pair(nc.vector.tensor_copy, 2, low[2], 0)
+        copy_pair(nc.scalar.copy, 2, high[2], 2)
+        store_y(nc.sync, 2)
+        y_rounded[1] = placed("y_rounded1", [P, H], BF16, TERM_11_AT)
         round_y(nc.vector.tensor_copy, 1, y_values[1])
-        nc.vector.tensor_copy(out=y_values[3][:, 0:2, :], in_=y_low[:, 0:2, :])
-        nc.scalar.copy(out=y_values[3][:, 2:4, :], in_=y_high[:, 2:4, :])
-        store_y(nc.scalar, 3)
-        quantize_y(0, 2)
+        copy_pair(nc.vector.tensor_copy, 3, low[3], 0)
+        copy_pair(nc.scalar.copy, 3, high[3], 2)
+        store_y(nc.sync, 3)
+        y_rounded[2] = placed("y_rounded2", [P, H], BF16, Z_CODES_3_AT)
+        round_y(nc.scalar.copy, 2, y_values[2])
+        quantize_y(1)
         store_codes(0, 2)
-        round_y(nc.vector.tensor_copy, 2, y_values[2])
         round_y(nc.vector.tensor_copy, 3, y_values[3])
-        quantize_y(2, 3)
-        quantize_y(3, 4)
+        quantize_y(2)
+        quantize_y(3)
         store_codes(2, 4)
         for q in range(QUADRANTS):
             (nc.sync, nc.scalar)[q % 2].dma_start(

@@ -30,6 +30,8 @@ TURNED = 2
 
 LEFT_FIELD = (1, 0)
 RIGHT_FIELDS = ((2,), (2, 1))
+TURNED_LEFT_FIELDS = ((1, 0), (0,))
+TURNED_RIGHT_FIELD = (2, 1)
 
 W1_CUTS = (0, 32, 96, 128)
 W1_GPSIMD = (0, 24, 12)
@@ -218,10 +220,11 @@ def tile_picked_zfibi_none_po_kernel(
 
         def right_factor(chunk, n, bank_index):
             bank = bank_at(f"right_bank{chunk}{n}", bank_index)
-            operands = [picked_operand(field, chunk) for field in RIGHT_FIELDS[n]]
             if chunk == TURNED:
+                operands = [picked_operand(TURNED_RIGHT_FIELD[n], chunk)]
                 turned_project(bank, operands, w2_codes[:].bitcast(FP4X4), w2_plane[:])
             else:
+                operands = [picked_operand(field, chunk) for field in RIGHT_FIELDS[n]]
                 project(bank, w2_slice, operands, range(PACK))
             right_bank[chunk, n] = bank
 
@@ -241,11 +244,11 @@ def tile_picked_zfibi_none_po_kernel(
 
         def left_factor(chunk, n, bank_index):
             bank = bank_at(f"left_bank{chunk}{n}", bank_index)
-            operands = [picked_operand(LEFT_FIELD[n], chunk)]
             if chunk == TURNED:
+                operands = [picked_operand(field, chunk) for field in TURNED_LEFT_FIELDS[n]]
                 turned_project(bank, operands, w1_codes[:].bitcast(FP8X4), w1_plane[:])
             else:
-                project(bank, w1_slice, operands, range(PACK))
+                project(bank, w1_slice, [picked_operand(LEFT_FIELD[n], chunk)], range(PACK))
             left_bank[chunk, n] = bank
 
         def multiply(chunk, n):
@@ -404,6 +407,7 @@ def tile_picked_zfibi_none_po_kernel(
 
         y_codes = placed("y_codes", [P, V], I32, TERM_00_AT)
         quantize_y(0)
+        store_codes(0, 1)
         copy_pair(nc.vector.tensor_copy, 2, low[2], 0)
         copy_pair(nc.scalar.copy, 2, high[2], 2)
         store_y(nc.sync, 2)
@@ -415,11 +419,10 @@ def tile_picked_zfibi_none_po_kernel(
         y_rounded[2] = placed("y_rounded2", [P, H], BF16, Z_CODES_3_AT)
         round_y(nc.scalar.copy, 2, y_values[2])
         quantize_y(1)
-        store_codes(0, 2)
         round_y(nc.vector.tensor_copy, 3, y_values[3])
         quantize_y(2)
         quantize_y(3)
-        store_codes(2, 4)
+        store_codes(1, 4)
         for q in range(QUADRANTS):
             (nc.sync, nc.scalar)[q % 2].dma_start(
                 out=out_2[0, 4 * q : 4 * q + 4, :].bitcast(I32), in_=y_plane[32 * q : 32 * q + 4, :].bitcast(I32)

@@ -391,8 +391,11 @@ def tile_picked_zfibi_none_po_kernel(
         last_layer("warm_up", 0, 3)
         multiply(3, 1)
         quantize_z(1, z_1[:], *z_tiles(1))
-        y_bank = last_layer("y_bank1", 1, 4)
-        copy_y(1, y_bank)
+        for first, bank_index in ((0, 4), (2, 1)):
+            pair = slice(first, first + 2)
+            y_bank = last_layer(f"y_bank1{first}", 1, bank_index, range(first, first + 2))
+            nc.scalar.copy(out=y_values[1][:, pair, :], in_=y_bank[:, pair, :])
+            nc.sync.dma_start(out=y_rows[:, pair, P : 2 * P], in_=y_values[1][:, pair, :])
         z_3 = placed("z_3", [P, H], BF16, TERM_10_AT)
         add_terms(nc.vector, 3, z_3[:])
         quantize_z(2, z_2[:], *z_tiles(2, TERM_11_AT))

from contextlib import ExitStack

import concourse.mybir as mybir
from concourse.masks import make_identity

K, T, S, V, H, N = 512, 2048, 1536, 512, 512, 512
FLOPS = 5 * 2 * K * H * V

F32 = mybir.dt.float32
BF16 = mybir.dt.bfloat16
I32 = mybir.dt.int32
U32 = mybir.dt.uint32
U16 = mybir.dt.uint16
U8 = mybir.dt.uint8
FP8X4 = mybir.dt.float8_e4m3fn_x4
FP4X4 = mybir.dt.float4_e2m1fn_x4
MULT = mybir.AluOpType.mult
ADD = mybir.AluOpType.add

P = 128
PACK = 4
QUADRANTS = 4
LIST_ROWS = 16
HALF = V // 2
CHUNKS = V // P
BANK_BYTES = 2048
ALIGN = 64

TURNED = 2

LEFT_FIELD = (1, 0)
RIGHT_FIELDS = ((2,), (2, 1))
TURNED_LEFT_FIELDS = ((1, 0), (0,))
TURNED_RIGHT_FIELD = (2, 1)

W1_CUTS = (0, 32, 96, 128)
W1_GPSIMD = (0, 24, 12)

TERM_BYTES = 4 * H
W1_FIRST_AT = 0
RIGHT_AT = 2048
W1_LAST_AT = RIGHT_AT + 2 * CHUNKS * TERM_BYTES - ALIGN
LAST_WORDS_AT = W1_LAST_AT + ALIGN
W1_ROUNDED_AT = W1_LAST_AT + 4096 + ALIGN
TERM_00_AT = W1_ROUNDED_AT + 4096
TERM_01_AT = TERM_00_AT + 2 * TERM_BYTES
TERM_10_AT = TERM_01_AT + 2 * TERM_BYTES
TERM_11_AT = TERM_10_AT + TERM_BYTES
Z_EARLY_AT = TERM_11_AT + TERM_BYTES
Z_CODES_3_AT = Z_EARLY_AT + 2 * H
PLACED_TERMS = {
    (0, 0): TERM_00_AT,
    (0, 1): TERM_01_AT,
    (1, 0): TERM_10_AT,
    (1, 1): TERM_11_AT,
    (2, 1): TERM_01_AT - TERM_BYTES + ALIGN,
    (3, 0): TERM_00_AT,
    (3, 1): TERM_01_AT + ALIGN,
}


def load_plane(nc, plane, rows, places):
    for r in places:
        nc.sync.dma_start(out=plane[r:P:32, :].bitcast(I32), in_=rows[0, r::QUADRANTS, :].bitcast(I32))


def deal_codes_as_words(nc, dealt, codes):
    nc.scalar.copy(
        out=dealt[:].bitcast(U16).rearrange("k (t p) -> k t p", t=PACK),
        in_=codes[:].bitcast(U16).rearrange("k (p t) -> k t p", t=PACK),
    )


def deal_codes_as_bytes(nc, dealt, codes):
    nc.gpsimd.tensor_copy(
        out=dealt[:].rearrange("k (t p b) -> k t p b", t=PACK, b=2),
        in_=codes[:].rearrange("k (p t b) -> k t p b", t=PACK, b=2),
    )


def deal_plane(nc, dealt, plane):
    nc.gpsimd.tensor_copy(
        out=dealt[:].rearrange("k (t p) -> k t p", t=PACK),
        in_=plane[:].rearrange("k (p t) -> k t p", t=PACK),
    )


def as_words(flat):
    return flat.rearrange("p (v t) -> p v t", t=PACK)


def slices_as_words(slices):
    return slices.rearrange("p t v -> p v t")


def tile_picked_zfibi_none_po_kernel(
    tc, x_words, x_scales, w1, w2_words, w2_scales, w3_words, w3_scales, offs, out_0, out_1, out_2
):
    nc = tc.nc
    with ExitStack() as ctx:
        keep = ctx.enter_context(tc.tile_pool(name="keep", bufs=1))
        reused = ctx.enter_context(tc.tile_pool(name="reused", bufs=1))
        psum = ctx.enter_context(tc.psum_pool(name="psum", bufs=1))

        def kept(name, shape, dtype):
            return keep.tile(shape, dtype, name=name, align_bytes=ALIGN)

        def placed(name, shape, dtype, offset):
            return reused.tile(shape, dtype, name=name, align_bytes=ALIGN, offset=offset)

        def bank_at(name, index):
            return psum.tile([P, PACK, P], F32, name=name, offset=index * BANK_BYTES)

        offsets = keep.tile([P, S // LIST_ROWS], U16, name="offsets")
        x_scale_table = kept("x_scale_table", [P, T], U8)
        x_word_table = kept("x_word_table", [P, T], I32)
        w2_codes = kept("w2_codes", [P, 2 * H], U8)
        w2_plane = kept("w2_plane", [P, H], U8)
        w3_codes = kept("w3_codes", [P, 2 * N], U8)
        w3_plane = kept("w3_plane", [P, N], U8)
        w1_widths = [PACK * (W1_CUTS[u + 1] - W1_CUTS[u]) for u in range(3)]
        w1_pieces = [
            placed("w1_first", [P, PACK, w1_widths[0]], F32, W1_FIRST_AT),
            kept("w1_middle", [P, PACK, w1_widths[1]], F32),
            placed("w1_last", [P, PACK, w1_widths[2]], F32, W1_LAST_AT),
        ]
        w1_rows = w1.rearrange("(p j) c -> p j c", j=PACK)

        nc.vector.memset(x_scale_table[:].bitcast(I32), 0)
        nc.vector.memset(w2_plane[:].bitcast(I32), 0)
        nc.vector.memset(w3_plane[:].bitcast(I32), 0)
        nc.sync.dma_start(offsets[:], offs)
        nc.sync.dma_start(out=w2_codes[:].bitcast(I32), in_=w2_words[0].bitcast(I32))
        load_plane(nc, x_scale_table, x_scales, range(QUADRANTS))
        load_plane(nc, w2_plane, w2_scales, range(0, 1))
        nc.sync.dma_start(out=x_word_table[:], in_=x_words[0].rearrange("p c r -> p (c r)").bitcast(I32))
        load_plane(nc, w2_plane, w2_scales, range(1, QUADRANTS))
        for u in range(3):
            nc.sync.dma_start(out=w1_pieces[u][:], in_=w1_rows[:, :, PACK * W1_CUTS[u] : PACK * W1_CUTS[u + 1]])
        nc.sync.dma_start(out=w3_codes[:].bitcast(I32), in_=w3_words[0].bitcast(I32))
        load_plane(nc, w3_plane, w3_scales, range(QUADRANTS))

        picked_scales, picked_words = {}, {}

        def gather(picked, table, field, half, halves, tile, calls, only=None):
            width = halves * HALF // calls
            for call in range(calls) if only is None else (only,):
                first = field * V + half * HALF + call * width
                entries = offsets[:, first // LIST_ROWS : (first + width) // LIST_ROWS]
                nc.vector.tensor_copy(tile[:, call * width : (call + 1) * width], table.indirect(entries))
            for n in range(halves):
                picked[divmod(2 * field + half + n, 2)] = tile[:, n * HALF : (n + 1) * HALF]

        def gather_scales(field, half, halves, tile):
            gather(picked_scales, x_scale_table[:], field, half, halves, tile, 1)

        def gather_words(field, half, halves, tile, calls=1, only=None):
            gather(picked_words, x_word_table[:].bitcast(U32), field, half, halves, tile, calls, only)

        def picked_operand(field, chunk):
            half, first = divmod(chunk * P, HALF)
            words = picked_words[field, half][:, first : first + P]
            return words.bitcast(FP8X4), picked_scales[field, half][:, first : first + P]

        w2_dealt = kept("w2_dealt", [P, 2 * H], U8)
        w2_dealt_plane = kept("w2_dealt_plane", [P, H], U8)
        w1_rounded = placed("w1_rounded", [P, PACK, P, PACK], BF16, W1_ROUNDED_AT)
        w1_codes = kept("w1_codes", [P, H], U32)
        w1_plane = kept("w1_plane", [P, H], U8)

        def round_groups(copy, walk, u, first, end):
            piece = w1_pieces[u][:].rearrange("p j (m t) -> " + walk, t=PACK)
            copy(
                out=w1_rounded[:, :, first:end, :].rearrange("p t m j -> " + walk),
                in_=piece[:, first - W1_CUTS[u] : end - W1_CUTS[u], :, :],
            )

        def round_w1(u):
            cut = W1_CUTS[u + 1] - W1_GPSIMD[u]
            round_groups(nc.scalar.copy, "p m j t", u, W1_CUTS[u], cut)
            if W1_GPSIMD[u]:
                round_groups(nc.gpsimd.tensor_copy, "p m t j", u, cut, W1_CUTS[u + 1])

        def w1_slice(t):
            return w1_codes[:, t * P : (t + 1) * P].bitcast(FP8X4), w1_plane[:, t * P : (t + 1) * P]

        def w2_slice(t):
            return w2_dealt[:, 2 * t * P : 2 * (t + 1) * P].bitcast(FP4X4), w2_dealt_plane[:, t * P : (t + 1) * P]

        def w3_slice(t):
            return w3_dealt[:, 2 * t * P : 2 * (t + 1) * P].bitcast(FP4X4), w3_dealt_plane[:, t * P : (t + 1) * P]

        def project(bank, dealt_slice, moving, slices):
            for t in slices:
                codes, plane = dealt_slice(t)
                for n, (words, scales) in enumerate(moving):
                    nc.tensor.matmul_mx(
                        out=bank[:, t, :],
                        lhsT=codes,
                        lhsT_scale=plane,
                        rhs=words,
                        rhs_scale=scales,
                        start=(n == 0),
                        stop=(n == len(moving) - 1),
                    )

        right_bank, left_bank, right, terms, z_quantised = {}, {}, {}, {}, {}

        def turned_project(bank, operands, codes, plane):
            for n, (words, scales) in enumerate(operands):
                nc.tensor.matmul_mx(
                    out=bank[:].rearrange("r t p -> r (t p)"),
                    lhsT=words,
                    lhsT_scale=scales,
                    rhs=codes,
                    rhs_scale=plane,
                    start=(n == 0),
                    stop=(n == len(operands) - 1),
                )

        def right_factor(chunk, n, bank_index):
            bank = bank_at(f"right_bank{chunk}{n}", bank_index)
            if chunk == TURNED:
                operands = [picked_operand(TURNED_RIGHT_FIELD[n], chunk)]
                turned_project(bank, operands, w2_codes[:].bitcast(FP4X4), w2_plane[:])
            else:
                operands = [picked_operand(field, chunk) for field in RIGHT_FIELDS[n]]
                project(bank, w2_slice, operands, range(PACK))
            right_bank[chunk, n] = bank

        def copy_right(chunk, n):
            first = (2 * chunk + n) * H
            flat = right_all[:, first : first + H]
            bank = right_bank[chunk, n][:]
            if chunk == TURNED:
                right[chunk, n] = flat
                nc.scalar.copy(
                    out=flat.rearrange("r (t p) -> r t p", t=PACK),
                    in_=bank.rearrange("r a b -> r (a b)").rearrange("r (p t) -> r t p", t=PACK),
                )
            else:
                right[chunk, n] = as_words(flat)
                nc.scalar.copy(out=right[chunk, n], in_=slices_as_words(bank))

        def left_factor(chunk, n, bank_index):
            bank = bank_at(f"left_bank{chunk}{n}", bank_index)
            if chunk == TURNED:
                operands = [picked_operand(field, chunk) for field in TURNED_LEFT_FIELDS[n]]
                turned_project(bank, operands, w1_codes[:].bitcast(FP8X4), w1_plane[:])
            else:
                project(bank, w1_slice, [picked_operand(LEFT_FIELD[n], chunk)], range(PACK))
            left_bank[chunk, n] = bank

        def multiply(chunk, n):
            if (chunk, n) in PLACED_TERMS:
                term = placed(f"term{chunk}{n}", [P, H], F32, PLACED_TERMS[chunk, n])
            else:
                term = kept(f"term{chunk}{n}", [P, H], F32)
            bank = left_bank[chunk, n][:]
            if chunk == TURNED:
                out, left = term[:], bank.rearrange("r t p -> r (t p)")
            else:
                out, left = as_words(term[:]), slices_as_words(bank)
            nc.vector.tensor_tensor(out=out, in0=left, in1=right[chunk, n], op=MULT)
            terms[chunk, n] = term

        def turn_and_add(bank, chunk, n):
            for t in range(PACK):
                nc.tensor.matmul(
                    out=bank[:, t, :],
                    lhsT=terms[chunk, n][:, t * P : (t + 1) * P],
                    rhs=identity[:],
                    is_transpose=True,
                    start=(n == 0 and t == 0),
                    stop=(n == 1 and t == PACK - 1),
                )

        def add_terms(engine, chunk, z):
            engine.tensor_tensor(out=z, in0=terms[chunk, 0][:], in1=terms[chunk, 1][:], op=ADD)

        def quantize_z(chunk, z, codes, plane):
            nc.vector.quantize_mx(out=codes.bitcast(FP8X4), scales=plane, in_=z)
            for n in range(codes.shape[1] // P):
                z_quantised[chunk + n] = (codes[:, n * P : (n + 1) * P].bitcast(FP8X4), plane[:, n * P : (n + 1) * P])

        y_rows = out_0.rearrange("(p t) v -> p t v", t=PACK)
        y_words = out_1[0].rearrange("p v r -> p (v r)").bitcast(I32)
        y_plane = kept("y_plane", [P, V], U8)
        y_rounded = {chunk: kept(f"y_rounded{chunk}", [P, H], BF16) for chunk in (0, 3)}
        y_values = [kept(f"y{chunk}", [P, PACK, P], F32) for chunk in range(CHUNKS)]

        def last_layer(name, chunk, bank_index, slices=range(PACK)):
            bank = bank_at(name, bank_index)
            project(bank, w3_slice, [z_quantised[chunk]], slices)
            return bank

        def store_y(queue, chunk):
            queue.dma_start(out=y_rows[:, :, chunk * P : (chunk + 1) * P], in_=y_values[chunk][:])

        def round_y(copy, chunk, source):
            copy(out=as_words(y_rounded[chunk][:]), in_=slices_as_words(source[:]))

        def quantize_y(chunk):
            nc.vector.quantize_mx(
                out=y_codes[:, chunk * P : (chunk + 1) * P].bitcast(FP8X4),
                scales=y_plane[:, chunk * P : (chunk + 1) * P],
                in_=y_rounded[chunk][:],
            )

        def store_codes(first, end):
            nc.sync.dma_start(out=y_words[:, first * P : end * P], in_=y_codes[:, first * P : end * P])

        identity = kept("identity", [P, P], F32)
        nc.vector.memset(identity[:], 0.0)
        make_identity(nc, identity[:], nomemset=True)
        gather_scales(1, 0, 4, kept("scales_12", [P, 4 * HALF], U8)[:])
        gather_scales(0, 0, 1, kept("scales_0_low", [P, HALF], U8)[:])
        deal_codes_as_bytes(nc, w2_dealt, w2_codes)
        deal_plane(nc, w2_dealt_plane, w2_plane)
        words_12 = kept("words_12", [P, 4 * HALF], U32)
        gather_words(2, 1, 1, words_12[:, 0:HALF], calls=2, only=0)
        gather_words(1, 1, 1, words_12[:, HALF : 2 * HALF])
        gather_words(2, 0, 1, words_12[:, 3 * HALF : 4 * HALF])
        gather_words(1, 0, 1, words_12[:, 2 * HALF : 3 * HALF])
        gather_words(2, 1, 1, words_12[:, 0:HALF], calls=2, only=1)
        round_w1(0)
        gather_scales(0, 1, 1, placed("scales_0_high", [P, HALF], U8, W1_FIRST_AT)[:])
        gather_words(0, 0, 1, placed("words_0_low", [P, HALF], U32, W1_FIRST_AT + 4 * HALF)[:])
        round_w1(1)
        round_w1(2)
        nc.vector.quantize_mx(
            out=w1_codes[:].bitcast(FP8X4), scales=w1_plane[:], in_=w1_rounded[:].rearrange("p t m j -> p (t m j)")
        )
        w3_dealt_plane = placed("w3_dealt_plane", [P, N], U8, W1_ROUNDED_AT)
        deal_plane(nc, w3_dealt_plane, w3_plane)
        gather_words(0, 1, 1, placed("words_0_high", [P, HALF], U32, LAST_WORDS_AT)[:])
        right_all = placed("right_all", [P, 2 * CHUNKS * H], F32, RIGHT_AT)

        def z_tiles(chunk, codes_at=None):
            name = f"z_codes{chunk}"
            codes = kept(name, [P, P], U32) if codes_at is None else placed(name, [P, P], U32, codes_at)
            return codes[:], kept(f"z_plane{chunk}", [P, P], U8)[:]

        def copy_y(chunk, bank):
            nc.scalar.copy(out=y_values[chunk][:], in_=bank[:])
            store_y(nc.sync, chunk)

        right_factor(2, 0, 0)
        right_factor(2, 1, 1)
        for chunk in (0, 1):
            right_factor(chunk, 0, 2 * chunk + 2)
            right_factor(chunk, 1, 2 * chunk + 3)
        for chunk in (0, 1, 2):
            copy_right(chunk, 0)
            copy_right(chunk, 1)
        left_factor(0, 0, 6)
        left_factor(0, 1, 7)
        left_factor(1, 0, 2)
        left_factor(1, 1, 3)
        right_factor(3, 0, 4)
        left_factor(2, 0, 5)

        z_0 = placed("z_0", [P, H], BF16, Z_EARLY_AT)
        multiply(0, 0)
        multiply(0, 1)
        add_terms(nc.gpsimd, 0, z_0[:])
        left_factor(2, 1, 6)
        right_factor(3, 1, 7)
        w3_dealt = placed("w3_dealt", [P, 2 * N], U8, W1_ROUNDED_AT + 1024)
        deal_codes_as_words(nc, w3_dealt, w3_codes)
        copy_right(3, 0)
        copy_right(3, 1)
        multiply(1, 0)
        multiply(1, 1)
        left_factor(3, 0, 3)
        left_factor(3, 1, 0)
        multiply(2, 0)
        quantize_z(0, z_0[:], *z_tiles(0))
        z_1 = placed("z_1", [P, H], BF16, Z_EARLY_AT)
        add_terms(nc.gpsimd, 1, z_1[:])
        y_bank = last_layer("y_bank0", 0, 1)
        copy_y(0, y_bank)
        multiply(2, 1)
        z_bank = bank_at("z_bank", 6)
        turn_and_add(z_bank, 2, 0)
        turn_and_add(z_bank, 2, 1)
        z_2 = kept("z_2", [P, H], BF16)
        round_y(nc.scalar.copy, 0, y_bank)
        nc.scalar.copy(out=as_words(z_2[:]), in_=slices_as_words(z_bank[:]))
        multiply(3, 0)
        last_layer("warm_up", 0, 3)
        multiply(3, 1)
        quantize_z(1, z_1[:], *z_tiles(1))
        for first, bank_index in ((0, 4), (2, 1)):
            pair = slice(first, first + 2)
            y_bank = last_layer(f"y_bank1{first}", 1, bank_index, range(first, first + 2))
            nc.scalar.copy(out=y_values[1][:, pair, :], in_=y_bank[:, pair, :])
            nc.sync.dma_start(out=y_rows[:, pair, P : 2 * P], in_=y_values[1][:, pair, :])
        z_3 = placed("z_3", [P, H], BF16, TERM_10_AT)
        add_terms(nc.vector, 3, z_3[:])
        quantize_z(2, z_2[:], *z_tiles(2, TERM_11_AT))
        quantize_z(3, z_3[:], *z_tiles(3, Z_CODES_3_AT))
        low, high = {}, {}
        for chunk, low_bank, high_bank in ((2, 5, 2), (3, 0, 7)):
            low[chunk] = last_layer(f"y_low{chunk}", chunk, low_bank, range(0, 2))
            high[chunk] = last_layer(f"y_high{chunk}", chunk, high_bank, range(2, 4))

        def copy_pair(copy, chunk, bank, first):
            copy(out=y_values[chunk][:, first : first + 2, :], in_=bank[:, first : first + 2, :])

        y_codes = placed("y_codes", [P, V], I32, TERM_00_AT)
        quantize_y(0)
        store_codes(0, 1)
        copy_pair(nc.vector.tensor_copy, 2, low[2], 0)
        copy_pair(nc.scalar.copy, 2, high[2], 2)
        store_y(nc.sync, 2)
        y_rounded[1] = placed("y_rounded1", [P, H], BF16, TERM_11_AT)
        round_y(nc.vector.tensor_copy, 1, y_values[1])
        copy_pair(nc.vector.tensor_copy, 3, low[3], 0)
        copy_pair(nc.scalar.copy, 3, high[3], 2)
        store_y(nc.sync, 3)
        y_rounded[2] = placed("y_rounded2", [P, H], BF16, Z_CODES_3_AT)
        round_y(nc.scalar.copy, 2, y_values[2])
        quantize_y(1)
        round_y(nc.vector.tensor_copy, 3, y_values[3])
        quantize_y(2)
        quantize_y(3)
        store_codes(1, 4)
        for q in range(QUADRANTS):
            (nc.sync, nc.scalar)[q % 2].dma_start(
                out=out_2[0, 4 * q : 4 * q + 4, :].bitcast(I32), in_=y_plane[32 * q : 32 * q + 4, :].bitcast(I32)
            )
